import numpy as np, ml_dtypes
CORES = [16,17,18,19,32,33,34,35]
N = 8
BF = ml_dtypes.bfloat16
W, T, K, R = 4096, 2048, 192, 5
SR, SG = (1, 5, 3), (0, 3, 1)
def pack(x, ix, q, c):
    return {"rec": np.ascontiguousarray(x.reshape(N, 128, W)).astype(np.float32).astype(BF), "idx": np.ascontiguousarray(ix.reshape(N, 128, T)).astype(np.int32),
            "que": np.ascontiguousarray(q).astype(np.int32), "cur": np.ascontiguousarray(c.reshape(N, 8, 1)).astype(np.int32)}
def setup_inputs(rng):
    x = rng.integers(0, 16, (N, 8, 16, W)); ix = rng.integers(0, W, (N, 8, 16, T))
    q = np.ascontiguousarray(np.argsort(rng.random((N, 8, T)), axis=-1)[..., :K]); q[..., 17::32] = q[..., 2::32]
    return pack(x, ix, q, rng.integers(0, T, (N, 8)))
def regions(rng):
    o = 1 + rng.permutation(W - 2)
    return o[:816], o[816:820], np.concatenate([np.array([0, W - 1]), o[820:1330]]), o[1330:]
def give(rng, x, at, k, v):
    v = np.asarray(v)
    x[k, at] = (v >> 8) + (W >> 8) * rng.integers(0, 4096 // W, v.shape); x[(k + 1) % 16, at] = (v >> 4) & 15; x[(k + 2) % 16, at] = v & 15
def twin(rng, rd, w, bits, on):
    return int(rng.choice(rd[np.isin(rd ^ w, rd) & ((rd & bits) == on)]))
def group(rng, reg, edge):
    ixr, sp, dat, rdp = reg
    x = rng.integers(0, 16, (16, W)); x[:, rdp] = rng.integers(1, 16, (16, len(rdp))); o = rng.permutation(ixr); d0 = rng.permutation(dat)
    c0 = int(rng.choice(np.array([0, T - K, T - K - 1, T - 5, int(rng.integers(0, T))]))); q = (c0 + np.arange(K)) & (T - 1); c = (c0 + K) & (T - 1)
    i, j = c & 511, int(np.argmax(d0 == edge)); d0[[i, j]] = d0[[j, i]]
    give(rng, x, o[:512], 0, d0)
    at = o[512:752].reshape(15, 16); give(rng, x, at, np.arange(1, 16)[:, None], rng.choice(rdp, (15, 16)))
    ix = np.zeros((16, T), np.int64); ix[0] = o[np.arange(T) & 511]; ix[1:] = at[np.arange(15)[:, None], rng.integers(0, 16, (15, T))]
    return x, ix, q, c, d0, o[752:]
def blank():
    return np.zeros((N, 8, 16, W), np.int64), np.zeros((N, 8, 16, T), np.int64), np.zeros((N, 8, K), np.int64), np.zeros((N, 8), np.int64)
def setup_inputs_calm(rng):
    reg = regions(rng); s, s2, s3, e = [int(v) for v in reg[1]]; rd = reg[3]; x, ix, q, c = blank(); m = R + 2
    for r in range(N):
        for g in range(8):
            xa, ia, qa, ca, d0, sp = group(rng, reg, (0, W - 1)[(r + g) & 1]); n = (r + g) % 4
            give(rng, xa, sp[:3], 0, np.array([s, s2, s3])); give(rng, xa, sp[3:18], np.arange(1, 16), np.full(15, e))
            ia[0, qa[0]] = sp[0]; ia[0, qa[3:m + 2]] = sp[0]; ia[0, qa[1]] = sp[1]; ia[0, qa[2]] = sp[2]; ia[1:, qa[1:3]] = sp[3:18][:, None]
            kk = int(rng.integers(1, 16)); give(rng, xa, np.array([s]), kk, np.array([s]))
            vic = qa[m + 2 + rng.permutation(K - m - 2)[:n + 1]]; ia[kk, vic[:n]] = s
            j = int(vic[n]); ed = np.zeros(16, np.int64); k2, k3, k4 = [int(v) for v in 1 + rng.permutation(15)[:3]]; a2, a3 = np.array([s2]), np.array([s3])
            if g == 1:
                w = 2184 & (W - 1); v = twin(rng, rd, w, 0, 0); ed[:] = 8
                give(rng, xa, a2, k2, np.array([v])); give(rng, xa, a3, k3, np.array([v ^ w])); ia[k2, j] = s2; ia[k3, j] = s3
            elif g == 3:
                k2 = int(rng.integers(2, 8)); k3 = 2 * k2 + 1; k4 = 1; ed[k2 + 2] = 8; ed[(k3 + 2) & 15] = 12
                give(rng, xa, a2, k2, np.array([twin(rng, rd, 8, 8, 0)])); give(rng, xa, a3, k3, np.array([twin(rng, rd, 4, 4, 4)])); ia[k2, j] = s2; ia[k3, j] = s3
            elif g == 5:
                ed[(k2 + 1) & 15] = 8; give(rng, xa, a2, k2, np.array([twin(rng, rd, 128, 0, 0)])); ia[k2, j] = s2
            elif g == 7:
                k2 = 2 * int(rng.integers(1, 8)); k3 = k2 + 1; k4 = 1; ed[(k3 + 2) & 15] = 1
                give(rng, xa, a2, k3, np.array([twin(rng, rd, 1, 3, 2)])); give(rng, xa, sp[19:20], k2, np.array([W - 1])); ia[k2, j] = sp[19]; ia[k3, j] = s2
            else:
                ed[(k2 + 3 + int(rng.integers(0, 13))) & 15] = 8; give(rng, xa, a2, k2, rng.choice(rd, 1)); ia[k2, j] = s2
            give(rng, xa, sp[18:19], k4, np.array([s2])); ia[k4, j] = sp[18]; xa[:, e] = ed
            x[r, g] = xa; ix[r, g] = ia; q[r, g] = qa; c[r, g] = ca
    return pack(x, ix, q, c)
def setup_inputs_corners(rng):
    reg = regions(rng); s, s2, e = int(reg[1][0]), int(reg[1][1]), int(reg[1][3]); x, ix, q, c = blank(); par = int(rng.integers(0, 2))
    for r in range(N):
        for g in range(8):
            xa, ia, qa, ca, d0, sp = group(rng, reg, (0, W - 1)[(r + g) & 1]); xa[:, e] = 8
            if r % 2 == par:
                z = s2 if g == 4 else s
                kk = int(rng.integers(1, 16)); give(rng, xa, np.array([z]), kk, rng.choice(reg[3], 1)); was = ia[kk].copy(); ia[kk] = z
                if g == 6: ia[0] = int(ia[0, qa[0]])
                if g % 4 == 1: j = np.array([(ca + K - 1) & (T - 1)])
                elif g % 4 == 2: j = np.array([ca])
                elif g % 4 == 3: j = np.nonzero(rng.random(T) < 0.5)[0]
                else: j = np.zeros(0, np.int64)
                ia[kk, j] = was[j]
            else:
                give(rng, xa, sp[:1], 0, np.array([s])); give(rng, xa, sp[33:48], np.arange(1, 16), np.full(15, e)); give(rng, xa, sp[48:49], 0, np.array([s2]))
                two = qa[1:3] if g % 2 == 0 else qa[R + 34:R + 36]
                if g % 2 == 0:
                    ia[0] = sp[0]
                    if g == 2: qa = np.full(K, qa[0])
                else:
                    ia[0, qa[:R + 2]] = sp[0]; j = qa[R + 2:R + 34]
                    give(rng, xa, sp[1:33], 7, d0[j & 511]); ia[7, j] = sp[1:33]
                if g != 2:
                    ia[0, two] = sp[48]; ia[1:, two] = sp[33:48][:, None]
            x[r, g] = xa; ix[r, g] = ia; q[r, g] = qa; c[r, g] = ca
    return pack(x, ix, q, c)
def setup_inputs_crowd(rng):
    reg = regions(rng); x, ix, q, c = blank(); al = np.arange(T)
    for r in range(N):
        kinds = rng.permutation(8)
        for g in range(8):
            xa, ia, qa, ca, d0, sp = group(rng, reg, (0, W - 1)[(r + g) & 1]); h = int(kinds[g])
            if h == 1:
                give(rng, xa, sp[:1], 15, d0[qa[:1] & 511]); ia[15, qa[K - 1]] = sp[0]
            if h == 2: ia[0] = int(ia[0, ca])
            if h == 3:
                j = int(qa[int(rng.choice(np.array([0, K >> 1, K - 1])))]); was = int(ia[0, j]); ia[0] = int(ia[0, ca]); ia[0, j] = was
            if h == 4: ia[0] = ia[0, (ca + rng.integers(0, 2, T)) & (T - 1)]
            if h == 5: ia[0] = ia[0, (ca + rng.integers(0, 3, T)) & (T - 1)]
            if h == 6:
                give(rng, xa, sp[:15], np.arange(1, 16), np.full(15, d0[qa[0] & 511])); kk = rng.integers(1, 16, T); m = al != qa[0]
                ia[kk[m], al[m]] = sp[kk[m] - 1]
            if h == 7:
                give(rng, xa, sp[:15], np.arange(1, 16), np.full(15, d0[ca & 511])); ia[0] = int(ia[0, ca]); ia[1:] = sp[:15][:, None]
            x[r, g] = xa; ix[r, g] = ia; q[r, g] = qa; c[r, g] = ca
    return pack(x, ix, q, c)
def setup_inputs_ends(rng):
    x = 15 * rng.integers(0, 2, (N, 8, 16, W)); x = np.where(rng.random((N, 8, 1, W)) < 0.5, x[:, :, :1], x)
    fr = rng.random((N, 8, W)) < 0.33; fr[..., 0] = False; fr[..., W - 1] = False
    x = np.where(fr[:, :, None], rng.integers(0, 16, x.shape), x)
    z = 15 * (rng.random((N, 8, 1)) < 0.25).astype(np.int64); x[..., 0] = z; x[..., W - 1] = 15 - z
    d, ix, q, c = blank(); c = (T - 1) * rng.integers(0, 2, (N, 8)); c[:, 0] = 0; c[:, 7] = T - 1
    for r in range(N):
        for g in range(8):
            end = rng.random(T) < 0.65; end[0] = True; end[T - 1] = True
            e = rng.integers(0, 2, (16, T)); e = np.where(rng.random(T) < 0.5, e[:1], e)
            if g % 2 == 0: e[:, 0] = 0
            e[:, T - 1] = rng.integers(0, 2, 16); e[0, T - 1] = 1; e[8, T - 1] = 0; e[15, T - 1] = 1
            ix[r, g] = np.where(end, e * (W - 1), rng.choice(np.nonzero(fr[r, g])[0], (16, T)))
            qa = rng.choice(np.nonzero(~end)[0], K); at = rng.permutation(K)[:2 * K // 3]
            qa[at] = (T - 1) * rng.integers(0, 2, len(at)); qa[K - 1] = T - 1; q[r, g] = qa
    return pack(x, ix, q, c)
def setup_inputs_spread(rng):
    e = rng.choice(np.array([0.5, 1.0, 1.0, 2.0, 3.0]), (N, 8, 1, 1)); i = rng.choice(np.array([1.0, 1.0, 2.0, 3.0]), (N, 8, 1, 1)); j = rng.choice(np.array([1.0, 2.0]), (N, 8, 1))
    x = np.minimum((16 * rng.random((N, 8, 16, W)) ** e).astype(np.int64), 15); ix = np.minimum((W * rng.random((N, 8, 16, T)) ** i).astype(np.int64), W - 1)
    q = np.minimum((T * rng.random((N, 8, K)) ** j).astype(np.int64), T - 1)
    return pack(x, ix, q, rng.integers(0, T, (N, 8)))
def check_inputs(d):
    bad = []
    for k, hi in (("rec", 15), ("idx", W - 1), ("que", T - 1), ("cur", T - 1)):
        v = np.asarray(d[k]).astype(np.float64)
        if not np.all((v >= 0) & (v <= hi)): bad.append("range of " + k)
        elif np.any(v != np.floor(v)): bad.append("whole numbers of " + k)
    return bad
def reference(rec, idx, que, cur):
    x = rec.astype(np.float32).astype(np.int64).reshape(N, 8, 16, W); ix = idx.astype(np.int64).reshape(N, 8, 16, T)
    q = que.astype(np.int64); c = cur.astype(np.int64).reshape(N, 8); kept = np.full((N, 8, 16, K), -1, np.int64); pl = np.arange(K)
    ra = np.arange(N)[:, None, None, None]; ga = np.arange(8)[None, :, None, None]; ka = np.arange(16)[None, None, :, None]
    for t in range(R):
        sr, sg = SR[t % len(SR)], SG[t % len(SG)]
        at = ix[ra, ga, ka, q[:, :, None, :]]
        d = (256 * x[ra, ga, ka, at] + 16 * x[ra, ga, (ka + 1) % 16, at] + x[ra, ga, (ka + 2) % 16, at]) & (W - 1)
        fresh = kept[:, :, 0] < 0; redo = ~fresh & np.any(d != kept, axis=2); sent = ~fresh & ~redo
        lock = np.full((N, 8, W), K, np.int64); np.minimum.at(lock, (ra[..., 0], ga[..., 0], d[:, :, 0]), np.where(sent, pl, K))
        low = np.min(np.take_along_axis(lock, d.reshape(N, 8, 16 * K), 2).reshape(N, 8, 16, K), axis=2)
        go = sent & (low >= pl)
        rr, gg, ii = np.nonzero(go); nm = d[rr, gg, :, ii]; ro, go_ = (rr + sr) % N, (gg + sg) % 8
        v = x[ro[:, None], go_[:, None], :, nm]
        x[ro, go_, :, nm[:, 0]] = (v[:, 0] + np.max(v[:, 1:], axis=1)) & 15
        o = np.argsort(np.where(go, 2, np.where(redo, 1, 0)), axis=2, kind="stable"); n = np.sum(go, axis=2)[..., None]
        tail = pl >= K - n
        q = np.where(tail, (c[..., None] + pl - (K - n)) & (T - 1), np.take_along_axis(q, o, 2))
        kept = np.where(tail[:, :, None], -1, np.take_along_axis(d, o[:, :, None, :], 3)); c = (c + n[..., 0]) & (T - 1)
    return {"yx": x.reshape(N, 128, W).astype(np.float32).astype(BF), "yq": q.astype(np.float32), "yd": kept.reshape(N, 128, K).astype(np.float32)}

@@ -1,0 +1,472 @@
+from concourse.mybir import AluOpType, ActivationFunctionType
+
+K = 192
+W = 4096
+WX = W + K
+NT = 2048
+NX = NT + 4 * K
+NW = NX + 2 * K
+SR, SG = (1, 5, 3), (0, 3, 1)
+BF, F, I, U = "bfloat16", "float32", "int32", "uint16"
+ZC = WX // 4
+CFG = {"a": (28, 32, 32), "b1": (32, 32, 32), "b": (40, 40, 40), "b4": (40, 40, 40), "d": (0, 64, 128, K), "d4": (0, 64, 128, K),
+       "kq": "S"}
+
+SCRATCH = {
+    "x": ("sbuf", [128, WX], BF), "idw": ("sbuf", [128, NW], I), "qw": ("sbuf", [128, NW], F), "z": ("sbuf", [128, ZC], BF),
+    "lt1": ("sbuf", [128, WX], BF), "lt2": ("sbuf", [128, WX], BF), "lt3": ("sbuf", [128, WX], BF), "lt4": ("sbuf", [128, WX], BF),
+    "ga": ("sbuf", [128, 16 * K], BF), "gb": ("sbuf", [128, 16 * K], BF), "gd": ("sbuf", [128, 16 * K], BF),
+    "sc": ("sbuf", [128, 16 * K], BF), "rm": ("sbuf", [128, 1024], BF), "wk": ("sbuf", [128, 2048], BF),
+    "w0": ("sbuf", [128, 256], BF), "o16": ("sbuf", [128, 256], BF), "o8": ("sbuf", [128, 256], BF),
+    "on16": ("sbuf", [128, 128], BF), "idb": ("sbuf", [128, 128], BF), "idf": ("sbuf", [128, 256], F),
+    "lt0": ("sbuf", [128, 128], BF), "ltri": ("sbuf", [128, 128], BF), "ones": ("sbuf", [128, 256], F),
+    "sel0": ("sbuf", [128, 256], F), "sel": ("sbuf", [128, 256], F),
+    "gm": ("sbuf", [128, 8], F), "di": ("sbuf", [128, 208], I), "dj": ("sbuf", [128, 208], I), "dm": ("sbuf", [128, 208], F),
+    "m1": ("sbuf", [128, K], BF), "m2": ("sbuf", [128, K], BF), "d0": ("sbuf", [128, K], F), "da": ("sbuf", [128, K], F),
+    "t1": ("sbuf", [128, K], F), "t2": ("sbuf", [128, K], F), "t3": ("sbuf", [128, K], F), "t4": ("sbuf", [128, K], F),
+    "t5": ("sbuf", [128, K], F), "t6": ("sbuf", [128, K], F), "t7": ("sbuf", [128, K], F),
+    "vc": ("sbuf", [128, K], BF), "thr": ("sbuf", [128, K], F), "hb": ("sbuf", [128, K], F),
+    "dum": ("sbuf", [128, 12], F), "col": ("sbuf", [128, 8], F), "wa": ("sbuf", [128, 16], F), "wb": ("sbuf", [128, 16], F),
+    "wc": ("sbuf", [128, 16], F), "wd": ("sbuf", [128, 16], F),
+    "qi": ("sbuf", [128, K], I), "qf": ("sbuf", [128, K], F), "ci": ("sbuf", [128, 8], I), "cf": ("sbuf", [128, 8], F),
+    "at": ("sbuf", [128, K], U), "nm": ("sbuf", [128, K + 16], F), "kp": ("sbuf", [128, K], F), "zs": ("sbuf", [128, 2 * K], F),
+    "ne": ("sbuf", [128, K], BF), "fr": ("sbuf", [128, K], BF), "ks": ("sbuf", [128, K], F), "eq": ("sbuf", [128, 2 * K], BF),
+    "ls": ("sbuf", [128, K], F), "ll": ("sbuf", [128, 16], U), "wf": ("sbuf", [128, K], BF), "gs": ("sbuf", [128, K], F),
+    "gl": ("sbuf", [128, 64], U), "glr": ("sbuf", [128, 64], U), "nl": ("sbuf", [128, 4 * K], U), "nlr": ("sbuf", [128, 4 * K], U),
+    "ys": ("sbuf", [128, K], F), "fw": ("sbuf", [128, 24], BF), "cz": ("sbuf", [128, 32], BF),
+    "ma": ("sbuf", [128, 12], F), "mb": ("sbuf", [128, 12], F), "dl": ("sbuf", [128, 16], U), "cc": ("sbuf", [128, 8], F),
+    "qs": ("sbuf", [128, K], F), "ql": ("sbuf", [128, 16], U), "kl": ("sbuf", [128, 16], U),
+    "s1": ("sbuf", [128, K], BF), "s2": ("sbuf", [128, K], BF), "lg": ("sbuf", [128, 2 * K], F), "rb": ("sbuf", [128, 2 * K], BF),
+    "pn": ("psum", [128, 512], F), "pk": ("psum", [128, 512], F), "pm": ("psum", [128, 512], F), "pl": ("psum", [128, 512], F),
+    "ps": ("psum", [128, 512], F), "pg": ("psum", [128, 512], F), "py": ("psum", [128, 512], F), "pr": ("psum", [128, 512], F),
+}
+PSUM = ("pn", "pk", "pm", "pl", "ps", "pg", "py", "pr")
+SEMAPHORES = (["cv", "cs", "cp", "cg", "sent", "lq", "li", "lr", "le", "lc", "z1", "z2", "z3", "z4", "oa", "ob", "oq", "od"]
+              + ["an%d" % t for t in range(1, 5)] + ["ag%d" % t for t in range(1, 5)])
+QSEM = {"V": "cv", "S": "cs", "P": "cp", "G": "cg"}
+
+
+def emit(g, T, ops):
+    eng = {"V": g.vector, "S": g.scalar, "P": g.tensor, "G": g, "Y": g.sync}
+    writer, readers = {}, {}
+    known = {q: {} for q in eng}
+    clock, waits, needed = [], [], set()
+    for n, o in enumerate(ops):
+        q = o["q"]
+        deps = set()
+        for k in o["r"]:
+            if k in writer:
+                deps.add(writer[k])
+            if k in PSUM:
+                deps.update(m for m in readers.get(k, []) if ops[m]["q"] != q)
+        for k in o["w"]:
+            if k in writer:
+                deps.add(writer[k])
+            deps.update(readers.get(k, []))
+        kn = known[q]
+        mine = []
+        for m in sorted(deps, reverse=True):
+            d = ops[m]
+            if d["remote"]:
+                continue
+            if d["dma"] is None and d["q"] == q and o["dma"] is None and q == "P":
+                continue
+            key = d["q"] if d["dma"] is None else "dma:" + d["dma"]
+            if kn.get(key, -1) >= m:
+                continue
+            mine.append(m)
+            needed.add(m)
+            for a, b in clock[m].items():
+                if kn.get(a, -1) < b:
+                    kn[a] = b
+            kn[key] = max(kn.get(key, -1), m)
+        ext = []
+        for s, v in o["ext"]:
+            if kn.get("ext:" + s, -1) < v:
+                ext.append((s, v))
+                kn["ext:" + s] = v
+        waits.append((mine, ext))
+        clock.append(dict(kn))
+        for k in o["r"]:
+            readers.setdefault(k, []).append(n)
+        for k in o["w"]:
+            writer[k] = n
+            readers[k] = []
+    count, total = {}, {}
+    for n, o in enumerate(ops):
+        if o["dma"] is not None:
+            total[o["dma"]] = total.get(o["dma"], 0) + 16
+        elif n in needed:
+            total[o["q"]] = total.get(o["q"], 0) + 1
+            count[n] = total[o["q"]]
+    seen = set()
+    for n, o in enumerate(ops):
+        e = eng[o["q"]]
+        mine, ext = waits[n]
+        for s, v in ext:
+            e.wait_ge(T.sem[s], v)
+        done = set()
+        for m in mine:
+            d = ops[m]
+            if d["dma"] is not None:
+                if d["dma"] not in done:
+                    e.wait_ge(T.sem[d["dma"]], total[d["dma"]])
+                    done.add(d["dma"])
+                    seen.add(d["dma"])
+            else:
+                e.wait_ge(T.sem[QSEM[d["q"]]], count[m])
+        ins = o["fn"]()
+        if o["dma"] is not None:
+            ins.then_inc(T.sem[o["dma"]], 16)
+        elif n in needed:
+            ins.then_inc(T.sem[QSEM[o["q"]]], 1)
+    for s in total:
+        if s not in QSEM and s not in seen:
+            g.wait_ge(T.sem[s], total[s])
+
+
+def rank_program(g, core, T, topo):
+    rank = T.rank_of(core)
+    if rank is None:
+        return
+    A, AF = AluOpType, ActivationFunctionType
+    V, S, P = g.vector, g.scalar, g.tensor
+    n = len(T.cores)
+    ne = min(len(topo.engines(a, b)) for a in T.cores for b in T.cores if a != b)
+    ops = []
+
+    def op(q, fn, r=(), w=(), ext=(), dma=None, remote=False):
+        ops.append({"q": q, "fn": fn, "r": list(r), "w": list(w), "ext": list(ext), "dma": dma, "remote": remote})
+
+    def ts(out, in0, s1, s2, o0, o1, r, w, ext=()):
+        if o1 is None:
+            op("V", lambda: V.tensor_scalar(out, in0, s1, None, o0), r, w, ext)
+        else:
+            op("V", lambda: V.tensor_scalar(out, in0, s1, s2, o0, o1), r, w, ext)
+
+    def tt(out, in0, in1, o, r, w, ext=()):
+        op("V", lambda: V.tensor_tensor(out, in0, in1, o), r, w, ext)
+
+    def cp(out, in_, r, w, ext=()):
+        op("V", lambda: V.tensor_copy(out, in_), r, w, ext)
+
+    def scan(out, d0, d1, init, o0, o1, r, w):
+        op("V", lambda: V.tensor_tensor_scan(out, d0, d1, init, o0, o1), r, w)
+
+    def ms(ap, c, w):
+        op("V", lambda: V.memset(ap, c), (), w)
+
+    def act(out, in_, r, w, func=None, bias=None, scale=None, ext=()):
+        if bias is None and scale is None:
+            op("S", lambda: S.activation(out, in_, func or AF.Copy), r, w, ext)
+        elif bias is None:
+            op("S", lambda: S.activation(out, in_, func or AF.Identity, scale=scale), r, w, ext)
+        else:
+            op("S", lambda: S.activation(out, in_, func or AF.Identity, bias=bias, scale=1.0 if scale is None else scale), r, w, ext)
+
+    def mm(out, lhsT, rhs, start, stop, r, w):
+        op("P", lambda: P.matmul(out, lhsT, rhs, start, stop), r, w)
+
+    def iota(out, pat, base, cm, w):
+        op("G", lambda: g.iota(out, pat, base, cm, allow_small_or_imprecise_dtypes=True), (), w)
+
+    def pick(out, in_, pat, cmp, fill, base, cm, r, w):
+        op("G", lambda: g.affine_select(out, in_, pat, cmp, fill, base, cm), r, w)
+
+    def load(out, in_, r, w, sem, q="Y", ext=()):
+        op(q, lambda: (g.sync if q == "Y" else g.scalar).dma_start(out, in_), r, w, ext, dma=sem)
+
+    def send(t, dst_ap, src_ap, sem, r):
+        dst = T.cores[(rank + SR[t % 3]) % n]
+        rid, pid, _ = topo.addr(dst)
+        mask = sum(1 << e for e in topo.engines(core, dst)[:ne])
+        op("G", lambda: g.remote_dma(dst_ap, src_ap, T.sem[sem], T.sem.sent, pid, rid, mask), r, (), remote=True)
+
+    def turned(buf, t):
+        a = 128 - 16 * SG[t % 3]
+        return buf[:, a:a + 128]
+
+    def back(buf, t):
+        a = 16 * SG[t % 3]
+        return buf[:, a:a + 128]
+
+    def clear_locks(t, ext=(), start=0):
+        for j in range(start, 4):
+            load(T["lt%d" % t][:, j * ZC:(j + 1) * ZC], T.z[:], ["z"], ["lt%d_%d" % (t, j)], "z%d" % t, ext=ext)
+
+    def gather(q, out, src, r, w, ext=(), **kw):
+        if q == "V":
+            cp(out, src, r, w, ext)
+        else:
+            act(out, src, r, w, ext=ext, **kw)
+
+    xw = T.x
+    DM = T.dm[:, 1:K + 1]
+    NM = T.nm[:, 8:K + 8]
+    BIG = float(2 ** 22)
+
+    def held(buf, t):
+        return buf[:, NW - K:NW] if t % 2 else buf[:, 0:K]
+
+    def window(buf, t):
+        return buf[:, K:NW] if t % 2 else buf[:, 0:NW - K]
+
+    load(T.qi[0:8, :], T.que[:], (), ["qi"], "lq", q="S")
+    load(T.idw[:, K:K + NT], T.idx[:], (), ["idw"], "li")
+    load(xw[:, 0:W], T.rec[:], (), ["x"], "lr")
+    ms(T.ones[:], 1.0, ["ones"])
+    op("G", lambda: g.iota(T.di[:], [[-1, 208]], K + 1 + 16, 1), (), ["di"])
+    pick(T.sel0[0:8, :], T.ones[0:8, :], [[0, 2], [1, 128]], A.is_ge, 0.0, 0, -16, ["ones"], ["sel0"])
+    pick(T.sel[0:8, :], T.sel0[0:8, :], [[0, 2], [-1, 128]], A.is_ge, 0.0, 15, 16, ["sel0"], ["sel"])
+    iota(T.t1[:], [[1, K]], W + 10, 0, ["t1"])
+    pick(T.idf[:], T.ones[:], [[0, 2], [-1, 128]], A.is_equal, 0.0, 0, 1, ["ones"], ["idf"])
+    ms(T.z[:], 0.0, ["z"])
+    ts(T.dj[:], T.di[:], 15, None, A.bitwise_and, None, ["di"], ["dj"])
+    ts(T.dm[:], T.dj[:], 0.0, None, A.is_equal, None, ["dj"], ["dm"])
+    act(T.t2[:], T.dm[:, 0:K], ["dm"], ["t2"], scale=4096.0)
+    act(T.t3[:], DM, ["dm"], ["t3"], scale=-8192.0)
+    ms(T.wk[:], 0.0, ["wk"])
+    ts(T.wa[:], T.dm[:, 1:17], 256.0, None, A.mult, None, ["dm"], ["wa"])
+    ts(T.wb[:], T.dm[:, 2:18], 16.0, None, A.mult, None, ["dm"], ["wb"])
+    ts(T.col[:, 0:1], T.dm[:, 16:17], -4096.0, 4096.0, A.mult, A.add, ["dm"], ["col0"])
+    tt(T.wc[:], T.wa[:], T.dm[:, 3:19], A.add, ["wa", "dm"], ["wc"])
+    tt(T.da[:], T.t2[:], T.t3[:], A.add, ["t2", "t3"], ["da"])
+    tt(T.wd[:], T.wc[:], T.wb[:], A.add, ["wc", "wb"], ["wd"])
+    cp(T.qf[0:8, :], T.qi[0:8, :], ["qi"], ["qf"])
+    mm(T.pk[:, 0:256], T.sel[0:8, 0:128], T.sel[0:8, :], True, True, ["sel"], ["pk"])
+    mm(T.pr[:, 0:K], T.sel[0:8, 0:128], T.qf[0:8, :], True, True, ["sel", "qf"], ["pr"])
+    act(T.gm[:], T.pk[:, 0:128:16], ["pk"], ["gm"])
+    for k in range(16):
+        act(T.wk[:, 129 * k:128 * (k + 1):16], T.gm[:], ["gm", "wd", "wk"], ["wk%d" % k], scale=T.wd[:, k:k + 1])
+    act(T.w0[:], T.pk[:, 0:256], ["pk", "wd"], ["w0"], scale=T.wd[:, 0:1])
+    act(T.o8[:], T.pk[:, 0:256], ["pk"], ["o8"], scale=8192.0)
+    act(T.m1[:], DM, ["dm"], ["m1"], scale=-BIG, bias=BIG)
+    act(T.m2[:], DM, ["dm"], ["m2"], scale=-BIG - 8192.0, bias=BIG)
+    act(T.idb[:], T.idf[:, 0:128], ["idf"], ["idb"])
+    tt(T.t4[:], T.t1[:], DM, A.mult, ["t1", "dm"], ["t4"])
+    scan(T.qs[:], T.da[:], T.pr[:, 0:K], 0.0, A.add, A.max, ["da", "pr"], ["qs"])
+    ts(T.d0[:], T.t4[:], -10.0, None, A.add, None, ["t4"], ["d0"])
+    ts(T.ql[:, 0:12], T.qs[:, 15:K:16], T.col[:, 0:1], None, A.subtract, None, ["qs", "col0"], ["ql"])
+    act(T.t5[:], DM, ["dm"], ["t5"], scale=1.0 / 32 - 1.0, bias=1.0)
+    act(T.t6[:], DM, ["dm"], ["t6"], scale=-float(2 ** 40), bias=float(2 ** 40))
+    act(held(T.qw, 1), T.pr[:, 0:K], ["pr"], ["qh1"])
+    act(T.o16[:], T.pk[:, 0:256], ["pk"], ["o16"], scale=16384.0)
+    act(T.on16[:], T.pk[:, 0:128], ["pk"], ["on16"], scale=-16384.0)
+    iota(T.hb[:], [[1, K]], NX, 0, ["hb"])
+    iota(T.qw[:, K:K + NT], [[1, NT]], 0, 0, ["qw"])
+    pick(T.lt0[:], T.o8[:, 0:128], [[1, 128]], A.is_ge, 0.0, 0, -1, ["o8"], ["lt0"])
+    pick(T.ltri[:], T.lt0[:], [[1, 128]], A.not_equal, float(2 ** 23), 0, -1, ["lt0"], ["ltri"])
+    ms(xw[:, W:WX], 0.0, ["xd"])
+    ms(T.cz[:, 0:1], 12.0, ["cz0"])
+    ms(T.nm[:, 0:8], -1.0, ["nma"])
+    ms(T.nm[:, K + 8:K + 16], -1.0, ["nmb"])
+    ms(T.zs[:, 0:K], 0.0, ["zsd"])
+    ms(T.lt1[:, 0:2 * ZC], 0.0, ["lt1_0", "lt1_1"])
+    scan(T.vc[:], T.t5[:], T.z[:, 0:K], float(2 ** 30), A.mult, A.add, ["t5", "z"], ["vc"])
+    ts(T.col[:, 1:2], T.dj[:, 1:2], float(1024 - W - 10), None, A.add, None, ["dj"], ["col1"])
+    ts(T.t7[:], T.vc[:], 24.0, None, A.mult, None, ["vc"], ["t7"])
+    ts(T.dum[:], T.t1[:, 0:K:16], T.col[:, 1:2], 8192.0, A.add, A.mult, ["t1", "col1"], ["dum"])
+    tt(T.thr[:], T.t7[:], T.t6[:], A.max, ["t7", "t6"], ["thr"])
+    clear_locks(1, start=2)
+    cp(T.at[:], T.idw[:, K:K + NT].indirect(T.ql[:, 0:12]), ["idw", "ql"], ["at"])
+    WK = ["wk%d" % k for k in range(16)]
+
+    def masks(t):
+        mm(T.pm[:, 0:K], T.idb[:], T.m1[:], True, False, ["idb", "m1"], ["pm"])
+        mm(T.pl[:, 0:K], T.idb[:], T.m2[:], True, False, ["idb", "m2"], ["pl"])
+        mm(T.pg[:, 0:K], T.idb[:], T.m1[:], True, False, ["idb", "m1"], ["pg"])
+        mm(T.py[:, 0:K], T.idb[:], T.m1[:], True, False, ["idb", "m1"], ["py"])
+
+    def shared(buf, name, win, lst, o, c, v, r, order="VS"):
+        a = 64 * c
+        for e in order:
+            lo, hi = (a, a + v) if e == "V" else (a + v, a + 64)
+            if hi > lo:
+                gather(e, buf[:, 16 * lo:16 * hi], win[:, 0:W].indirect(lst[:, o + lo:o + hi]), r, ["%s%s%d" % (name, e, c)])
+        return ["%s%s%d" % (name, e, c) for e in "VS"]
+
+    def names(share, before=None):
+        for c in range(3):
+            a = 64 * c
+            keys = shared(T.ga, "ga", xw, T.at, 0, c, share[c], ["x", "at"], "SV")
+            for k in range(16):
+                mm(T.pn[:, a:a + 64], T.wk[:, 128 * k:128 * (k + 1)], T.ga[:, 16 * a + k:16 * (a + 64):16], k == 0, k == 15,
+                   keys + WK, ["pn"])
+
+    GA = ["ga%s%d" % (e, c) for e in "VS" for c in range(3)]
+
+    def turn_list(t, src, key):
+        mm(T.pr[:, 0:K], turned(T.idf, t), src, True, True, ["idf", key], ["pr"])
+
+    def send_list(t):
+        o = K * (t - 1)
+        cp(T.nl[:, o:o + K], T.pr[:, 0:K], ["pr"], ["nl%d" % t])
+        send(t, T.nlr[:, o:o + K], T.nl[:, o:o + K], "an%d" % t, ["nl%d" % t])
+
+    def digits(t, c, cut, power):
+        a, b, o = cut[c], cut[c + 1], K * (t - 1)
+        kw = {"func": AF.Exp, "scale": 3.0, "bias": -24.0} if power else {}
+        gather("S", T.gd[:, 16 * a:16 * b], xw[:, 0:W].indirect(T.nlr[:, o + a:o + b]), ["x"], ["gd%d" % c],
+               ext=[("an%d" % t, ne)], **kw)
+
+    def sums(a, b, keys):
+        mm(T.pn[:, K + a:K + b], T.idb[:], T.gd[:, 16 * a:16 * b:16], True, True, ["idb"] + keys, ["pn"])
+        for k in range(1, 16):
+            mm(T.pn[:, a:b], T.idb[:], T.gd[:, 16 * a + k:16 * b:16], k == 1, k == 15, ["idb"] + keys, ["pn"])
+
+    def logs():
+        act(T.lg[:], T.pn[:, 0:2 * K], ["pn"], ["lg"], func=AF.Ln)
+        act(T.rb[:], T.lg[:], ["lg"], ["rb"], scale=1.0 / 3, bias=130.0 + 8.0 - 0.45)
+        mm(T.pk[:, 0:K], T.idb[:], T.rb[:, 0:K], True, False, ["idb", "rb"], ["pk"])
+        mm(T.pk[:, 0:K], T.idb[:], T.rb[:, K:2 * K], False, True, ["idb", "rb"], ["pk"])
+        mm(T.pn[:, 0:K], T.idb[:], T.rb[:, 0:K], True, False, ["idb", "rb"], ["pn"])
+        mm(T.pn[:, 0:K], T.idb[:], T.rb[:, K:2 * K], False, True, ["idb", "rb"], ["pn"])
+        act(T.s1[:], T.pn[:, 0:K], ["pn"], ["s1"], bias=-260.0)
+
+    def wraps():
+        ts(T.s2[:], T.pk[:, 0:K], 276.0, -16.0, A.is_ge, A.mult, ["pk"], ["s2"])
+
+    def largest(c):
+        scan(T.sc[:, 1024 * c:1024 * (c + 1)], T.rm[:], T.gd[:, 1024 * c:1024 * (c + 1)], 0.0, A.min, A.max,
+             ["rm", "gd%d" % c], ["sc%d" % c])
+
+    def new_digits():
+        tt(T.s1[:], T.sc[:, 0:16 * K:16], T.sc[:, 15:16 * K:16], A.add, ["sc0", "sc1", "sc2"], ["s1"])
+        ts(T.s2[:], T.s1[:], 16.0, -16.0, A.is_ge, A.mult, ["s1"], ["s2"])
+
+    def write_records(t, power):
+        o = 16 * (t - 1)
+        out = xw[:, 0:WX].indirect(T.glr[:, o:o + 12])
+        if power:
+            wraps()
+        tt(out, T.s1[:], T.s2[:], A.add, ["s1", "s2", "xd"], ["x"], ext=[("ag%d" % t, ne)])
+
+    masks(1)
+    names((32, 32, 32))
+    cp(held(T.idw, 1), T.at[:], ["at"], ["ah1"])
+    for t in range(1, 5):
+        first, last = t == 1, t == 4
+        power = not first
+        cut = (0, 64, 128, K) if first else CFG["d4"] if last else CFG["d"]
+        lt = T["lt%d" % t]
+        LT = ["lt%d_%d" % (t, j) for j in range(4)]
+        g0 = T.ga[:, 0:16 * K:16]
+        if first:
+            act(NM, T.pn[:, 0:K], ["pn"], ["nm"])
+        else:
+            tt(T.ne[:], T.pn[:, 0:K], T.kp[:], A.not_equal, ["pn", "kp"], ["ne"])
+            digits(t, 0, cut, power)
+            act(NM, T.pn[:, 0:K], ["pn"], ["nm"])
+        mm(T.pm[:, 0:K], turned(T.w0, t), g0, False, first, GA + ["w0"], ["pm"])
+        mm(T.pk[:, 0:K], turned(T.w0, t), g0, True, first, GA + ["w0"], ["pk"])
+        mm(T.pl[:, 0:K], turned(T.w0, t), g0, False, False, GA + ["w0"], ["pl"])
+        if first:
+            turn_list(1, NM, "nm")
+        else:
+            mm(T.pm[:, 0:K], turned(T.o16, t), T.ne[:], False, True, ["o16", "ne"], ["pm"])
+            mm(T.pk[:, 0:K], turned(T.o16, t), T.ne[:], False, True, ["o16", "ne"], ["pk"])
+            mm(T.pl[:, 0:K], turned(T.o16, t), T.ne[:], False, False, ["o16", "ne"], ["pl"])
+        mm(T.pg[:, 0:K], turned(T.w0, t), g0, False, False, GA + ["w0"], ["pg"])
+        if not first:
+            mm(T.pg[:, 0:K], turned(T.o16, t), T.ne[:], False, False, ["o16", "ne"], ["pg"])
+            mm(T.py[:, 0:K], T.on16[:], T.ne[:], False, False, ["on16", "ne"], ["py"])
+            mm(T.py[:, 0:K], T.idb[:], T.fr[:], False, False, ["idb", "fr"], ["py"])
+        scan(T.ks[:], T.d0[:], T.pm[:, 0:K], -5.0, A.max, A.min, ["d0", "pm"], ["ks"])
+        tt(T.eq[:, 0:K], T.pk[:, 0:K], T.ks[:], A.is_equal, ["pk", "ks"], ["eq0"])
+        tt(T.eq[:, K + 16:2 * K], T.pk[:, 16:K], T.ks[:, 0:K - 16], A.is_equal, ["pk", "ks"], ["eq1"])
+        mm(T.pl[:, 0:K], T.o8[:, 0:128], T.eq[:, 0:K], False, False, ["o8", "eq0"], ["pl"])
+        mm(T.pl[:, 16:K], T.o8[:, 0:128], T.eq[:, K + 16:2 * K], False, True, ["o8", "eq1"], ["pl"])
+        if first:
+            send_list(1)
+            op("G", lambda: g.dma_start(T.ci[0:8, 0:1], T.cur[:], allow_slow_non_contiguous=True), (), ["ci"], dma="lc")
+            iota(T.rm[:], [[0, 64], [16, 16]], -16, 0, ["rm"])
+            iota(T.qw[:, K + NT:K + NX], [[1, NX - NT]], 0, 0, ["qe"])
+            load(T.idw[:, K + NT:K + NX], T.idx[:, 0:NX - NT], (), ["ide"], "le", ext=[("an1", ne)])
+        else:
+            digits(t, 1, cut, power)
+        if not last:
+            clear_locks(t + 1, ext=[("an%d" % t, ne)])
+        scan(T.ls[:], T.d0[:], T.pl[:, 0:K], -5.0, A.max, A.min, ["d0", "pl"], ["ls"])
+        cp(T.ll[:, 0:12], T.ls[:, 15:K:16], ["ls"], ["ll"])
+        for j in range(5, -1, -1):
+            cp(lt[:, 0:WX].indirect(T.ll[:, 2 * j:2 * j + 2]), T.vc[:, 32 * j:32 * j + 32], ["vc", "ll"], LT)
+        if power:
+            sums(0, cut[1], ["gd0"])
+            sums(cut[1], cut[2], ["gd1"])
+        share = CFG["b1"] if first else CFG["b4"] if last else CFG["b"]
+        for c in range(3):
+            a = 64 * c
+            keys = shared(T.gb, "gb", lt, T.nl, K * (t - 1), c, share[c], LT + ["nl%d" % t])
+            for k in range(16):
+                mm(T.ps[:, a:a + 64], T.idb[:], T.gb[:, 16 * a + k:16 * (a + 64):16], k == 0, k == 15, keys + ["idb"], ["ps"])
+        if first:
+            cp(T.cf[0:8, 0:1], T.ci[0:8, 0:1], ["ci"], ["cf"])
+            mm(T.pr[:, 256:257], T.sel[0:8, 0:128], T.cf[0:8, 0:1], True, True, ["sel", "cf"], ["pr"])
+            digits(1, 0, cut, False)
+            act(T.cc[:, 0:1], T.pr[:, 256:257], ["pr"], ["cc0"])
+        else:
+            digits(t, 2, cut, power)
+        tt(T.wf[:], T.ps[:, 0:K], T.thr[:], A.is_ge, ["ps", "thr"], ["wf"])
+        mm(T.pg[:, 0:K], T.o8[:, 0:128], T.wf[:], False, True, ["o8", "wf"], ["pg"])
+        mm(T.py[:, 0:K], back(T.o8, t), T.wf[:], False, True, ["o8", "wf"], ["py"])
+        scan(T.gs[:], T.d0[:], T.pg[:, 0:K], -5.0, A.max, A.min, ["d0", "pg"], ["gs"])
+        o = 16 * (t - 1)
+        cp(T.gl[:, o:o + 12], T.gs[:, 15:K:16], ["gs"], ["gl%d" % t])
+        send(t, T.glr[:, o:o + 12], T.gl[:, o:o + 12], "ag%d" % t, ["gl%d" % t])
+        if power:
+            sums(cut[2], K, ["gd2"])
+        scan(T.ys[:], T.d0[:], T.py[:, 0:K], -5.0, A.max, A.min, ["d0", "py"], ["ys"])
+        ts(T.fw[:, 0:12], T.ys[:, 15:K:16], 0.0, None, A.is_gt, None, ["ys"], ["fw0"])
+        ts(T.fw[:, 12:24], T.ys[:, 15:K:16], 0.0, None, A.is_lt, None, ["ys"], ["fw1"])
+        scan(T.cz[:, 1:25], T.z[:, 0:24], T.fw[:], 12.0, A.add, A.add, ["z", "fw0", "fw1"], ["cz"])
+        mm(T.ps[:, 256:281], T.o8[:, 0:128], T.cz[:, 0:25], True, False, ["o8", "cz", "cz0"], ["ps"])
+        mm(T.ps[:, 256:280], T.ltri[:], T.fw[:], False, True, ["ltri", "fw0", "fw1"], ["ps"])
+        ts(T.cc[:, t:t + 1], T.ps[:, 280:281], -1.0 / 8192, T.cc[:, t - 1:t], A.mult, A.add, ["ps", "cc%d" % (t - 1)], ["cc%d" % t])
+        tt(T.ma[:], T.ps[:, 256:268], T.dum[:], A.max, ["ps", "dum"], ["ma"])
+        a = 2 * K * t + (0 if t % 2 else K)
+        ts(T.zs[:, K:2 * K], T.qw[:, a:a + K], T.cc[:, t:t + 1], None, A.add, None, ["qw", "cc%d" % t], ["zs"])
+        if first:
+            digits(1, 1, cut, False)
+            digits(1, 2, cut, False)
+        else:
+            logs()
+        tt(T.mb[:], T.ps[:, 268:280], T.ma[:], A.max, ["ps", "ma"], ["mb"])
+        ts(T.dl[:, 0:12], T.mb[:], 1.0 / 8192, -1024.0, A.mult, A.add, ["mb"], ["dl"])
+        cp(T.zs[:, 0:2 * K].indirect(T.dl[:, 0:12]), T.hb[:] if t % 2 else T.qw[:, K:2 * K], ["hb", "qw", "dl", "zsd", "zs"], ["zs"])
+        scan(T.qs[:], T.da[:], T.zs[:, K:2 * K], 0.0, A.add, A.max, ["da", "zs"], ["qs"])
+        if t % 2:
+            ts(T.kl[:, 0:12], T.qs[:, 15:K:16], T.col[:, 0:1], float(NX - 8), A.subtract, A.subtract, ["qs", "col0"], ["kl"])
+        else:
+            ts(T.kl[:, 0:12], T.qs[:, 15:K:16], T.col[:, 0:1], float(K), A.subtract, A.min, ["qs", "col0"], ["kl"])
+        ts(T.ql[:, 0:12], T.qs[:, 15:K:16], T.col[:, 0:1], None, A.subtract, None, ["qs", "col0"], ["ql"])
+        nw = T.nm[:, 0:K + 8] if t % 2 else T.nm[:, 8:K + 16]
+        late = power and not last and CFG["kq"] == "S"
+        gather("S" if late else "V", T.kp[:], nw.indirect(T.kl[:, 0:12]), ["nm", "nma", "nmb", "kl"], ["kp"])
+        qh, qh2 = "qh%d" % (t % 2), "qh%d" % ((t + 1) % 2)
+        if last:
+            load(T.yd[:], T.kp[:], ["kp"], (), "od")
+            cp(held(T.qw, t + 1), window(T.qw, t).indirect(T.ql[:, 0:12]), ["qw", "qe", qh, "ql"], [qh2])
+            load(T.yq[:], T.qw[0:128:16, NW - K:NW], [qh2], (), "oq")
+            write_records(t, power)
+            load(T.yx[0:64, :], xw[0:64, 0:W], ["x"], (), "oa")
+            load(T.yx[64:128, :], xw[64:128, 0:W], ["x"], (), "ob", q="S")
+        else:
+            turn_list(t + 1, T.kp[:], "kp")
+            masks(t + 1)
+            cp(T.at[:], window(T.idw, t).indirect(T.ql[:, 0:12]), ["idw", "ide", "ah%d" % (t % 2), "ql"], ["at"])
+            if not late:
+                send_list(t + 1)
+            if first:
+                for c in range(3):
+                    largest(c)
+                new_digits()
+            act(T.fr[:], T.kp[:], ["kp"], ["fr"], func=AF.Relu, scale=-float(2 ** 20))
+            act(held(T.qw, t + 1), window(T.qw, t).indirect(T.ql[:, 0:12]), ["qw", "qe", qh, "ql"], [qh2])
+            write_records(t, power)
+            if late:
+                send_list(t + 1)
+            names(CFG["a"])
+            if t < 3:
+                cp(held(T.idw, t + 1), T.at[:], ["at"], ["ah%d" % ((t + 1) % 2)])
+    emit(g, T, ops)
+    g.wait_ge(T.sem.sent, 8 * ne)

@@ -9,17 +9,18 @@ NW = NX + 2 * K
 SR, SG = (1, 5, 3), (0, 3, 1)
 BF, F, I, U = "bfloat16", "float32", "int32", "uint16"
 ZC = WX // 4
-CFG = {"a": (28, 32, 32), "b1": (32, 32, 32), "b": (40, 40, 40), "b4": (40, 40, 40), "d": (0, 64, 128, K), "d4": (0, 64, 128, K),
-       "kq": "S"}
+CFG = {"a": (38, 32, 32), "b1": (32, 32, 32), "b": (32, 32, 30), "b4": (32, 32, 30), "d": (0, 64, 136, K), "d4": (0, 64, 132, K),
+       "kq": "V", "nl": 1, "al": 1}
 
 SCRATCH = {
     "x": ("sbuf", [128, WX], BF), "idw": ("sbuf", [128, NW], I), "qw": ("sbuf", [128, NW], F), "z": ("sbuf", [128, ZC], BF),
-    "lt1": ("sbuf", [128, WX], BF), "lt2": ("sbuf", [128, WX], BF), "lt3": ("sbuf", [128, WX], BF), "lt4": ("sbuf", [128, WX], BF),
+    "lt1": ("sbuf", [128, WX], BF), "vc2": ("sbuf", [128, K], BF), "thr2": ("sbuf", [128, K], F),
     "ga": ("sbuf", [128, 16 * K], BF), "gb": ("sbuf", [128, 16 * K], BF), "gd": ("sbuf", [128, 16 * K], BF),
     "sc": ("sbuf", [128, 16 * K], BF), "rm": ("sbuf", [128, 1024], BF), "wk": ("sbuf", [128, 2048], BF),
     "w0": ("sbuf", [128, 256], BF), "o16": ("sbuf", [128, 256], BF), "o8": ("sbuf", [128, 256], BF),
-    "on16": ("sbuf", [128, 128], BF), "idb": ("sbuf", [128, 128], BF), "idf": ("sbuf", [128, 256], F),
-    "lt0": ("sbuf", [128, 128], BF), "ltri": ("sbuf", [128, 128], BF), "ones": ("sbuf", [128, 256], F),
+    "on16": ("sbuf", [128, 256], BF), "id2": ("sbuf", [128, 256], BF), "idf": ("sbuf", [128, 256], F), "o1": ("sbuf", [128, 256], BF),
+    "lt0": ("sbuf", [128, 256], BF), "ltri": ("sbuf", [128, 256], BF), "ltn": ("sbuf", [128, 256], BF), "ones": ("sbuf", [128, 256], F),
+    "nw": ("sbuf", [128, NW], F), "gw": ("sbuf", [128, 24], BF),
     "sel0": ("sbuf", [128, 256], F), "sel": ("sbuf", [128, 256], F),
     "gm": ("sbuf", [128, 8], F), "di": ("sbuf", [128, 208], I), "dj": ("sbuf", [128, 208], I), "dm": ("sbuf", [128, 208], F),
     "m1": ("sbuf", [128, K], BF), "m2": ("sbuf", [128, K], BF), "d0": ("sbuf", [128, K], F), "da": ("sbuf", [128, K], F),
@@ -29,19 +30,19 @@ SCRATCH = {
     "dum": ("sbuf", [128, 12], F), "col": ("sbuf", [128, 8], F), "wa": ("sbuf", [128, 16], F), "wb": ("sbuf", [128, 16], F),
     "wc": ("sbuf", [128, 16], F), "wd": ("sbuf", [128, 16], F),
     "qi": ("sbuf", [128, K], I), "qf": ("sbuf", [128, K], F), "ci": ("sbuf", [128, 8], I), "cf": ("sbuf", [128, 8], F),
-    "at": ("sbuf", [128, K], U), "nm": ("sbuf", [128, K + 16], F), "kp": ("sbuf", [128, K], F), "zs": ("sbuf", [128, 2 * K], F),
+    "at": ("sbuf", [128, K], U), "kp": ("sbuf", [128, K], F), "zs": ("sbuf", [128, 2 * K], F),
     "ne": ("sbuf", [128, K], BF), "fr": ("sbuf", [128, K], BF), "ks": ("sbuf", [128, K], F), "eq": ("sbuf", [128, 2 * K], BF),
     "ls": ("sbuf", [128, K], F), "ll": ("sbuf", [128, 16], U), "wf": ("sbuf", [128, K], BF), "gs": ("sbuf", [128, K], F),
     "gl": ("sbuf", [128, 64], U), "glr": ("sbuf", [128, 64], U), "nl": ("sbuf", [128, 4 * K], U), "nlr": ("sbuf", [128, 4 * K], U),
     "ys": ("sbuf", [128, K], F), "fw": ("sbuf", [128, 24], BF), "cz": ("sbuf", [128, 32], BF),
     "ma": ("sbuf", [128, 12], F), "mb": ("sbuf", [128, 12], F), "dl": ("sbuf", [128, 16], U), "cc": ("sbuf", [128, 8], F),
-    "qs": ("sbuf", [128, K], F), "ql": ("sbuf", [128, 16], U), "kl": ("sbuf", [128, 16], U),
+    "qs": ("sbuf", [128, K], F), "ql": ("sbuf", [128, 16], U),
     "s1": ("sbuf", [128, K], BF), "s2": ("sbuf", [128, K], BF), "lg": ("sbuf", [128, 2 * K], F), "rb": ("sbuf", [128, 2 * K], BF),
     "pn": ("psum", [128, 512], F), "pk": ("psum", [128, 512], F), "pm": ("psum", [128, 512], F), "pl": ("psum", [128, 512], F),
     "ps": ("psum", [128, 512], F), "pg": ("psum", [128, 512], F), "py": ("psum", [128, 512], F), "pr": ("psum", [128, 512], F),
 }
 PSUM = ("pn", "pk", "pm", "pl", "ps", "pg", "py", "pr")
-SEMAPHORES = (["cv", "cs", "cp", "cg", "sent", "lq", "li", "lr", "le", "lc", "z1", "z2", "z3", "z4", "oa", "ob", "oq", "od"]
+SEMAPHORES = (["cv", "cs", "cp", "cg", "sent", "lq", "li", "lr", "le", "lc", "z1", "oa", "ob", "oq", "od"]
               + ["an%d" % t for t in range(1, 5)] + ["ag%d" % t for t in range(1, 5)])
 QSEM = {"V": "cv", "S": "cs", "P": "cp", "G": "cg"}
 
@@ -202,7 +203,7 @@ def rank_program(g, core, T, topo):
 
     xw = T.x
     DM = T.dm[:, 1:K + 1]
-    NM = T.nm[:, 8:K + 8]
+    IDB = T.id2[:, 0:128]
     BIG = float(2 ** 22)
 
     def held(buf, t):
@@ -225,6 +226,9 @@ def rank_program(g, core, T, topo):
     ts(T.dm[:], T.dj[:], 0.0, None, A.is_equal, None, ["dj"], ["dm"])
     act(T.t2[:], T.dm[:, 0:K], ["dm"], ["t2"], scale=4096.0)
     act(T.t3[:], DM, ["dm"], ["t3"], scale=-8192.0)
+    act(T.t5[:], DM, ["dm"], ["t5"], scale=1.0 / 32 - 1.0, bias=1.0)
+    act(T.m1[:], DM, ["dm"], ["m1"], scale=-BIG, bias=BIG)
+    act(T.m2[:], DM, ["dm"], ["m2"], scale=-BIG - 8192.0, bias=BIG)
     ms(T.wk[:], 0.0, ["wk"])
     ts(T.wa[:], T.dm[:, 1:17], 256.0, None, A.mult, None, ["dm"], ["wa"])
     ts(T.wb[:], T.dm[:, 2:18], 16.0, None, A.mult, None, ["dm"], ["wb"])
@@ -238,44 +242,35 @@ def rank_program(g, core, T, topo):
     act(T.gm[:], T.pk[:, 0:128:16], ["pk"], ["gm"])
     for k in range(16):
         act(T.wk[:, 129 * k:128 * (k + 1):16], T.gm[:], ["gm", "wd", "wk"], ["wk%d" % k], scale=T.wd[:, k:k + 1])
-    act(T.w0[:], T.pk[:, 0:256], ["pk", "wd"], ["w0"], scale=T.wd[:, 0:1])
     act(T.o8[:], T.pk[:, 0:256], ["pk"], ["o8"], scale=8192.0)
-    act(T.m1[:], DM, ["dm"], ["m1"], scale=-BIG, bias=BIG)
-    act(T.m2[:], DM, ["dm"], ["m2"], scale=-BIG - 8192.0, bias=BIG)
-    act(T.idb[:], T.idf[:, 0:128], ["idf"], ["idb"])
+    act(T.w0[:], T.pk[:, 0:256], ["pk", "wd"], ["w0"], scale=T.wd[:, 0:1])
+    act(T.id2[:], T.idf[:], ["idf"], ["idb"])
     tt(T.t4[:], T.t1[:], DM, A.mult, ["t1", "dm"], ["t4"])
     scan(T.qs[:], T.da[:], T.pr[:, 0:K], 0.0, A.add, A.max, ["da", "pr"], ["qs"])
     ts(T.d0[:], T.t4[:], -10.0, None, A.add, None, ["t4"], ["d0"])
     ts(T.ql[:, 0:12], T.qs[:, 15:K:16], T.col[:, 0:1], None, A.subtract, None, ["qs", "col0"], ["ql"])
-    act(T.t5[:], DM, ["dm"], ["t5"], scale=1.0 / 32 - 1.0, bias=1.0)
-    act(T.t6[:], DM, ["dm"], ["t6"], scale=-float(2 ** 40), bias=float(2 ** 40))
     act(held(T.qw, 1), T.pr[:, 0:K], ["pr"], ["qh1"])
-    act(T.o16[:], T.pk[:, 0:256], ["pk"], ["o16"], scale=16384.0)
-    act(T.on16[:], T.pk[:, 0:128], ["pk"], ["on16"], scale=-16384.0)
     iota(T.hb[:], [[1, K]], NX, 0, ["hb"])
-    iota(T.qw[:, K:K + NT], [[1, NT]], 0, 0, ["qw"])
-    pick(T.lt0[:], T.o8[:, 0:128], [[1, 128]], A.is_ge, 0.0, 0, -1, ["o8"], ["lt0"])
-    pick(T.ltri[:], T.lt0[:], [[1, 128]], A.not_equal, float(2 ** 23), 0, -1, ["lt0"], ["ltri"])
-    ms(xw[:, W:WX], 0.0, ["xd"])
-    ms(T.cz[:, 0:1], 12.0, ["cz0"])
-    ms(T.nm[:, 0:8], -1.0, ["nma"])
-    ms(T.nm[:, K + 8:K + 16], -1.0, ["nmb"])
-    ms(T.zs[:, 0:K], 0.0, ["zsd"])
-    ms(T.lt1[:, 0:2 * ZC], 0.0, ["lt1_0", "lt1_1"])
-    scan(T.vc[:], T.t5[:], T.z[:, 0:K], float(2 ** 30), A.mult, A.add, ["t5", "z"], ["vc"])
-    ts(T.col[:, 1:2], T.dj[:, 1:2], float(1024 - W - 10), None, A.add, None, ["dj"], ["col1"])
-    ts(T.t7[:], T.vc[:], 24.0, None, A.mult, None, ["vc"], ["t7"])
-    ts(T.dum[:], T.t1[:, 0:K:16], T.col[:, 1:2], 8192.0, A.add, A.mult, ["t1", "col1"], ["dum"])
-    tt(T.thr[:], T.t7[:], T.t6[:], A.max, ["t7", "t6"], ["thr"])
-    clear_locks(1, start=2)
+    iota(xw[:, W:WX], [[0, K]], 0, 0, ["xd"])
+    iota(T.zs[:, 0:K], [[0, K]], 0, 0, ["zsd"])
+    iota(T.cz[:, 0:1], [[0, 1]], 12, 0, ["cz0"])
+    iota(T.fw[:], [[-1, 2], [0, 12]], 1, 0, ["fw0", "fw1"])
+    iota(T.gw[:, 12:24], [[0, 12]], 0, 0, ["gw1"])
+    iota(T.nw[:, K + NT:K + NX], [[0, NX - NT]], -1, 0, ["nwb"])
+    pick(T.lt0[:], T.o8[:], [[0, 2], [1, 128]], A.is_ge, 0.0, 0, -1, ["o8"], ["lt0"])
+    pick(T.ltri[:], T.lt0[:], [[0, 2], [1, 128]], A.not_equal, float(2 ** 23), 0, -1, ["lt0"], ["ltri"])
+    clear_locks(1, start=1)
+    load(T.idw[:, K + NT:K + NX], T.idx[:, 0:NX - NT], (), ["ide"], "le")
+    ms(T.lt1[:, 0:ZC], 0.0, ["lt1_0"])
     cp(T.at[:], T.idw[:, K:K + NT].indirect(T.ql[:, 0:12]), ["idw", "ql"], ["at"])
     WK = ["wk%d" % k for k in range(16)]
 
     def masks(t):
-        mm(T.pm[:, 0:K], T.idb[:], T.m1[:], True, False, ["idb", "m1"], ["pm"])
-        mm(T.pl[:, 0:K], T.idb[:], T.m2[:], True, False, ["idb", "m2"], ["pl"])
-        mm(T.pg[:, 0:K], T.idb[:], T.m1[:], True, False, ["idb", "m1"], ["pg"])
-        mm(T.py[:, 0:K], T.idb[:], T.m1[:], True, False, ["idb", "m1"], ["py"])
+        mm(T.pm[:, 0:K], IDB, T.m1[:], True, False, ["idb", "m1"], ["pm"])
+        mm(T.pl[:, 0:K], IDB, T.m2[:], True, False, ["idb", "m2"], ["pl"])
+        mm(T.pg[:, 0:K], IDB, T.m1[:], True, False, ["idb", "m1"], ["pg"])
+        if t > 1:
+            mm(T.py[:, 0:K], IDB, T.m1[:], True, False, ["idb", "m1"], ["py"])
 
     def shared(buf, name, win, lst, o, c, v, r, order="VS"):
         a = 64 * c
@@ -285,7 +280,7 @@ def rank_program(g, core, T, topo):
                 gather(e, buf[:, 16 * lo:16 * hi], win[:, 0:W].indirect(lst[:, o + lo:o + hi]), r, ["%s%s%d" % (name, e, c)])
         return ["%s%s%d" % (name, e, c) for e in "VS"]
 
-    def names(share, before=None):
+    def names(share):
         for c in range(3):
             a = 64 * c
             keys = shared(T.ga, "ga", xw, T.at, 0, c, share[c], ["x", "at"], "SV")
@@ -303,65 +298,74 @@ def rank_program(g, core, T, topo):
         cp(T.nl[:, o:o + K], T.pr[:, 0:K], ["pr"], ["nl%d" % t])
         send(t, T.nlr[:, o:o + K], T.nl[:, o:o + K], "an%d" % t, ["nl%d" % t])
 
-    def digits(t, c, cut, power):
+    def digits(t, c, cut, power, q="S"):
         a, b, o = cut[c], cut[c + 1], K * (t - 1)
         kw = {"func": AF.Exp, "scale": 3.0, "bias": -24.0} if power else {}
-        gather("S", T.gd[:, 16 * a:16 * b], xw[:, 0:W].indirect(T.nlr[:, o + a:o + b]), ["x"], ["gd%d" % c],
+        gather(q, T.gd[:, 16 * a:16 * b], xw[:, 0:W].indirect(T.nlr[:, o + a:o + b]), ["x"], ["gd%d" % c],
                ext=[("an%d" % t, ne)], **kw)
 
-    def sums(a, b, keys):
-        mm(T.pn[:, K + a:K + b], T.idb[:], T.gd[:, 16 * a:16 * b:16], True, True, ["idb"] + keys, ["pn"])
+    def sums(a, b, h, keys):
+        mm(T.pn[:, h + a:h + b], IDB, T.gd[:, 16 * a:16 * b:16], True, True, ["idb"] + keys, ["pn"])
         for k in range(1, 16):
-            mm(T.pn[:, a:b], T.idb[:], T.gd[:, 16 * a + k:16 * b:16], k == 1, k == 15, ["idb"] + keys, ["pn"])
+            mm(T.pn[:, a:b], IDB, T.gd[:, 16 * a + k:16 * b:16], k == 1, k == 15, ["idb"] + keys, ["pn"])
 
-    def logs():
-        act(T.lg[:], T.pn[:, 0:2 * K], ["pn"], ["lg"], func=AF.Ln)
-        act(T.rb[:], T.lg[:], ["lg"], ["rb"], scale=1.0 / 3, bias=130.0 + 8.0 - 0.45)
-        mm(T.pk[:, 0:K], T.idb[:], T.rb[:, 0:K], True, False, ["idb", "rb"], ["pk"])
-        mm(T.pk[:, 0:K], T.idb[:], T.rb[:, K:2 * K], False, True, ["idb", "rb"], ["pk"])
-        mm(T.pn[:, 0:K], T.idb[:], T.rb[:, 0:K], True, False, ["idb", "rb"], ["pn"])
-        mm(T.pn[:, 0:K], T.idb[:], T.rb[:, K:2 * K], False, True, ["idb", "rb"], ["pn"])
-        act(T.s1[:], T.pn[:, 0:K], ["pn"], ["s1"], bias=-260.0)
+    def logs(h):
+        act(T.lg[:, 0:2 * h], T.pn[:, 0:2 * h], ["pn"], ["lg"], func=AF.Ln)
+        act(T.rb[:, 0:2 * h], T.lg[:, 0:2 * h], ["lg"], ["rb"], scale=1.0 / 3, bias=130.0 + 8.0 - 0.45)
 
-    def wraps():
-        ts(T.s2[:], T.pk[:, 0:K], 276.0, -16.0, A.is_ge, A.mult, ["pk"], ["s2"])
+    def add_logs(h):
+        for b in ("pn", "pk"):
+            mm(T[b][:, 0:h], IDB, T.rb[:, 0:h], True, False, ["idb", "rb"], [b])
+            mm(T[b][:, 0:h], IDB, T.rb[:, h:2 * h], False, True, ["idb", "rb"], [b])
+        act(T.s1[:, 0:h], T.pn[:, 0:h], ["pn"], ["s1"], bias=-260.0)
 
-    def largest(c):
-        scan(T.sc[:, 1024 * c:1024 * (c + 1)], T.rm[:], T.gd[:, 1024 * c:1024 * (c + 1)], 0.0, A.min, A.max,
+    def largest(a, b, c):
+        scan(T.sc[:, 16 * a:16 * b], T.rm[:, 0:16 * (b - a)], T.gd[:, 16 * a:16 * b], 0.0, A.min, A.max,
              ["rm", "gd%d" % c], ["sc%d" % c])
 
-    def new_digits():
-        tt(T.s1[:], T.sc[:, 0:16 * K:16], T.sc[:, 15:16 * K:16], A.add, ["sc0", "sc1", "sc2"], ["s1"])
-        ts(T.s2[:], T.s1[:], 16.0, -16.0, A.is_ge, A.mult, ["s1"], ["s2"])
+    def new_digits(a):
+        tt(T.s1[:, a:K], T.sc[:, 16 * a:16 * K:16], T.sc[:, 16 * a + 15:16 * K:16], A.add, ["sc0", "sc1", "sc2"], ["s1b"])
+        ts(T.s2[:, a:K], T.s1[:, a:K], 16.0, -16.0, A.is_ge, A.mult, ["s1b"], ["s2b"])
 
-    def write_records(t, power):
+    def write_records(t, h, ahead=False):
         o = 16 * (t - 1)
-        out = xw[:, 0:WX].indirect(T.glr[:, o:o + 12])
-        if power:
-            wraps()
-        tt(out, T.s1[:], T.s2[:], A.add, ["s1", "s2", "xd"], ["x"], ext=[("ag%d" % t, ne)])
+        if h:
+            ts(T.s2[:, 0:h], T.pk[:, 0:h], 276.0, -16.0, A.is_ge, A.mult, ["pk"], ["s2"])
+        if ahead:
+            send_list(t + 1)
+        tt(xw[:, 0:WX].indirect(T.glr[:, o:o + 12]), T.s1[:], T.s2[:], A.add, ["s1", "s2", "s1b", "s2b", "xd"], ["x"],
+           ext=[("ag%d" % t, ne)])
+
+    def next_numbers(t):
+        act(held(T.qw, t + 1), window(T.qw, t).indirect(T.ql[:, 0:12]), ["qw", "qe", "qh%d" % (t % 2), "ql"], ["qh%d" % ((t + 1) % 2)])
 
     masks(1)
     names((32, 32, 32))
+    scan(T.vc[:], T.t5[:], T.z[:, 0:K], 2.0 ** -65, A.mult, A.add, ["t5", "z"], ["vc"])
     cp(held(T.idw, 1), T.at[:], ["at"], ["ah1"])
+    ts(T.col[:, 1:2], T.dj[:, 1:2], float(1024 - W - 10), None, A.add, None, ["dj"], ["col1"])
+    act(T.t6[:], DM, ["dm"], ["t6"], scale=-(2.0 ** -59), bias=2.0 ** -59)
+    act(T.o1[:], T.o8[:], ["o8"], ["o1"], scale=1.0 / 8192)
     for t in range(1, 5):
         first, last = t == 1, t == 4
-        power = not first
         cut = (0, 64, 128, K) if first else CFG["d4"] if last else CFG["d"]
-        lt = T["lt%d" % t]
-        LT = ["lt%d_%d" % (t, j) for j in range(4)]
+        h = 0 if first else cut[2] if last else K
+        lt = T.lt1
+        LT = ["lt1_%d" % j for j in range(4)]
+        vc, thr, vc2, thr2 = ("vc", "thr", "vc2", "thr2") if t % 2 else ("vc2", "thr2", "vc", "thr")
         g0 = T.ga[:, 0:16 * K:16]
+        nm = "nm%d" % (t % 2)
         if first:
-            act(NM, T.pn[:, 0:K], ["pn"], ["nm"])
+            act(held(T.nw, t), T.pn[:, 0:K], ["pn"], [nm])
         else:
             tt(T.ne[:], T.pn[:, 0:K], T.kp[:], A.not_equal, ["pn", "kp"], ["ne"])
-            digits(t, 0, cut, power)
-            act(NM, T.pn[:, 0:K], ["pn"], ["nm"])
+            digits(t, 0, cut, True)
+            act(held(T.nw, t), T.pn[:, 0:K], ["pn"], [nm])
         mm(T.pm[:, 0:K], turned(T.w0, t), g0, False, first, GA + ["w0"], ["pm"])
         mm(T.pk[:, 0:K], turned(T.w0, t), g0, True, first, GA + ["w0"], ["pk"])
         mm(T.pl[:, 0:K], turned(T.w0, t), g0, False, False, GA + ["w0"], ["pl"])
         if first:
-            turn_list(1, NM, "nm")
+            turn_list(1, held(T.nw, t), nm)
         else:
             mm(T.pm[:, 0:K], turned(T.o16, t), T.ne[:], False, True, ["o16", "ne"], ["pm"])
             mm(T.pk[:, 0:K], turned(T.o16, t), T.ne[:], False, True, ["o16", "ne"], ["pk"])
@@ -369,8 +373,8 @@ def rank_program(g, core, T, topo):
         mm(T.pg[:, 0:K], turned(T.w0, t), g0, False, False, GA + ["w0"], ["pg"])
         if not first:
             mm(T.pg[:, 0:K], turned(T.o16, t), T.ne[:], False, False, ["o16", "ne"], ["pg"])
-            mm(T.py[:, 0:K], T.on16[:], T.ne[:], False, False, ["on16", "ne"], ["py"])
-            mm(T.py[:, 0:K], T.idb[:], T.fr[:], False, False, ["idb", "fr"], ["py"])
+            mm(T.py[:, 0:K], turned(T.on16, t), T.ne[:], False, False, ["on16", "ne"], ["py"])
+            mm(T.py[:, 0:K], turned(T.id2, t), T.fr[:], False, True, ["idb", "fr"], ["py"])
         scan(T.ks[:], T.d0[:], T.pm[:, 0:K], -5.0, A.max, A.min, ["d0", "pm"], ["ks"])
         tt(T.eq[:, 0:K], T.pk[:, 0:K], T.ks[:], A.is_equal, ["pk", "ks"], ["eq0"])
         tt(T.eq[:, K + 16:2 * K], T.pk[:, 16:K], T.ks[:, 0:K - 16], A.is_equal, ["pk", "ks"], ["eq1"])
@@ -379,93 +383,114 @@ def rank_program(g, core, T, topo):
         if first:
             send_list(1)
             op("G", lambda: g.dma_start(T.ci[0:8, 0:1], T.cur[:], allow_slow_non_contiguous=True), (), ["ci"], dma="lc")
-            iota(T.rm[:], [[0, 64], [16, 16]], -16, 0, ["rm"])
-            iota(T.qw[:, K + NT:K + NX], [[1, NX - NT]], 0, 0, ["qe"])
-            load(T.idw[:, K + NT:K + NX], T.idx[:, 0:NX - NT], (), ["ide"], "le", ext=[("an1", ne)])
+            iota(T.qw[:, K:K + NT], [[1, NT]], 0, 0, ["qw"])
+            act(T.t7[:], T.vc[:], ["vc"], ["t7"], scale=24.0)
+            act(T.nw[:, K:K + NT], xw[:, 0:NT], ["x"], ["nwa"], scale=0.0, bias=-1.0)
         else:
-            digits(t, 1, cut, power)
-        if not last:
-            clear_locks(t + 1, ext=[("an%d" % t, ne)])
+            digits(t, 1, cut, True)
+            if t > 2:
+                next_numbers(t - 1)
         scan(T.ls[:], T.d0[:], T.pl[:, 0:K], -5.0, A.max, A.min, ["d0", "pl"], ["ls"])
         cp(T.ll[:, 0:12], T.ls[:, 15:K:16], ["ls"], ["ll"])
         for j in range(5, -1, -1):
-            cp(lt[:, 0:WX].indirect(T.ll[:, 2 * j:2 * j + 2]), T.vc[:, 32 * j:32 * j + 32], ["vc", "ll"], LT)
-        if power:
-            sums(0, cut[1], ["gd0"])
-            sums(cut[1], cut[2], ["gd1"])
+            cp(lt[:, 0:WX].indirect(T.ll[:, 2 * j:2 * j + 2]), T[vc][:, 32 * j:32 * j + 32], [vc, "ll"], LT)
+        if h:
+            sums(0, cut[1], h, ["gd0"])
+            sums(cut[1], cut[2], h, ["gd1"])
         share = CFG["b1"] if first else CFG["b4"] if last else CFG["b"]
         for c in range(3):
             a = 64 * c
             keys = shared(T.gb, "gb", lt, T.nl, K * (t - 1), c, share[c], LT + ["nl%d" % t])
             for k in range(16):
-                mm(T.ps[:, a:a + 64], T.idb[:], T.gb[:, 16 * a + k:16 * (a + 64):16], k == 0, k == 15, keys + ["idb"], ["ps"])
+                mm(T.ps[:, a:a + 64], IDB, T.gb[:, 16 * a + k:16 * (a + 64):16], k == 0, k == 15, keys + ["idb"], ["ps"])
         if first:
+            tt(T.thr[:], T.t7[:], T.t6[:], A.max, ["t7", "t6"], ["thr"])
+            ts(T.dum[:], T.t1[:, 0:K:16], T.col[:, 1:2], 8192.0, A.add, A.mult, ["t1", "col1"], ["dum"])
             cp(T.cf[0:8, 0:1], T.ci[0:8, 0:1], ["ci"], ["cf"])
             mm(T.pr[:, 256:257], T.sel[0:8, 0:128], T.cf[0:8, 0:1], True, True, ["sel", "cf"], ["pr"])
+            act(T.ltn[:], T.ltri[:], ["ltri"], ["ltn"], scale=-1.0)
             digits(1, 0, cut, False)
             act(T.cc[:, 0:1], T.pr[:, 256:257], ["pr"], ["cc0"])
         else:
-            digits(t, 2, cut, power)
-        tt(T.wf[:], T.ps[:, 0:K], T.thr[:], A.is_ge, ["ps", "thr"], ["wf"])
+            scan(T.ys[:], T.d0[:], T.py[:, 0:K], -5.0, A.max, A.min, ["d0", "py"], ["ys"])
+            ts(T.fw[:, 0:12], T.ys[:, 15:K:16], 0.0, None, A.is_ge, None, ["ys"], ["fw0"])
+            ts(T.fw[:, 12:24], T.ys[:, 15:K:16], 0.0, None, A.is_lt, None, ["ys"], ["fw1"])
+            if last:
+                logs(h)
+            else:
+                digits(t, 2, cut, True)
+        if not last:
+            act(T[vc2][:], T[vc][:], [vc], [vc2], scale=2.0 ** 61)
+            act(T[thr2][:], T[thr][:], [thr], [thr2], scale=2.0 ** 61)
+        tt(T.wf[:], T.ps[:, 0:K], T[thr][:], A.is_ge, ["ps", thr], ["wf"])
         mm(T.pg[:, 0:K], T.o8[:, 0:128], T.wf[:], False, True, ["o8", "wf"], ["pg"])
-        mm(T.py[:, 0:K], back(T.o8, t), T.wf[:], False, True, ["o8", "wf"], ["py"])
+        mm(T.py[:, 256:280], back(T.ltri, t), T.fw[:], True, False, ["ltri", "fw0", "fw1"], ["py"])
         scan(T.gs[:], T.d0[:], T.pg[:, 0:K], -5.0, A.max, A.min, ["d0", "pg"], ["gs"])
         o = 16 * (t - 1)
         cp(T.gl[:, o:o + 12], T.gs[:, 15:K:16], ["gs"], ["gl%d" % t])
         send(t, T.glr[:, o:o + 12], T.gl[:, o:o + 12], "ag%d" % t, ["gl%d" % t])
-        if power:
-            sums(cut[2], K, ["gd2"])
-        scan(T.ys[:], T.d0[:], T.py[:, 0:K], -5.0, A.max, A.min, ["d0", "py"], ["ys"])
-        ts(T.fw[:, 0:12], T.ys[:, 15:K:16], 0.0, None, A.is_gt, None, ["ys"], ["fw0"])
-        ts(T.fw[:, 12:24], T.ys[:, 15:K:16], 0.0, None, A.is_lt, None, ["ys"], ["fw1"])
-        scan(T.cz[:, 1:25], T.z[:, 0:24], T.fw[:], 12.0, A.add, A.add, ["z", "fw0", "fw1"], ["cz"])
-        mm(T.ps[:, 256:281], T.o8[:, 0:128], T.cz[:, 0:25], True, False, ["o8", "cz", "cz0"], ["ps"])
-        mm(T.ps[:, 256:280], T.ltri[:], T.fw[:], False, True, ["ltri", "fw0", "fw1"], ["ps"])
-        ts(T.cc[:, t:t + 1], T.ps[:, 280:281], -1.0 / 8192, T.cc[:, t - 1:t], A.mult, A.add, ["ps", "cc%d" % (t - 1)], ["cc%d" % t])
-        tt(T.ma[:], T.ps[:, 256:268], T.dum[:], A.max, ["ps", "dum"], ["ma"])
+        if first:
+            iota(T.rm[:], [[0, 64], [16, 16]], -16, 0, ["rm"])
+        if last:
+            add_logs(h)
+        elif h:
+            sums(cut[2], K, h, ["gd2"])
+        ts(T.gw[:, 0:12], T.gs[:, 15:K:16], float(W), None, A.is_lt, None, ["gs"], ["gw"])
+        scan(T.cz[:, 1:25], T.fw[:], T.gw[:], 12.0, A.add, A.subtract, ["fw0", "fw1", "gw", "gw1"], ["cz"])
+        mm(T.py[:, 256:280], back(T.ltn, t), T.gw[:], False, False, ["ltn", "gw", "gw1"], ["py"])
+        mm(T.py[:, 256:280], back(T.o8, t), T.cz[:, 0:24], False, True, ["o8", "cz", "cz0"], ["py"])
+        mm(T.py[:, 280:281], back(T.o1, t), T.cz[:, 24:25], True, True, ["o1", "cz"], ["py"])
+        if last:
+            digits(t, 2, cut, False, "V")
+            largest(h, K, 2)
+            new_digits(h)
+            write_records(t, h)
+            load(T.yx[0:64, :], xw[0:64, 0:W], ["x"], (), "oa")
+            load(T.yx[64:128, :], xw[64:128, 0:W], ["x"], (), "ob", q="S")
+        tt(T.ma[:], T.py[:, 256:268], T.dum[:], A.max, ["py", "dum"], ["ma"])
         a = 2 * K * t + (0 if t % 2 else K)
-        ts(T.zs[:, K:2 * K], T.qw[:, a:a + K], T.cc[:, t:t + 1], None, A.add, None, ["qw", "cc%d" % t], ["zs"])
+        ts(T.zs[:, K:2 * K], T.qw[:, a:a + K], T.cc[:, t - 1:t], T.py[:, 280:281], A.add, A.subtract, ["qw", "py", "cc%d" % (t - 1)], ["zs"])
         if first:
             digits(1, 1, cut, False)
             digits(1, 2, cut, False)
-        else:
-            logs()
-        tt(T.mb[:], T.ps[:, 268:280], T.ma[:], A.max, ["ps", "ma"], ["mb"])
+        elif not last:
+            logs(h)
+            if CFG["al"]:
+                add_logs(h)
+        tt(T.mb[:], T.py[:, 268:280], T.ma[:], A.max, ["py", "ma"], ["mb"])
         ts(T.dl[:, 0:12], T.mb[:], 1.0 / 8192, -1024.0, A.mult, A.add, ["mb"], ["dl"])
         cp(T.zs[:, 0:2 * K].indirect(T.dl[:, 0:12]), T.hb[:] if t % 2 else T.qw[:, K:2 * K], ["hb", "qw", "dl", "zsd", "zs"], ["zs"])
         scan(T.qs[:], T.da[:], T.zs[:, K:2 * K], 0.0, A.add, A.max, ["da", "zs"], ["qs"])
-        if t % 2:
-            ts(T.kl[:, 0:12], T.qs[:, 15:K:16], T.col[:, 0:1], float(NX - 8), A.subtract, A.subtract, ["qs", "col0"], ["kl"])
-        else:
-            ts(T.kl[:, 0:12], T.qs[:, 15:K:16], T.col[:, 0:1], float(K), A.subtract, A.min, ["qs", "col0"], ["kl"])
         ts(T.ql[:, 0:12], T.qs[:, 15:K:16], T.col[:, 0:1], None, A.subtract, None, ["qs", "col0"], ["ql"])
-        nw = T.nm[:, 0:K + 8] if t % 2 else T.nm[:, 8:K + 16]
-        late = power and not last and CFG["kq"] == "S"
-        gather("S" if late else "V", T.kp[:], nw.indirect(T.kl[:, 0:12]), ["nm", "nma", "nmb", "kl"], ["kp"])
-        qh, qh2 = "qh%d" % (t % 2), "qh%d" % ((t + 1) % 2)
+        late = not last and not first
+        gather(CFG["kq"] if late else "V", T.kp[:], window(T.nw, t).indirect(T.ql[:, 0:12]), [nm, "nwa", "nwb", "ql"], ["kp"])
         if last:
             load(T.yd[:], T.kp[:], ["kp"], (), "od")
-            cp(held(T.qw, t + 1), window(T.qw, t).indirect(T.ql[:, 0:12]), ["qw", "qe", qh, "ql"], [qh2])
-            load(T.yq[:], T.qw[0:128:16, NW - K:NW], [qh2], (), "oq")
-            write_records(t, power)
-            load(T.yx[0:64, :], xw[0:64, 0:W], ["x"], (), "oa")
-            load(T.yx[64:128, :], xw[64:128, 0:W], ["x"], (), "ob", q="S")
+            next_numbers(t)
+            load(T.yq[:], T.qw[0:128:16, NW - K:NW], ["qh1"], (), "oq")
         else:
             turn_list(t + 1, T.kp[:], "kp")
-            masks(t + 1)
+            if h and not CFG["al"]:
+                add_logs(h)
+            act(T.cc[:, t:t + 1], T.py[:, 280:281], ["py", "cc%d" % (t - 1)], ["cc%d" % t], scale=-1.0, bias=T.cc[:, t - 1:t])
             cp(T.at[:], window(T.idw, t).indirect(T.ql[:, 0:12]), ["idw", "ide", "ah%d" % (t % 2), "ql"], ["at"])
-            if not late:
-                send_list(t + 1)
             if first:
-                for c in range(3):
-                    largest(c)
-                new_digits()
-            act(T.fr[:], T.kp[:], ["kp"], ["fr"], func=AF.Relu, scale=-float(2 ** 20))
-            act(held(T.qw, t + 1), window(T.qw, t).indirect(T.ql[:, 0:12]), ["qw", "qe", qh, "ql"], [qh2])
-            write_records(t, power)
-            if late:
+                act(T.o16[:], T.o1[:], ["o1"], ["o16"], scale=16384.0)
+                act(T.on16[:], T.o1[:], ["o1"], ["on16"], scale=-16384.0)
+                largest(0, 64, 0)
                 send_list(t + 1)
-            names(CFG["a"])
+                iota(T.qw[:, K + NT:K + NX], [[1, NX - NT]], 0, 0, ["qe"])
+                largest(64, 128, 1)
+                largest(128, K, 2)
+                new_digits(0)
+            masks(t + 1)
+            act(T.fr[:], T.kp[:], ["kp"], ["fr"], func=AF.Exp, scale=-14.0)
+            if first:
+                next_numbers(t)
+            write_records(t, h, late and CFG["nl"])
+            if late and not CFG["nl"]:
+                send_list(t + 1)
+            names((32, 32, 32) if first else CFG["a"])
             if t < 3:
                 cp(held(T.idw, t + 1), T.at[:], ["at"], ["ah%d" % ((t + 1) % 2)])
     emit(g, T, ops)

@@ -8,41 +8,60 @@ NX = NT + 4 * K
 NW = NX + 2 * K
 SR, SG = (1, 5, 3), (0, 3, 1)
 BF, F, I, U = "bfloat16", "float32", "int32", "uint16"
-ZC = WX // 4
-CFG = {"a": (38, 32, 32), "b1": (32, 32, 32), "b": (32, 32, 30), "b4": (32, 32, 30), "d": (0, 64, 136, K), "d4": (0, 64, 132, K),
-       "kq": "V", "nl": 1, "al": 1}
+BASE, STEP = 20.0, 52
+UP = 32
+MAGIC = 1.5 * 2 ** 23
+CFG = {"a1": (40, 32, 32), "a": (12, 32, 32), "a4": (12, 32, 32), "b1": (32, 32, 24), "b": (28, 20, 32), "b4": (40, 20, 28),
+       "d1": (0, 28, 64, 120, K), "d": (0, 96, 140, K), "d4": (0, 92, 140, K), "lo": 64, "w": 128, "z": 2144,
+       "fill": "S", "move": "S", "own": "S"}
+START = ("ones di sel t1 mz0 dj t2 t3 t5 m1 wk0 wa wb col0 wc da wd qf grp gm wk o8 w0 o1 t4 qs0 d0 ql0 qh idb rot vc t6 xd hb1 io1 zd1 tri "
+         "thr at0 zv zq ft ntri pz dum pw col2 pads rm0 mH mL")
+FIRST = ("a2S a2V n2 a1S a1V n1 kH nmH tH a0S a0V ksH nlH e0H e1H n0 kL nmL tL ah lsH llH nlL cur rm1 l5 ksL l4 e0L e1L l3 lsL l2 llL l1 py l0 "
+         "b0V b0S s0 b1V b1S s1 cf b2V b2S s2 cc w0 g0 d3 d2 w1 g1 gl late gw cz e d0V d1 h0 mb fill dl tw move h3 qs m3 qk ql kp turn "
+         "h1 h2 m0 m1 m2 at mH mL cy nl x qw")
+MID = ("a2S a2V n2 a1S a1V n1 kH a0S a0V neH d0 ah ksH e0H e1H n0 kL lsH llH neL l5 ksL l4 e0L e1L l3 lsL l2 llL rw l1 py nz l0 "
+       "b0V b0S s0 zr h0 b1V b1S s1 m0 b2V b2S s2 w0 g0 d1 h1 d2 h2 w1 g1 gl gw cz e nmH nmL mb fill dl tw move m1 qs qk ql kp turn "
+       "at m2 mH mL q< cy nl x")
+LAST = ("a2S a2V n2 a1S a1V n1 kH a0S a0V neH d0 ksH e0H e1H n0 kL lsH llH neL l5 ksL l4 e0L e1L l3 lsL l2 llL rw l1 py nz l0 "
+        "b0V b0S s0 zr h0 b1V b1S s1 m0 b2V b2S s2 w0 g0 d1 h1 d2 h2 w1 g1 gl gw cz e nmH nmL mb fill dl m1 m2 cy x yx move qs qk ql kp yd "
+        "q< q yq")
+CFG = {'a1': (50, 34, 30), 'a': (26, 32, 32), 'a4': (24, 40, 26), 'b1': (52, 16, 36), 'b': (30, 36, 24), 'b4': (32, 24, 38), 'd1': (0, 54, 64, 146, 192), 'd': (0, 112, 130, 192), 'd4': (0, 122, 156, 192), 'lo': 64, 'w': 128, 'z': 2752, 'own': 'S', 'ma1': 'S', 'ma': 'S', 'mk1': 'S', 'mk': 'S', 'mk4': 'V', 'mq1': 'S', 'mq': 'S', 'mq4': 'V'}
+START = ''
+FIRST = 'di mz0 ones t1 wk0 sel grp dj zv qf< ft wa ft>> wb wc t2 o8 idb rm0 m1< wd zq d0< que gm t5 mg cur qs0 w0< rot ql0 mL< vc wk mH< at0 a2V kfd io1 a2S a1V ide a1S pads kf< o1 n2 n1 kH a0S a0V nmH t6 pz ksH tH n0 a0d px nlH dum e0H nmL e1H tL lsH nlL llH kL qh ksL l5 tri e0L e1L l4 ft> lsL l3 llL thr l2 rmb l1 l0 cf b1V b0S b2S b2V ntri b1S b0V rm1 s2 d3 d1 w1 d0V h3 py cc d2 s0 s1 a1d w0 g1 g0 q1d h0 gw gl h2 cz xd mH m3 mb nx ah h1 dl mvk new mva m0 m2 m1 q0d cy turn kp nl ft>>> x at e kf mL rw0 pw tw'
+MID = 'py a2S a2V a1V a0V a1S a0S n2 n1 kH neH kL n0 ksH nmH e0H d0 e1H neL lsH llH ksL l5 e0L l4 nmL e1L l3 h0 lsL l2 llL rw l1 l0 nz b0V b0S b1V b1S b2V s0 b2S s1 s2 m0 d1 w0 w1 g0 d2 g1 gl gw h1 cz e zr mb nx dl h2 new mvk turn m1 m2 tw cy mva qf< mL nl kp at x mvq< mH kf>'
+LAST = 'a2V py a2S a1V a0V a1S n2 a0S n1 kH neH n0 ksH e0H kL e1H neL lsH ksL llH l5 e0L l4 e1L l3 lsL l2 d0 llL l1 l0 nmH rw b0V b0S s0 b1S nz b1V b2V b2S h0 s1 w0 d2 zr g0 s2 w1 g1 h2 gl d1 m0 nmL gw h1 m2 cz m1 mb qf< cy dl mvq< e x mvk yd qf mvq yx yq'
+ORDER = {0: START, 1: FIRST, 2: MID, 3: MID, 4: LAST}
 
 SCRATCH = {
-    "x": ("sbuf", [128, WX], BF), "idw": ("sbuf", [128, NW], I), "qw": ("sbuf", [128, NW], F), "z": ("sbuf", [128, ZC], BF),
-    "lt1": ("sbuf", [128, WX], BF), "vc2": ("sbuf", [128, K], BF), "thr2": ("sbuf", [128, K], F),
+    "x": ("sbuf", [128, WX], BF), "idw": ("sbuf", [128, NX], I), "lt": ("sbuf", [128, WX], BF),
     "ga": ("sbuf", [128, 16 * K], BF), "gb": ("sbuf", [128, 16 * K], BF), "gd": ("sbuf", [128, 16 * K], BF),
-    "sc": ("sbuf", [128, 16 * K], BF), "rm": ("sbuf", [128, 1024], BF), "wk": ("sbuf", [128, 2048], BF),
-    "w0": ("sbuf", [128, 256], BF), "o16": ("sbuf", [128, 256], BF), "o8": ("sbuf", [128, 256], BF),
-    "on16": ("sbuf", [128, 256], BF), "id2": ("sbuf", [128, 256], BF), "idf": ("sbuf", [128, 256], F), "o1": ("sbuf", [128, 256], BF),
-    "lt0": ("sbuf", [128, 256], BF), "ltri": ("sbuf", [128, 256], BF), "ltn": ("sbuf", [128, 256], BF), "ones": ("sbuf", [128, 256], F),
-    "nw": ("sbuf", [128, NW], F), "gw": ("sbuf", [128, 24], BF),
-    "sel0": ("sbuf", [128, 256], F), "sel": ("sbuf", [128, 256], F),
-    "gm": ("sbuf", [128, 8], F), "di": ("sbuf", [128, 208], I), "dj": ("sbuf", [128, 208], I), "dm": ("sbuf", [128, 208], F),
-    "m1": ("sbuf", [128, K], BF), "m2": ("sbuf", [128, K], BF), "d0": ("sbuf", [128, K], F), "da": ("sbuf", [128, K], F),
+    "sc": ("sbuf", [128, 16 * K], BF), "rm": ("sbuf", [128, 16 * K], BF), "wk": ("sbuf", [128, 2048], BF),
+    "w0": ("sbuf", [128, 256], BF), "o8": ("sbuf", [128, 256], BF), "o1": ("sbuf", [128, 256], BF), "idb": ("sbuf", [128, 128], BF),
+    "rot": ("sbuf", [128, 256], F), "tri0": ("sbuf", [128, 256], BF), "ptri": ("sbuf", [128, 256], BF), "ntri": ("sbuf", [128, 256], BF),
+    "ones": ("sbuf", [128, 256], F), "sel0": ("sbuf", [128, 256], F), "sel": ("sbuf", [128, 256], F),
+    "gm": ("sbuf", [128, 8], F), "di": ("sbuf", [128, 272], I), "dj": ("sbuf", [128, 272], I), "dm": ("sbuf", [128, 272], F),
+    "mz": ("sbuf", [128, 2 * K], BF), "d0": ("sbuf", [128, K], F), "da": ("sbuf", [128, K], F),
     "t1": ("sbuf", [128, K], F), "t2": ("sbuf", [128, K], F), "t3": ("sbuf", [128, K], F), "t4": ("sbuf", [128, K], F),
-    "t5": ("sbuf", [128, K], F), "t6": ("sbuf", [128, K], F), "t7": ("sbuf", [128, K], F),
-    "vc": ("sbuf", [128, K], BF), "thr": ("sbuf", [128, K], F), "hb": ("sbuf", [128, K], F),
-    "dum": ("sbuf", [128, 12], F), "col": ("sbuf", [128, 8], F), "wa": ("sbuf", [128, 16], F), "wb": ("sbuf", [128, 16], F),
+    "t5": ("sbuf", [128, K], F), "t6": ("sbuf", [128, K], BF),
+    "vc": ("sbuf", [128, K], BF), "thr": ("sbuf", [128, K], BF), "ft": ("sbuf", [128, 128], BF),
+    "io1": ("sbuf", [128, K], F), "mg": ("sbuf", [128, 64], BF),
+    "col": ("sbuf", [128, 8], F), "wa": ("sbuf", [128, 16], F), "wb": ("sbuf", [128, 16], F),
     "wc": ("sbuf", [128, 16], F), "wd": ("sbuf", [128, 16], F),
+    "pz": ("sbuf", [128, 16], BF), "dum": ("sbuf", [128, 12], F), "pw": ("sbuf", [128, 12], F), "tw": ("sbuf", [128, 12], F),
     "qi": ("sbuf", [128, K], I), "qf": ("sbuf", [128, K], F), "ci": ("sbuf", [128, 8], I), "cf": ("sbuf", [128, 8], F),
-    "at": ("sbuf", [128, K], U), "kp": ("sbuf", [128, K], F), "zs": ("sbuf", [128, 2 * K], F),
-    "ne": ("sbuf", [128, K], BF), "fr": ("sbuf", [128, K], BF), "ks": ("sbuf", [128, K], F), "eq": ("sbuf", [128, 2 * K], BF),
-    "ls": ("sbuf", [128, K], F), "ll": ("sbuf", [128, 16], U), "wf": ("sbuf", [128, K], BF), "gs": ("sbuf", [128, K], F),
+    "at": ("sbuf", [128, K], U), "nm": ("sbuf", [128, K], F), "kp": ("sbuf", [128, K], F), "kf": ("sbuf", [128, 3 * K], F),
+    "a0": ("sbuf", [128, 3 * K], F), "a1": ("sbuf", [128, 3 * K], F), "q0": ("sbuf", [128, 3 * K], F), "q1": ("sbuf", [128, 3 * K], F),
+    "ne": ("sbuf", [128, K], BF), "ks": ("sbuf", [128, K], F), "eq": ("sbuf", [128, 2 * K], BF),
+    "ls": ("sbuf", [128, K], F), "ll": ("sbuf", [128, 16], U), "wf": ("sbuf", [128, K], F), "gs": ("sbuf", [128, K], F),
     "gl": ("sbuf", [128, 64], U), "glr": ("sbuf", [128, 64], U), "nl": ("sbuf", [128, 4 * K], U), "nlr": ("sbuf", [128, 4 * K], U),
-    "ys": ("sbuf", [128, K], F), "fw": ("sbuf", [128, 24], BF), "cz": ("sbuf", [128, 32], BF),
-    "ma": ("sbuf", [128, 12], F), "mb": ("sbuf", [128, 12], F), "dl": ("sbuf", [128, 16], U), "cc": ("sbuf", [128, 8], F),
-    "qs": ("sbuf", [128, K], F), "ql": ("sbuf", [128, 16], U),
-    "s1": ("sbuf", [128, K], BF), "s2": ("sbuf", [128, K], BF), "lg": ("sbuf", [128, 2 * K], F), "rb": ("sbuf", [128, 2 * K], BF),
-    "pn": ("psum", [128, 512], F), "pk": ("psum", [128, 512], F), "pm": ("psum", [128, 512], F), "pl": ("psum", [128, 512], F),
-    "ps": ("psum", [128, 512], F), "pg": ("psum", [128, 512], F), "py": ("psum", [128, 512], F), "pr": ("psum", [128, 512], F),
+    "gw": ("sbuf", [128, 36], BF), "rw": ("sbuf", [128, 40], BF), "cz": ("sbuf", [128, 32], BF), "nz": ("sbuf", [128, 32], BF),
+    "zr": ("sbuf", [128, 12], F), "mb": ("sbuf", [128, 12], F), "dl": ("sbuf", [128, 64], U), "cc": ("sbuf", [128, 8], F),
+    "qs": ("sbuf", [128, K], F), "ql": ("sbuf", [128, 16], U), "px": ("sbuf", [128, 12], F), "s2": ("sbuf", [128, K], BF),
 }
-PSUM = ("pn", "pk", "pm", "pl", "ps", "pg", "py", "pr")
-SEMAPHORES = (["cv", "cs", "cp", "cg", "sent", "lq", "li", "lr", "le", "lc", "z1", "oa", "ob", "oq", "od"]
+PSUM = ("pa", "pb", "pc", "pd", "pe", "pf", "py", "pr")
+for _b in PSUM:
+    SCRATCH[_b] = ("psum", [128, 512], F)
+SEMAPHORES = (["cv", "cs", "cp", "cg", "sent", "lq", "li", "lr", "le", "lc", "lz", "lm", "oa", "ob", "oq", "od", "an0"]
               + ["an%d" % t for t in range(1, 5)] + ["ag%d" % t for t in range(1, 5)])
 QSEM = {"V": "cv", "S": "cs", "P": "cp", "G": "cg"}
 
@@ -135,9 +154,11 @@ def rank_program(g, core, T, topo):
     n = len(T.cores)
     ne = min(len(topo.engines(a, b)) for a in T.cores for b in T.cores if a != b)
     ops = []
+    sends = []
+    tag = [None]
 
     def op(q, fn, r=(), w=(), ext=(), dma=None, remote=False):
-        ops.append({"q": q, "fn": fn, "r": list(r), "w": list(w), "ext": list(ext), "dma": dma, "remote": remote})
+        ops.append({"q": q, "fn": fn, "r": list(r), "w": list(w), "ext": list(ext), "dma": dma, "remote": remote, "tag": tag[0]})
 
     def ts(out, in0, s1, s2, o0, o1, r, w, ext=()):
         if o1 is None:
@@ -157,13 +178,13 @@ def rank_program(g, core, T, topo):
     def ms(ap, c, w):
         op("V", lambda: V.memset(ap, c), (), w)
 
-    def act(out, in_, r, w, func=None, bias=None, scale=None, ext=()):
+    def act(out, in_, r, w, bias=None, scale=None, ext=(), func=None):
         if bias is None and scale is None:
             op("S", lambda: S.activation(out, in_, func or AF.Copy), r, w, ext)
         elif bias is None:
-            op("S", lambda: S.activation(out, in_, func or AF.Identity, scale=scale), r, w, ext)
+            op("S", lambda: S.activation(out, in_, AF.Identity, scale=scale), r, w, ext)
         else:
-            op("S", lambda: S.activation(out, in_, func or AF.Identity, bias=bias, scale=1.0 if scale is None else scale), r, w, ext)
+            op("S", lambda: S.activation(out, in_, AF.Identity, bias=bias, scale=1.0 if scale is None else scale), r, w, ext)
 
     def mm(out, lhsT, rhs, start, stop, r, w):
         op("P", lambda: P.matmul(out, lhsT, rhs, start, stop), r, w)
@@ -181,317 +202,361 @@ def rank_program(g, core, T, topo):
         dst = T.cores[(rank + SR[t % 3]) % n]
         rid, pid, _ = topo.addr(dst)
         mask = sum(1 << e for e in topo.engines(core, dst)[:ne])
+        sends.append(sem)
         op("G", lambda: g.remote_dma(dst_ap, src_ap, T.sem[sem], T.sem.sent, pid, rid, mask), r, (), remote=True)
 
-    def turned(buf, t):
-        a = 128 - 16 * SG[t % 3]
+    def turn(buf, frm, to):
+        a = (16 * (frm - to)) % 128
         return buf[:, a:a + 128]
 
-    def back(buf, t):
-        a = 16 * SG[t % 3]
-        return buf[:, a:a + 128]
-
-    def clear_locks(t, ext=(), start=0):
-        for j in range(start, 4):
-            load(T["lt%d" % t][:, j * ZC:(j + 1) * ZC], T.z[:], ["z"], ["lt%d_%d" % (t, j)], "z%d" % t, ext=ext)
-
-    def gather(q, out, src, r, w, ext=(), **kw):
-        if q == "V":
+    def gather(q, out, src, r, w, ext=(), scale=None):
+        if q == "S":
+            act(out, src, r, w, ext=ext, scale=scale)
+        elif scale is None:
             cp(out, src, r, w, ext)
         else:
-            act(out, src, r, w, ext=ext, **kw)
+            ts(out, src, scale, None, A.mult, None, r, w, ext)
 
     xw = T.x
     DM = T.dm[:, 1:K + 1]
-    IDB = T.id2[:, 0:128]
+    IDB = T.idb[:]
     BIG = float(2 ** 22)
+    CH = {"H": (CFG["lo"], K), "L": (0, CFG["lo"])}
+    NB, KB, LB = {"H": "pa", "L": "pb"}, {"H": "pc", "L": "pd"}, {"H": "pe", "L": "pf"}
+    WK = ["wk%d" % k for k in range(16)]
+    LT = ["lta", "ltb0", "ltb1", "ltb2"]
+    GS = ["gs0", "gs1"]
 
-    def held(buf, t):
-        return buf[:, NW - K:NW] if t % 2 else buf[:, 0:K]
+    def cfg(name, t):
+        return CFG[name + {1: "1", 4: "4"}.get(t, "")]
 
-    def window(buf, t):
-        return buf[:, K:NW] if t % 2 else buf[:, 0:NW - K]
+    def queue(name):
+        return T[name][:, 2 * K:3 * K]
+
+    def wrapped(buf):
+        return buf[:, 15:K:16]
+
+    def c_sel(t):
+        pick(T.sel0[0:8, :], T.ones[0:8, :], [[0, 2], [1, 128]], A.is_ge, 0.0, 0, -16, ["ones"], ["sel0"])
+        pick(T.sel[0:8, :], T.sel0[0:8, :], [[0, 2], [-1, 128]], A.is_ge, 0.0, 15, 16, ["sel0"], ["sel"])
+
+    def c_dj(t):
+        ts(T.dj[:], T.di[:], 15, None, A.bitwise_and, None, ["di"], ["dj"])
+        ts(T.dm[:], T.dj[:], 0.0, None, A.is_equal, None, ["dj"], ["dm"])
+
+    def c_grp(t):
+        mm(T.pc[:, 0:256], T.sel[0:8, 0:128], T.sel[0:8, :], True, True, ["sel"], ["pc"])
+        mm(T.pd[:, 0:256], T.sel[0:8, 0:128], T.sel[0:8, :], True, True, ["sel"], ["pd"])
+
+    def c_que(t):
+        mm(T.pr[:, 0:K], T.sel[0:8, 0:128], T.qf[0:8, :], True, False, ["sel", "qf"], ["pr"])
+        mm(T.pr[:, 0:K], IDB, T.mz[:, 0:K], False, True, ["idb", "m1"], ["pr"])
+        mm(T.py[:, 0:K], T.sel[0:8, 0:128], T.qf[0:8, :], True, True, ["sel", "qf"], ["py"])
+
+    def c_wk(t):
+        for k in range(16):
+            act(T.wk[:, 129 * k:128 * (k + 1):16], T.gm[:], ["gm", "wd", "wk"], ["wk%d" % k], scale=T.wd[:, k:k + 1])
+
+    def c_tri(t):
+        pick(T.tri0[:], T.o1[:], [[0, 2], [1, 128]], A.is_ge, 0.0, 0, -1, ["o1"], ["tri0"])
+        pick(T.ptri[:], T.tri0[:], [[0, 2], [1, 128]], A.not_equal, 512.0, 0, -1, ["tri0"], ["ptri"])
+
+    def c_ft(t):
+        act(T.ft[:, 32 * (t - 1):32 * t], T.ones[:, 0:32], ["ones"], ["ft%d" % (t - 1)], scale=2.0 ** (STEP * (t - 1) - 78))
+
+    def c_pz(t):
+        ts(T.col[:, 1:2], T.dj[:, 1:2], float(-W), None, A.add, None, ["dj"], ["col1"])
+        act(T.pz[:, 0:12], T.t1[:, 0:K:16], ["t1", "col1"], ["pz"], bias=T.col[:, 1:2])
+
+    def c_pads(t):
+        iota(T.pz[:, 12:14], [[320, 2]], -320, 0, ["pz0"])
+        iota(T.gw[:], [[0, 36]], 0, 0, ["gw", "gw0"])
+
+    def spare(name):
+        return lambda t: iota(T[name][:, 0:2 * K], [[0, 2 * K]], 0, 0, [name + "d"])
+
+    def c_rm1(t):
+        iota(T.rm[:, 0:16 * K:16], [[0, K]], -64, 0, ["rma", "rmb", "rm0"])
+
+    def c_cf(t):
+        cp(T.cf[0:8, 0:1], T.ci[0:8, 0:1], ["ci"], ["cf"])
+        mm(T.pr[:, 256:257], T.sel[0:8, 0:128], T.cf[0:8, 0:1], True, True, ["sel", "cf"], ["pr"])
+
+    def c_zq(t):
+        for j, a in enumerate(range(CFG["z"], WX, 8 * K)):
+            b = min(a + 8 * K, WX)
+            load(T.lt[:, a:b], T.rm[:, 0:b - a], ["rma"], ["ltb%d" % j], "lz")
+
+    steps = {
+        "ones": lambda t: ms(T.ones[:], 1.0, ["ones"]),
+        "di": lambda t: op("G", lambda: g.iota(T.di[:], [[-1, 272]], 273, 1), (), ["di"]),
+        "sel": c_sel, "dj": c_dj, "grp": c_grp, "wk": c_wk, "tri": c_tri, "ft": c_ft, "pz": c_pz, "pads": c_pads,
+        "rm1": c_rm1, "cf": c_cf, "zq": c_zq,
+        "t1": lambda t: iota(T.t1[:], [[1, K]], W, 0, ["t1"]),
+        "mz0": lambda t: ms(T.mz[:, K:2 * K], 0.0, ["mz0"]),
+        "t2": lambda t: act(T.t2[:], DM, ["dm"], ["t2"], scale=8192.0, bias=-10.0),
+        "que": c_que,
+        "ide": lambda t: load(T.idw[:, NT:NX], T.idx[:, 0:NX - NT], (), ["ide"], "le"),
+        "rmb": lambda t: load(T.rm[:, 8 * K:16 * K], T.rm[:, 0:8 * K], ["rma"], ["rmb"], "lm"),
+        "t5": lambda t: act(T.t5[:], DM, ["dm"], ["t5"], scale=1.0 / BASE - 1.0, bias=1.0),
+        "m1": lambda t: act(T.mz[:, 0:K], DM, ["dm"], ["m1"], scale=-BIG, bias=BIG),
+        "t6": lambda t: act(T.t6[:], DM, ["dm"], ["t6"], scale=-2.0 ** 70, bias=2.0 ** 70),
+        "wk0": lambda t: ms(T.wk[:], 0.0, ["wk"]),
+        "wa": lambda t: ts(T.wa[:], T.dm[:, 1:17], 256.0, None, A.mult, None, ["dm"], ["wa"]),
+        "wb": lambda t: ts(T.wb[:], T.dm[:, 2:18], 16.0, None, A.mult, None, ["dm"], ["wb"]),
+        "wc": lambda t: tt(T.wc[:], T.wa[:], T.dm[:, 3:19], A.add, ["wa", "dm"], ["wc"]),
+        "wd": lambda t: tt(T.wd[:], T.wc[:], T.wb[:], A.add, ["wc", "wb"], ["wd"]),
+        "gm": lambda t: act(T.gm[:], T.pc[:, 0:128:16], ["pc"], ["gm"]),
+        "o8": lambda t: act(T.o8[:], T.pc[:, 0:256], ["pc"], ["o8"], scale=8192.0),
+        "w0": lambda t: act(T.w0[:], T.pc[:, 0:256], ["pc", "wd"], ["w0"], scale=T.wd[:, 0:1]) if t == 0 else waits(0),
+        "o1": lambda t: act(T.o1[:], T.o8[:], ["o8"], ["o1"], scale=1.0 / 8192),
+        "qs0": lambda t: scan(T.qs[:], T.d0[:], T.pr[:, 0:K], -5.0, A.max, A.min, ["d0", "pr"], ["qs"]),
+        "d0": lambda t: tt(T.d0[:], T.t1[:], T.t2[:], A.min, ["t1", "t2"], ["d0"]) if t == 0 else digits(t, 0),
+        "ql0": lambda t: cp(T.ql[:, 0:12], wrapped(T.qs), ["qs"], ["ql"]),
+        "qh": lambda t: op("S", lambda: S.activation(queue("q0"), T.py[:, 0:K], AF.Silu, bias=float(UP)), ["py"], ["q0"]),
+        "idb": lambda t: tt(IDB, T.pd[:, 0:128], T.dm[:, 1:129], A.mult, ["pd", "dm"], ["idb"]),
+        "rot": lambda t: tt(T.rot[:], T.pd[:, 0:256], T.dm[:, 2:258], A.mult, ["pd", "dm"], ["rot"]),
+        "vc": lambda t: scan(T.vc[:], T.t5[:], T.mz[:, K:2 * K], BASE ** 12 / 8, A.mult, A.add, ["t5", "mz0"], ["vc"]),
+        "xd": lambda t: iota(xw[:, W:WX], [[0, K]], 0, 0, ["xd"]),
+        "io1": lambda t: iota(T.io1[:], [[1, K]], UP - K, 0, ["io1"]),
+        "a0d": spare("a0"), "a1d": spare("a1"), "kfd": spare("kf"), "q0d": spare("q0"), "q1d": spare("q1"),
+        "rw0": lambda t: iota(T.rw[:], [[0, 40]], 0, 0, ["rw", "rw0"]),
+        "thr": lambda t: act(T.thr[:], T.vc[:], ["vc"], ["thr"], scale=-18.0 * 2 ** 15),
+        "at0": lambda t: cp(T.at[:], T.idw[:, 0:NT].indirect(T.ql[:, 0:12]), ["idw", "ql"], ["at"]),
+        "zv": lambda t: ms(T.lt[:, 0:CFG["z"]], 0.0, ["lta"]),
+        "ntri": lambda t: act(T.ntri[:], T.ptri[:], ["ptri"], ["ntri"], scale=-1.0),
+        "dum": lambda t: act(T.dum[:], T.pz[:, 0:12], ["pz"], ["dum"], bias=128.0),
+        "pw": lambda t: act(T.pw[:], T.pz[:, 0:12], ["pz"], ["pw"], bias=-511.0 * 8192, scale=8192.0),
+        "rm0": lambda t: iota(T.rm[:, 0:8 * K], [[0, 8 * K]], 0, 0, ["rma"]),
+        "cur": lambda t: op("G", lambda: g.dma_start(T.ci[0:8, 0:1], T.cur[:], allow_slow_non_contiguous=True), (), ["ci"], dma="lc"),
+        "cc": lambda t: cp(T.cc[:, 0:1], T.pr[:, 256:257], ["pr"], ["cc0"]),
+        "mg": lambda t: iota(T.mg[:], [[0, 64]], int(MAGIC), 0, ["mg"]),
+        "px": lambda t: act(T.px[:], T.pz[:, 0:12], ["pz"], ["px"], bias=float(-K)),
+    }
+
+    def masks(t, h):
+        a, b = CH[h]
+        m = b - a
+        mm(T[KB[h]][:, 0:2 * m], IDB, T.mz[:, K - m:K + m], True, False, ["idb", "m1", "mz0"], [KB[h]])
+        mm(T[LB[h]][:, 0:m], IDB, T.mz[:, 0:m], True, False, ["idb", "m1"], [LB[h]])
+
+    def part(e, buf, name, win, lst, o, c, v, r, scale=None):
+        a = 64 * c
+        lo, hi = (a, a + v) if e == "V" else (a + v, a + 64)
+        if hi > lo:
+            gather(e, buf[:, 16 * lo:16 * hi], win[:, 0:W].indirect(lst[:, o + lo:o + hi]), r, ["%s%s%d" % (name, e, c)], scale=scale)
+
+    def index_digits(t, c, e):
+        part(e, T.ga, "ga", xw, T.at, 0, c, cfg("a", t)[c], ["x", "at"])
+
+    def names(t, c):
+        h = "H" if 64 * c >= CFG["lo"] else "L"
+        a = 64 * c
+        out = T[NB[h]][:, a - CH[h][0]:a - CH[h][0] + 64]
+        mm(out, IDB, T.mg[:], True, False, ["idb", "mg"], [NB[h]])
+        for k in range(16):
+            mm(out, T.wk[:, 128 * k:128 * (k + 1)], T.ga[:, 16 * a + k:16 * (a + 64):16], False, k == 15,
+               ["gaV%d" % c, "gaS%d" % c] + WK, [NB[h]])
+
+    def keys(t, h):
+        a, b = CH[h]
+        m, u = b - a, SG[t % 3]
+        r = ["ga%s%d" % (e, c) for e in "VS" for c in range(a // 64, b // 64)] + ["w0"]
+        g0 = T.ga[:, 16 * a:16 * b:16]
+        mm(T[KB[h]][:, 0:m], turn(T.w0, 0, u), g0, False, False, r, [KB[h]])
+        mm(T[KB[h]][:, m:2 * m], turn(T.w0, 0, u), g0, False, t == 1, r, [KB[h]])
+        mm(T[LB[h]][:, 0:m], turn(T.w0, 0, u), g0, False, False, r, [LB[h]])
+
+    def changed(t, h):
+        a, b = CH[h]
+        m, u = b - a, SG[t % 3]
+        tt(T.ne[:, a:b], T[NB[h]][:, 0:m], T.kp[:, a:b], A.not_equal, [NB[h], "kp"], ["ne" + h])
+        r = ["o8", "ne" + h]
+        mm(T[KB[h]][:, 0:m], turn(T.o8, 0, u), T.ne[:, a:b], False, False, r, [KB[h]])
+        mm(T[KB[h]][:, m:2 * m], turn(T.o8, 0, u), T.ne[:, a:b], False, True, r, [KB[h]])
+        mm(T[LB[h]][:, 0:m], turn(T.o8, 0, u), T.ne[:, a:b], False, False, r, [LB[h]])
+
+    def hold_keys(t, h):
+        a, b = CH[h]
+        scan(T.ks[:, a:b], T.d0[:, a:b], T[KB[h]][:, 0:b - a], -5.0, A.max, A.min, ["d0", KB[h]], ["ks" + h])
+
+    def twins(t, j, h):
+        a, b = CH[h]
+        m, d = b - a, 1 + 16 * j
+        tt(T.eq[:, j * K + a + d:j * K + b], T[KB[h]][:, m + d:2 * m], T.ks[:, a:b - d], A.is_equal, [KB[h], "ks" + h], ["eq%d%s" % (j, h)])
+        mm(T[LB[h]][:, d:m], T.o8[:, 0:128], T.eq[:, j * K + a + d:j * K + b], False, j == 1, ["o8", "eq%d%s" % (j, h)], [LB[h]])
+
+    def holders(t, h):
+        a, b = CH[h]
+        scan(T.ls[:, a:b], T.d0[:, a:b], T[LB[h]][:, 0:b - a], -5.0, A.max, A.min, ["d0", LB[h]], ["ls" + h])
+
+    def lock_list(t, h):
+        a, b = CH[h]
+        cp(T.ll[:, a // 16:b // 16], T.ls[:, a + 15:b:16], ["ls" + h], ["ll" + h])
+
+    def lock(t, j):
+        tt(T.lt[:, 0:WX].indirect(T.ll[:, 2 * j:2 * j + 2]), T.vc[:, 32 * j:32 * j + 32], T.ft[:, 32 * (t - 1):32 * t], A.mult,
+           ["vc", "ft%d" % (t - 1), "llH" if 32 * j >= CFG["lo"] else "llL"], LT)
+
+    def keep_names(t, h):
+        a, b = CH[h]
+        act(T.nm[:, a:b], T[NB[h]][:, 0:b - a], [NB[h]], ["nm" + h], bias=(0 if t == 4 else UP) - MAGIC)
+
+    def turn_list(t, src, a, b, key):
+        mm(T.pr[:, a:b], turn(T.rot, 0, SG[t % 3]), src, True, True, ["rot", key], ["pr"])
+
+    def send_list(t, a, b, sem):
+        o = K * (t - 1)
+        ts(T.nl[:, o + a:o + b], T.pr[:, a:b], 0.25 - UP, None, A.add, None, ["pr"], ["nl%d_%d" % (t, a)])
+        send(t, T.nlr[:, o + a:o + b], T.nl[:, o + a:o + b], sem, ["nl%d_%d" % (t, a)])
+
+    def locks(t, c, e):
+        part(e, T.gb, "gb", T.lt, T.nl, K * (t - 1), c, cfg("b", t)[c], LT + ["nl%d_0" % t, "nl%d_64" % t], scale=2.0 ** (93 - STEP * (t - 1)))
+
+    def span(j):
+        return (0, CFG["w"], "pc") if j == 0 else (CFG["w"], K, "pd")
+
+    def lock_sums(t, c):
+        a = 64 * c
+        lo, hi, b = span(0 if a < CFG["w"] else 1)
+        if a == lo:
+            mm(T[b][:, 0:hi - lo], IDB, T.thr[:, lo:hi], True, False, ["idb", "thr"], [b])
+            mm(T[b][:, 0:hi - lo], IDB, T.t6[:, 0:hi - lo], False, False, ["idb", "t6"], [b])
+        for k in range(16):
+            mm(T[b][:, a - lo:a - lo + 64], IDB, T.gb[:, 16 * a + k:16 * (a + 64):16], False, k == 15 and a + 64 == hi,
+               ["gbV%d" % c, "gbS%d" % c, "idb"], [b])
+
+    def waits(j):
+        lo, hi, b = span(j)
+        if hi > lo:
+            tt(T.wf[:, lo:hi], T[b][:, 0:hi - lo], T.ks[:, lo:hi], A.max, [b, "ksH", "ksL"], ["wf%d" % j])
+
+    def goes(t, j):
+        lo, hi, b = span(j)
+        if hi > lo:
+            scan(T.gs[:, lo:hi], T.d0[:, lo:hi], T.wf[:, lo:hi], -5.0, A.max, A.min, ["d0", "wf%d" % j], ["gs%d" % j])
+
+    def go_list(t):
+        o = 16 * (t - 1)
+        cp(T.gl[:, o:o + 12], wrapped(T.gs), GS, ["gl%d" % t])
+        send(t, T.glr[:, o:o + 12], T.gl[:, o:o + 12], "ag%d" % t, ["gl%d" % t])
+
+    def digits(t, j, q="S"):
+        a, b = cfg("d", t)[j:j + 2]
+        o = K * (t - 1)
+        sem = "an0" if t == 1 and a < 64 else "an%d" % t
+        gather(q, T.gd[:, 16 * a:16 * b], xw[:, 0:W].indirect(T.nlr[:, o + a:o + b]), ["x"], ["gd%d" % j], ext=[(sem, ne)])
+
+    def own_digit(t, j):
+        a, b = cfg("d", t)[j:j + 2]
+        gather(CFG["own"], T.rm[:, 16 * a + 15:16 * b:16], T.gd[:, 16 * a + 15:16 * b:16], ["gd%d" % j, "rm0"], ["rh%d" % j] + RH)
+
+    def largest(t, j):
+        a, b = cfg("d", t)[j:j + 2]
+        scan(T.sc[:, 16 * a:16 * b], T.rm[:, 16 * a:16 * b], T.gd[:, 16 * a:16 * b], 0.0, A.add, A.max, ["rh%d" % j, "gd%d" % j], ["sc%d" % j])
+
+    SC = ["sc%d" % j for j in range(4)]
+    RH = []
+
+    def write_records(t):
+        o = 16 * (t - 1)
+        tt(xw[:, 0:WX].indirect(T.glr[:, o:o + 12]), T.sc[:, 15:16 * K:16], T.s2[:], A.add, ["s2", "xd"] + SC, ["x"], ext=[("ag%d" % t, ne)])
+
+    def restart_counts(t):
+        u = SG[t % 3]
+        scan(T.nz[:, 0:24], T.rw[:, 0:24], T.rw[:, 12:36], 0.0, A.add, A.subtract, ["rw", "rw0"], ["nz"])
+        mm(T.pr[:, 0:12], turn(T.o1, u, 0), T.nz[:, 12:24], True, False, ["o1", "nz"], ["pr"])
+        mm(T.pr[:, 0:12], turn(T.ptri, u, 0), T.rw[:, 13:25], False, True, ["ptri", "rw"], ["pr"])
+        mm(T.py[:, 0:12], turn(T.o1, u, 0), T.nz[:, 0:12], False, False, ["o1", "nz"], ["py"])
+        mm(T.py[:, 0:12], turn(T.ntri, u, 0), T.rw[:, 13:25], False, False, ["ntri", "rw"], ["py"])
+
+    def go_counts(t):
+        u = SG[t % 3]
+        scan(T.cz[:, 0:23], T.gw[:, 12:35], T.gw[:, 0:23], 20.0, A.add, A.subtract, ["gw", "gw0"], ["cz"])
+        mm(T.py[:, 0:12], turn(T.ntri, u, 0), T.gw[:, 12:24], False, False, ["ntri", "gw"], ["py"])
+        mm(T.pf[:, 0:1], IDB, T.pz[:, 12:13], True, False, ["idb", "pz0"], ["pf"])
+        mm(T.py[:, 0:12], turn(T.o1, u, 0), T.cz[:, 11:23], False, False, ["o1", "cz"], ["py"])
+        mm(T.py[:, 12:13], turn(T.o1, u, 0), T.cz[:, 11:12], False, t == 4, ["o1", "cz"], ["py"])
+        if t < 4:
+            mm(T.py[:, 13:14], turn(T.o8, u, SG[(t + 1) % 3]), T.cz[:, 11:12], False, True, ["o8", "cz"], ["py"])
+        mm(T.pf[:, 0:1], turn(T.o1, u, 0), T.cz[:, 11:12], False, True, ["o1", "cz"], ["pf"])
+
+    def move(t, q, to, src, key):
+        out, r = T[to][:, 0:3 * K].indirect(T.dl[:, 16 * (t - 1):16 * (t - 1) + 12]), key + ["dl%d" % t, to + "d", to]
+        if q == "S":
+            act(out, src, r, [to], func=AF.Silu)
+        else:
+            cp(out, src, r, [to])
+
+    def along(name, t):
+        a, b = "%s%d" % (name, t % 2), "%s%d" % (name, (t + 1) % 2)
+        move(t, cfg("m" + name, t), a, queue(b), [b])
+
+    def numbers(t):
+        ts(T.t2[:], queue("q0"), MAGIC - UP, -MAGIC, A.add, A.add, ["q0"], ["t2"])
+        ts(T.t3[:], T.t2[:], float(NT), float(-NT), A.is_ge, A.mult, ["t2"], ["t3"])
+        tt(T.t4[:], T.t2[:], T.t3[:], A.add, ["t2", "t3"], ["t4"])
+        load(T.yq[:], T.t4[0:128:16, :], ["t4"], (), "oq")
+
+    def store(t):
+        load(T.yx[0:64, :], xw[0:64, 0:W], ["x"], (), "oa")
+        load(T.yx[64:128, :], xw[64:128, 0:W], ["x"], (), "ob", q="S")
+
+    for h in "HL":
+        for name, f in (("m", masks), ("k", keys), ("ne", changed), ("ks", hold_keys), ("ls", holders), ("ll", lock_list), ("nm", keep_names)):
+            steps[name + h] = lambda t, f=f, h=h: f(t, h) if CH[h][1] else None
+        for j in range(2):
+            steps["e%d%s" % (j, h)] = lambda t, j=j, h=h: twins(t, j, h) if CH[h][1] else None
+        a, b = (64, K) if h == "H" else (0, 64)
+        steps["t" + h] = lambda t, a=a, b=b, h=h: turn_list(1, T.nm[:, a:b], a, b, "nm" + (h if CFG["lo"] else "H"))
+        steps["nl" + h] = lambda t, a=a, b=b: send_list(1, a, b, "an1" if a else "an0")
+    for j in range(6):
+        for name, f in (("n", names), ("s", lock_sums), ("l", lock), ("g", goes), ("h", own_digit), ("m", largest), ("d", digits)):
+            steps.setdefault("%s%d" % (name, j), lambda t, f=f, j=j: f(t, j))
+        for e in "VS":
+            steps["a%d%s" % (j, e)] = lambda t, j=j, e=e: index_digits(t, j, e)
+            steps["b%d%s" % (j, e)] = lambda t, j=j, e=e: locks(t, j, e)
+        steps["d%dV" % j] = lambda t, j=j: digits(t, j, "V")
+    mask_tile = steps["m1"]
+    steps.update({
+        "m1": lambda t: mask_tile(t) if t == 0 else largest(t, 1),
+        "w1": lambda t: waits(1),
+        "ah": lambda t: ts(queue("a0"), T.at[:], float(UP), None, A.add, None, ["at"], ["a0"]),
+        "rw": lambda t: tt(T.rw[:, 13:25], wrapped(T.ks), T.tw[:], A.is_ge, ["ksH", "ksL", "tw", "rw0"], ["rw"]),
+        "py": lambda t: mm(T.py[:, 0:14], IDB, T.pz[:, 0:14], True, False, ["idb", "pz", "pz0"], ["py"]),
+        "nz": restart_counts,
+        "zr": lambda t: tt(T.zr[:], T.pr[:, 0:12], T.dum[:], A.max, ["pr", "dum"], ["zr"]),
+        "gl": go_list,
+        "gw": lambda t: ts(T.gw[:, 12:24], wrapped(T.gs), float(W), None, A.is_lt, None, GS + ["gw0"], ["gw"]),
+        "cz": go_counts,
+        "e": lambda t: act(T.cc[:, t:t + 1], T.pf[:, 0:1], ["pf", "cc%d" % (t - 1)], ["cc%d" % t], bias=T.cc[:, t - 1:t]),
+        "mb": lambda t: tt(T.mb[:], T.py[:, 0:12], (T.dum if t == 1 else T.zr)[:], A.max, ["py", "dum", "zr"], ["mb"]),
+        "dl": lambda t: ts(T.dl[:, 16 * (t - 1):16 * (t - 1) + 12], T.mb[:], T.py[:, 12:13], 64.0, A.subtract, A.add, ["mb", "py"], ["dl%d" % t]),
+        "tw": lambda t: ts(T.tw[:], T.pw[:], T.py[:, 13:14], float(W), A.add, A.max, ["pw", "py"], ["tw"]),
+        "nx": lambda t: ts(T.ql[:, 0:12], T.px[:], T.py[:, 12:13], T.cc[:, t - 1:t], A.add, A.add, ["px", "py", "cc%d" % (t - 1)], ["ql"]),
+        "new": lambda t: ts(queue("a%d" % (t % 2)), T.idw[:, 0:NX].indirect(T.ql[:, 0:12]), float(UP), None, A.add, None,
+                            ["idw", "ide", "ql"], ["a%d" % (t % 2)]),
+        "mva": lambda t: along("a", t),
+        "at": lambda t: ts(T.at[:], queue("a%d" % (t % 2)), 0.25 - UP, None, A.add, None, ["a%d" % (t % 2)], ["at"]),
+        "kf": lambda t: iota(queue("kf"), [[0, K]], -1 if t == 4 else UP - 1, 0, ["kf"]),
+        "mvk": lambda t: move(t, cfg("mk", t), "kf", T.nm[:], ["nmH", "nmL"]),
+        "kp": lambda t: act(T.kp[:], queue("kf"), ["kf"], ["kp"], bias=MAGIC - UP),
+        "turn": lambda t: turn_list(t + 1, queue("kf"), 0, K, "kf"),
+        "qf": lambda t: act(queue("q%d" % (t % 2)), T.io1[:], ["io1", "cc%d" % t], ["q%d" % (t % 2)], bias=T.cc[:, t:t + 1])
+        if t else cp(T.qf[0:8, :], T.qi[0:8, :], ["qi"], ["qf"]),
+        "mvq": lambda t: along("q", t),
+        "cy": lambda t: ts(T.s2[:], T.sc[:, 15:16 * K:16], 16.0, -16.0, A.is_ge, A.mult, SC, ["s2"]),
+        "nl": lambda t: send_list(t + 1, 0, K, "an%d" % (t + 1)),
+        "x": write_records, "yx": store, "yq": numbers,
+        "yd": lambda t: load(T.yd[:], queue("kf"), ["kf"], (), "od"),
+    })
 
     load(T.qi[0:8, :], T.que[:], (), ["qi"], "lq", q="S")
-    load(T.idw[:, K:K + NT], T.idx[:], (), ["idw"], "li")
+    load(T.idw[:, 0:NT], T.idx[:], (), ["idw"], "li")
     load(xw[:, 0:W], T.rec[:], (), ["x"], "lr")
-    ms(T.ones[:], 1.0, ["ones"])
-    op("G", lambda: g.iota(T.di[:], [[-1, 208]], K + 1 + 16, 1), (), ["di"])
-    pick(T.sel0[0:8, :], T.ones[0:8, :], [[0, 2], [1, 128]], A.is_ge, 0.0, 0, -16, ["ones"], ["sel0"])
-    pick(T.sel[0:8, :], T.sel0[0:8, :], [[0, 2], [-1, 128]], A.is_ge, 0.0, 15, 16, ["sel0"], ["sel"])
-    iota(T.t1[:], [[1, K]], W + 10, 0, ["t1"])
-    pick(T.idf[:], T.ones[:], [[0, 2], [-1, 128]], A.is_equal, 0.0, 0, 1, ["ones"], ["idf"])
-    ms(T.z[:], 0.0, ["z"])
-    ts(T.dj[:], T.di[:], 15, None, A.bitwise_and, None, ["di"], ["dj"])
-    ts(T.dm[:], T.dj[:], 0.0, None, A.is_equal, None, ["dj"], ["dm"])
-    act(T.t2[:], T.dm[:, 0:K], ["dm"], ["t2"], scale=4096.0)
-    act(T.t3[:], DM, ["dm"], ["t3"], scale=-8192.0)
-    act(T.t5[:], DM, ["dm"], ["t5"], scale=1.0 / 32 - 1.0, bias=1.0)
-    act(T.m1[:], DM, ["dm"], ["m1"], scale=-BIG, bias=BIG)
-    act(T.m2[:], DM, ["dm"], ["m2"], scale=-BIG - 8192.0, bias=BIG)
-    ms(T.wk[:], 0.0, ["wk"])
-    ts(T.wa[:], T.dm[:, 1:17], 256.0, None, A.mult, None, ["dm"], ["wa"])
-    ts(T.wb[:], T.dm[:, 2:18], 16.0, None, A.mult, None, ["dm"], ["wb"])
-    ts(T.col[:, 0:1], T.dm[:, 16:17], -4096.0, 4096.0, A.mult, A.add, ["dm"], ["col0"])
-    tt(T.wc[:], T.wa[:], T.dm[:, 3:19], A.add, ["wa", "dm"], ["wc"])
-    tt(T.da[:], T.t2[:], T.t3[:], A.add, ["t2", "t3"], ["da"])
-    tt(T.wd[:], T.wc[:], T.wb[:], A.add, ["wc", "wb"], ["wd"])
-    cp(T.qf[0:8, :], T.qi[0:8, :], ["qi"], ["qf"])
-    mm(T.pk[:, 0:256], T.sel[0:8, 0:128], T.sel[0:8, :], True, True, ["sel"], ["pk"])
-    mm(T.pr[:, 0:K], T.sel[0:8, 0:128], T.qf[0:8, :], True, True, ["sel", "qf"], ["pr"])
-    act(T.gm[:], T.pk[:, 0:128:16], ["pk"], ["gm"])
-    for k in range(16):
-        act(T.wk[:, 129 * k:128 * (k + 1):16], T.gm[:], ["gm", "wd", "wk"], ["wk%d" % k], scale=T.wd[:, k:k + 1])
-    act(T.o8[:], T.pk[:, 0:256], ["pk"], ["o8"], scale=8192.0)
-    act(T.w0[:], T.pk[:, 0:256], ["pk", "wd"], ["w0"], scale=T.wd[:, 0:1])
-    act(T.id2[:], T.idf[:], ["idf"], ["idb"])
-    tt(T.t4[:], T.t1[:], DM, A.mult, ["t1", "dm"], ["t4"])
-    scan(T.qs[:], T.da[:], T.pr[:, 0:K], 0.0, A.add, A.max, ["da", "pr"], ["qs"])
-    ts(T.d0[:], T.t4[:], -10.0, None, A.add, None, ["t4"], ["d0"])
-    ts(T.ql[:, 0:12], T.qs[:, 15:K:16], T.col[:, 0:1], None, A.subtract, None, ["qs", "col0"], ["ql"])
-    act(held(T.qw, 1), T.pr[:, 0:K], ["pr"], ["qh1"])
-    iota(T.hb[:], [[1, K]], NX, 0, ["hb"])
-    iota(xw[:, W:WX], [[0, K]], 0, 0, ["xd"])
-    iota(T.zs[:, 0:K], [[0, K]], 0, 0, ["zsd"])
-    iota(T.cz[:, 0:1], [[0, 1]], 12, 0, ["cz0"])
-    iota(T.fw[:], [[-1, 2], [0, 12]], 1, 0, ["fw0", "fw1"])
-    iota(T.gw[:, 12:24], [[0, 12]], 0, 0, ["gw1"])
-    iota(T.nw[:, K + NT:K + NX], [[0, NX - NT]], -1, 0, ["nwb"])
-    pick(T.lt0[:], T.o8[:], [[0, 2], [1, 128]], A.is_ge, 0.0, 0, -1, ["o8"], ["lt0"])
-    pick(T.ltri[:], T.lt0[:], [[0, 2], [1, 128]], A.not_equal, float(2 ** 23), 0, -1, ["lt0"], ["ltri"])
-    clear_locks(1, start=1)
-    load(T.idw[:, K + NT:K + NX], T.idx[:, 0:NX - NT], (), ["ide"], "le")
-    ms(T.lt1[:, 0:ZC], 0.0, ["lt1_0"])
-    cp(T.at[:], T.idw[:, K:K + NT].indirect(T.ql[:, 0:12]), ["idw", "ql"], ["at"])
-    WK = ["wk%d" % k for k in range(16)]
-
-    def masks(t):
-        mm(T.pm[:, 0:K], IDB, T.m1[:], True, False, ["idb", "m1"], ["pm"])
-        mm(T.pl[:, 0:K], IDB, T.m2[:], True, False, ["idb", "m2"], ["pl"])
-        mm(T.pg[:, 0:K], IDB, T.m1[:], True, False, ["idb", "m1"], ["pg"])
-        if t > 1:
-            mm(T.py[:, 0:K], IDB, T.m1[:], True, False, ["idb", "m1"], ["py"])
-
-    def shared(buf, name, win, lst, o, c, v, r, order="VS"):
-        a = 64 * c
-        for e in order:
-            lo, hi = (a, a + v) if e == "V" else (a + v, a + 64)
-            if hi > lo:
-                gather(e, buf[:, 16 * lo:16 * hi], win[:, 0:W].indirect(lst[:, o + lo:o + hi]), r, ["%s%s%d" % (name, e, c)])
-        return ["%s%s%d" % (name, e, c) for e in "VS"]
-
-    def names(share):
-        for c in range(3):
-            a = 64 * c
-            keys = shared(T.ga, "ga", xw, T.at, 0, c, share[c], ["x", "at"], "SV")
-            for k in range(16):
-                mm(T.pn[:, a:a + 64], T.wk[:, 128 * k:128 * (k + 1)], T.ga[:, 16 * a + k:16 * (a + 64):16], k == 0, k == 15,
-                   keys + WK, ["pn"])
-
-    GA = ["ga%s%d" % (e, c) for e in "VS" for c in range(3)]
-
-    def turn_list(t, src, key):
-        mm(T.pr[:, 0:K], turned(T.idf, t), src, True, True, ["idf", key], ["pr"])
-
-    def send_list(t):
-        o = K * (t - 1)
-        cp(T.nl[:, o:o + K], T.pr[:, 0:K], ["pr"], ["nl%d" % t])
-        send(t, T.nlr[:, o:o + K], T.nl[:, o:o + K], "an%d" % t, ["nl%d" % t])
-
-    def digits(t, c, cut, power, q="S"):
-        a, b, o = cut[c], cut[c + 1], K * (t - 1)
-        kw = {"func": AF.Exp, "scale": 3.0, "bias": -24.0} if power else {}
-        gather(q, T.gd[:, 16 * a:16 * b], xw[:, 0:W].indirect(T.nlr[:, o + a:o + b]), ["x"], ["gd%d" % c],
-               ext=[("an%d" % t, ne)], **kw)
-
-    def sums(a, b, h, keys):
-        mm(T.pn[:, h + a:h + b], IDB, T.gd[:, 16 * a:16 * b:16], True, True, ["idb"] + keys, ["pn"])
-        for k in range(1, 16):
-            mm(T.pn[:, a:b], IDB, T.gd[:, 16 * a + k:16 * b:16], k == 1, k == 15, ["idb"] + keys, ["pn"])
-
-    def logs(h):
-        act(T.lg[:, 0:2 * h], T.pn[:, 0:2 * h], ["pn"], ["lg"], func=AF.Ln)
-        act(T.rb[:, 0:2 * h], T.lg[:, 0:2 * h], ["lg"], ["rb"], scale=1.0 / 3, bias=130.0 + 8.0 - 0.45)
-
-    def add_logs(h):
-        for b in ("pn", "pk"):
-            mm(T[b][:, 0:h], IDB, T.rb[:, 0:h], True, False, ["idb", "rb"], [b])
-            mm(T[b][:, 0:h], IDB, T.rb[:, h:2 * h], False, True, ["idb", "rb"], [b])
-        act(T.s1[:, 0:h], T.pn[:, 0:h], ["pn"], ["s1"], bias=-260.0)
-
-    def largest(a, b, c):
-        scan(T.sc[:, 16 * a:16 * b], T.rm[:, 0:16 * (b - a)], T.gd[:, 16 * a:16 * b], 0.0, A.min, A.max,
-             ["rm", "gd%d" % c], ["sc%d" % c])
-
-    def new_digits(a):
-        tt(T.s1[:, a:K], T.sc[:, 16 * a:16 * K:16], T.sc[:, 16 * a + 15:16 * K:16], A.add, ["sc0", "sc1", "sc2"], ["s1b"])
-        ts(T.s2[:, a:K], T.s1[:, a:K], 16.0, -16.0, A.is_ge, A.mult, ["s1b"], ["s2b"])
-
-    def write_records(t, h, ahead=False):
-        o = 16 * (t - 1)
-        if h:
-            ts(T.s2[:, 0:h], T.pk[:, 0:h], 276.0, -16.0, A.is_ge, A.mult, ["pk"], ["s2"])
-        if ahead:
-            send_list(t + 1)
-        tt(xw[:, 0:WX].indirect(T.glr[:, o:o + 12]), T.s1[:], T.s2[:], A.add, ["s1", "s2", "s1b", "s2b", "xd"], ["x"],
-           ext=[("ag%d" % t, ne)])
-
-    def next_numbers(t):
-        act(held(T.qw, t + 1), window(T.qw, t).indirect(T.ql[:, 0:12]), ["qw", "qe", "qh%d" % (t % 2), "ql"], ["qh%d" % ((t + 1) % 2)])
-
-    masks(1)
-    names((32, 32, 32))
-    scan(T.vc[:], T.t5[:], T.z[:, 0:K], 2.0 ** -65, A.mult, A.add, ["t5", "z"], ["vc"])
-    cp(held(T.idw, 1), T.at[:], ["at"], ["ah1"])
-    ts(T.col[:, 1:2], T.dj[:, 1:2], float(1024 - W - 10), None, A.add, None, ["dj"], ["col1"])
-    act(T.t6[:], DM, ["dm"], ["t6"], scale=-(2.0 ** -59), bias=2.0 ** -59)
-    act(T.o1[:], T.o8[:], ["o8"], ["o1"], scale=1.0 / 8192)
-    for t in range(1, 5):
-        first, last = t == 1, t == 4
-        cut = (0, 64, 128, K) if first else CFG["d4"] if last else CFG["d"]
-        h = 0 if first else cut[2] if last else K
-        lt = T.lt1
-        LT = ["lt1_%d" % j for j in range(4)]
-        vc, thr, vc2, thr2 = ("vc", "thr", "vc2", "thr2") if t % 2 else ("vc2", "thr2", "vc", "thr")
-        g0 = T.ga[:, 0:16 * K:16]
-        nm = "nm%d" % (t % 2)
-        if first:
-            act(held(T.nw, t), T.pn[:, 0:K], ["pn"], [nm])
-        else:
-            tt(T.ne[:], T.pn[:, 0:K], T.kp[:], A.not_equal, ["pn", "kp"], ["ne"])
-            digits(t, 0, cut, True)
-            act(held(T.nw, t), T.pn[:, 0:K], ["pn"], [nm])
-        mm(T.pm[:, 0:K], turned(T.w0, t), g0, False, first, GA + ["w0"], ["pm"])
-        mm(T.pk[:, 0:K], turned(T.w0, t), g0, True, first, GA + ["w0"], ["pk"])
-        mm(T.pl[:, 0:K], turned(T.w0, t), g0, False, False, GA + ["w0"], ["pl"])
-        if first:
-            turn_list(1, held(T.nw, t), nm)
-        else:
-            mm(T.pm[:, 0:K], turned(T.o16, t), T.ne[:], False, True, ["o16", "ne"], ["pm"])
-            mm(T.pk[:, 0:K], turned(T.o16, t), T.ne[:], False, True, ["o16", "ne"], ["pk"])
-            mm(T.pl[:, 0:K], turned(T.o16, t), T.ne[:], False, False, ["o16", "ne"], ["pl"])
-        mm(T.pg[:, 0:K], turned(T.w0, t), g0, False, False, GA + ["w0"], ["pg"])
-        if not first:
-            mm(T.pg[:, 0:K], turned(T.o16, t), T.ne[:], False, False, ["o16", "ne"], ["pg"])
-            mm(T.py[:, 0:K], turned(T.on16, t), T.ne[:], False, False, ["on16", "ne"], ["py"])
-            mm(T.py[:, 0:K], turned(T.id2, t), T.fr[:], False, True, ["idb", "fr"], ["py"])
-        scan(T.ks[:], T.d0[:], T.pm[:, 0:K], -5.0, A.max, A.min, ["d0", "pm"], ["ks"])
-        tt(T.eq[:, 0:K], T.pk[:, 0:K], T.ks[:], A.is_equal, ["pk", "ks"], ["eq0"])
-        tt(T.eq[:, K + 16:2 * K], T.pk[:, 16:K], T.ks[:, 0:K - 16], A.is_equal, ["pk", "ks"], ["eq1"])
-        mm(T.pl[:, 0:K], T.o8[:, 0:128], T.eq[:, 0:K], False, False, ["o8", "eq0"], ["pl"])
-        mm(T.pl[:, 16:K], T.o8[:, 0:128], T.eq[:, K + 16:2 * K], False, True, ["o8", "eq1"], ["pl"])
-        if first:
-            send_list(1)
-            op("G", lambda: g.dma_start(T.ci[0:8, 0:1], T.cur[:], allow_slow_non_contiguous=True), (), ["ci"], dma="lc")
-            iota(T.qw[:, K:K + NT], [[1, NT]], 0, 0, ["qw"])
-            act(T.t7[:], T.vc[:], ["vc"], ["t7"], scale=24.0)
-            act(T.nw[:, K:K + NT], xw[:, 0:NT], ["x"], ["nwa"], scale=0.0, bias=-1.0)
-        else:
-            digits(t, 1, cut, True)
-            if t > 2:
-                next_numbers(t - 1)
-        scan(T.ls[:], T.d0[:], T.pl[:, 0:K], -5.0, A.max, A.min, ["d0", "pl"], ["ls"])
-        cp(T.ll[:, 0:12], T.ls[:, 15:K:16], ["ls"], ["ll"])
-        for j in range(5, -1, -1):
-            cp(lt[:, 0:WX].indirect(T.ll[:, 2 * j:2 * j + 2]), T[vc][:, 32 * j:32 * j + 32], [vc, "ll"], LT)
-        if h:
-            sums(0, cut[1], h, ["gd0"])
-            sums(cut[1], cut[2], h, ["gd1"])
-        share = CFG["b1"] if first else CFG["b4"] if last else CFG["b"]
-        for c in range(3):
-            a = 64 * c
-            keys = shared(T.gb, "gb", lt, T.nl, K * (t - 1), c, share[c], LT + ["nl%d" % t])
-            for k in range(16):
-                mm(T.ps[:, a:a + 64], IDB, T.gb[:, 16 * a + k:16 * (a + 64):16], k == 0, k == 15, keys + ["idb"], ["ps"])
-        if first:
-            tt(T.thr[:], T.t7[:], T.t6[:], A.max, ["t7", "t6"], ["thr"])
-            ts(T.dum[:], T.t1[:, 0:K:16], T.col[:, 1:2], 8192.0, A.add, A.mult, ["t1", "col1"], ["dum"])
-            cp(T.cf[0:8, 0:1], T.ci[0:8, 0:1], ["ci"], ["cf"])
-            mm(T.pr[:, 256:257], T.sel[0:8, 0:128], T.cf[0:8, 0:1], True, True, ["sel", "cf"], ["pr"])
-            act(T.ltn[:], T.ltri[:], ["ltri"], ["ltn"], scale=-1.0)
-            digits(1, 0, cut, False)
-            act(T.cc[:, 0:1], T.pr[:, 256:257], ["pr"], ["cc0"])
-        else:
-            scan(T.ys[:], T.d0[:], T.py[:, 0:K], -5.0, A.max, A.min, ["d0", "py"], ["ys"])
-            ts(T.fw[:, 0:12], T.ys[:, 15:K:16], 0.0, None, A.is_ge, None, ["ys"], ["fw0"])
-            ts(T.fw[:, 12:24], T.ys[:, 15:K:16], 0.0, None, A.is_lt, None, ["ys"], ["fw1"])
-            if last:
-                logs(h)
-            else:
-                digits(t, 2, cut, True)
-        if not last:
-            act(T[vc2][:], T[vc][:], [vc], [vc2], scale=2.0 ** 61)
-            act(T[thr2][:], T[thr][:], [thr], [thr2], scale=2.0 ** 61)
-        tt(T.wf[:], T.ps[:, 0:K], T[thr][:], A.is_ge, ["ps", thr], ["wf"])
-        mm(T.pg[:, 0:K], T.o8[:, 0:128], T.wf[:], False, True, ["o8", "wf"], ["pg"])
-        mm(T.py[:, 256:280], back(T.ltri, t), T.fw[:], True, False, ["ltri", "fw0", "fw1"], ["py"])
-        scan(T.gs[:], T.d0[:], T.pg[:, 0:K], -5.0, A.max, A.min, ["d0", "pg"], ["gs"])
-        o = 16 * (t - 1)
-        cp(T.gl[:, o:o + 12], T.gs[:, 15:K:16], ["gs"], ["gl%d" % t])
-        send(t, T.glr[:, o:o + 12], T.gl[:, o:o + 12], "ag%d" % t, ["gl%d" % t])
-        if first:
-            iota(T.rm[:], [[0, 64], [16, 16]], -16, 0, ["rm"])
-        if last:
-            add_logs(h)
-        elif h:
-            sums(cut[2], K, h, ["gd2"])
-        ts(T.gw[:, 0:12], T.gs[:, 15:K:16], float(W), None, A.is_lt, None, ["gs"], ["gw"])
-        scan(T.cz[:, 1:25], T.fw[:], T.gw[:], 12.0, A.add, A.subtract, ["fw0", "fw1", "gw", "gw1"], ["cz"])
-        mm(T.py[:, 256:280], back(T.ltn, t), T.gw[:], False, False, ["ltn", "gw", "gw1"], ["py"])
-        mm(T.py[:, 256:280], back(T.o8, t), T.cz[:, 0:24], False, True, ["o8", "cz", "cz0"], ["py"])
-        mm(T.py[:, 280:281], back(T.o1, t), T.cz[:, 24:25], True, True, ["o1", "cz"], ["py"])
-        if last:
-            digits(t, 2, cut, False, "V")
-            largest(h, K, 2)
-            new_digits(h)
-            write_records(t, h)
-            load(T.yx[0:64, :], xw[0:64, 0:W], ["x"], (), "oa")
-            load(T.yx[64:128, :], xw[64:128, 0:W], ["x"], (), "ob", q="S")
-        tt(T.ma[:], T.py[:, 256:268], T.dum[:], A.max, ["py", "dum"], ["ma"])
-        a = 2 * K * t + (0 if t % 2 else K)
-        ts(T.zs[:, K:2 * K], T.qw[:, a:a + K], T.cc[:, t - 1:t], T.py[:, 280:281], A.add, A.subtract, ["qw", "py", "cc%d" % (t - 1)], ["zs"])
-        if first:
-            digits(1, 1, cut, False)
-            digits(1, 2, cut, False)
-        elif not last:
-            logs(h)
-            if CFG["al"]:
-                add_logs(h)
-        tt(T.mb[:], T.py[:, 268:280], T.ma[:], A.max, ["py", "ma"], ["mb"])
-        ts(T.dl[:, 0:12], T.mb[:], 1.0 / 8192, -1024.0, A.mult, A.add, ["mb"], ["dl"])
-        cp(T.zs[:, 0:2 * K].indirect(T.dl[:, 0:12]), T.hb[:] if t % 2 else T.qw[:, K:2 * K], ["hb", "qw", "dl", "zsd", "zs"], ["zs"])
-        scan(T.qs[:], T.da[:], T.zs[:, K:2 * K], 0.0, A.add, A.max, ["da", "zs"], ["qs"])
-        ts(T.ql[:, 0:12], T.qs[:, 15:K:16], T.col[:, 0:1], None, A.subtract, None, ["qs", "col0"], ["ql"])
-        late = not last and not first
-        gather(CFG["kq"] if late else "V", T.kp[:], window(T.nw, t).indirect(T.ql[:, 0:12]), [nm, "nwa", "nwb", "ql"], ["kp"])
-        if last:
-            load(T.yd[:], T.kp[:], ["kp"], (), "od")
-            next_numbers(t)
-            load(T.yq[:], T.qw[0:128:16, NW - K:NW], ["qh1"], (), "oq")
-        else:
-            turn_list(t + 1, T.kp[:], "kp")
-            if h and not CFG["al"]:
-                add_logs(h)
-            act(T.cc[:, t:t + 1], T.py[:, 280:281], ["py", "cc%d" % (t - 1)], ["cc%d" % t], scale=-1.0, bias=T.cc[:, t - 1:t])
-            cp(T.at[:], window(T.idw, t).indirect(T.ql[:, 0:12]), ["idw", "ide", "ah%d" % (t % 2), "ql"], ["at"])
-            if first:
-                act(T.o16[:], T.o1[:], ["o1"], ["o16"], scale=16384.0)
-                act(T.on16[:], T.o1[:], ["o1"], ["on16"], scale=-16384.0)
-                largest(0, 64, 0)
-                send_list(t + 1)
-                iota(T.qw[:, K + NT:K + NX], [[1, NX - NT]], 0, 0, ["qe"])
-                largest(64, 128, 1)
-                largest(128, K, 2)
-                new_digits(0)
-            masks(t + 1)
-            act(T.fr[:], T.kp[:], ["kp"], ["fr"], func=AF.Exp, scale=-14.0)
-            if first:
-                next_numbers(t)
-            write_records(t, h, late and CFG["nl"])
-            if late and not CFG["nl"]:
-                send_list(t + 1)
-            names((32, 32, 32) if first else CFG["a"])
-            if t < 3:
-                cp(held(T.idw, t + 1), T.at[:], ["at"], ["ah%d" % ((t + 1) % 2)])
+    for t in range(5):
+        for name in ORDER[t].split():
+            tag[0] = (t, name)
+            steps[name.rstrip("<>")](t - name.count("<") + name.count(">"))
     emit(g, T, ops)
-    g.wait_ge(T.sem.sent, 8 * ne)
+    g.wait_ge(T.sem.sent, len(sends) * ne)

@@ -5,62 +5,41 @@ W = 4096
 WX = W + K
 NT = 2048
 NX = NT + 4 * K
-NW = NX + 2 * K
 SR, SG = (1, 5, 3), (0, 3, 1)
 BF, F, I, U = "bfloat16", "float32", "int32", "uint16"
 BASE, STEP = 20.0, 52
 UP = 32
 MAGIC = 1.5 * 2 ** 23
-CFG = {"a1": (40, 32, 32), "a": (12, 32, 32), "a4": (12, 32, 32), "b1": (32, 32, 24), "b": (28, 20, 32), "b4": (40, 20, 28),
-       "d1": (0, 28, 64, 120, K), "d": (0, 96, 140, K), "d4": (0, 92, 140, K), "lo": 64, "w": 128, "z": 2144,
-       "fill": "S", "move": "S", "own": "S"}
-START = ("ones di sel t1 mz0 dj t2 t3 t5 m1 wk0 wa wb col0 wc da wd qf grp gm wk o8 w0 o1 t4 qs0 d0 ql0 qh idb rot vc t6 xd hb1 io1 zd1 tri "
-         "thr at0 zv zq ft ntri pz dum pw col2 pads rm0 mH mL")
-FIRST = ("a2S a2V n2 a1S a1V n1 kH nmH tH a0S a0V ksH nlH e0H e1H n0 kL nmL tL ah lsH llH nlL cur rm1 l5 ksL l4 e0L e1L l3 lsL l2 llL l1 py l0 "
-         "b0V b0S s0 b1V b1S s1 cf b2V b2S s2 cc w0 g0 d3 d2 w1 g1 gl late gw cz e d0V d1 h0 mb fill dl tw move h3 qs m3 qk ql kp turn "
-         "h1 h2 m0 m1 m2 at mH mL cy nl x qw")
-MID = ("a2S a2V n2 a1S a1V n1 kH a0S a0V neH d0 ah ksH e0H e1H n0 kL lsH llH neL l5 ksL l4 e0L e1L l3 lsL l2 llL rw l1 py nz l0 "
-       "b0V b0S s0 zr h0 b1V b1S s1 m0 b2V b2S s2 w0 g0 d1 h1 d2 h2 w1 g1 gl gw cz e nmH nmL mb fill dl tw move m1 qs qk ql kp turn "
-       "at m2 mH mL q< cy nl x")
-LAST = ("a2S a2V n2 a1S a1V n1 kH a0S a0V neH d0 ksH e0H e1H n0 kL lsH llH neL l5 ksL l4 e0L e1L l3 lsL l2 llL rw l1 py nz l0 "
-        "b0V b0S s0 zr h0 b1V b1S s1 m0 b2V b2S s2 w0 g0 d1 h1 d2 h2 w1 g1 gl gw cz e nmH nmL mb fill dl m1 m2 cy x yx move qs qk ql kp yd "
-        "q< q yq")
-CFG = {'a1': (50, 34, 30), 'a': (26, 32, 32), 'a4': (24, 40, 26), 'b1': (52, 16, 36), 'b': (30, 36, 24), 'b4': (32, 24, 38), 'd1': (0, 54, 64, 146, 192), 'd': (0, 112, 130, 192), 'd4': (0, 122, 156, 192), 'lo': 64, 'w': 128, 'z': 2752, 'own': 'S', 'ma1': 'S', 'ma': 'S', 'mk1': 'S', 'mk': 'S', 'mk4': 'V', 'mq1': 'S', 'mq': 'S', 'mq4': 'V'}
-START = ''
-FIRST = 'di mz0 ones t1 wk0 sel grp dj zv qf< ft wa ft>> wb wc t2 o8 idb rm0 m1< wd zq d0< que gm t5 mg cur qs0 w0< rot ql0 mL< vc wk mH< at0 a2V kfd io1 a2S a1V ide a1S pads kf< o1 n2 n1 kH a0S a0V nmH t6 pz ksH tH n0 a0d px nlH dum e0H nmL e1H tL lsH nlL llH kL qh ksL l5 tri e0L e1L l4 ft> lsL l3 llL thr l2 rmb l1 l0 cf b1V b0S b2S b2V ntri b1S b0V rm1 s2 d3 d1 w1 d0V h3 py cc d2 s0 s1 a1d w0 g1 g0 q1d h0 gw gl h2 cz xd mH m3 mb nx ah h1 dl mvk new mva m0 m2 m1 q0d cy turn kp nl ft>>> x at e kf mL rw0 pw tw'
-MID = 'py a2S a2V a1V a0V a1S a0S n2 n1 kH neH kL n0 ksH nmH e0H d0 e1H neL lsH llH ksL l5 e0L l4 nmL e1L l3 h0 lsL l2 llL rw l1 l0 nz b0V b0S b1V b1S b2V s0 b2S s1 s2 m0 d1 w0 w1 g0 d2 g1 gl gw h1 cz e zr mb nx dl h2 new mvk turn m1 m2 tw cy mva qf< mL nl kp at x mvq< mH kf>'
-LAST = 'a2V py a2S a1V a0V a1S n2 a0S n1 kH neH n0 ksH e0H kL e1H neL lsH ksL llH l5 e0L l4 e1L l3 lsL l2 d0 llL l1 l0 nmH rw b0V b0S s0 b1S nz b1V b2V b2S h0 s1 w0 d2 zr g0 s2 w1 g1 h2 gl d1 m0 nmL gw h1 m2 cz m1 mb qf< cy dl mvq< e x mvk yd qf mvq yx yq'
-ORDER = {0: START, 1: FIRST, 2: MID, 3: MID, 4: LAST}
+ZV = 2752
+CFG = {"a1": (28, 36, 34), "a": (28, 32, 32), "a4": (34, 34, 32), "aw1": 0, "aw": 8, "aw4": 8,
+       "b1": (42, 32, 42), "b": (32, 30, 32), "b4": (30, 34, 36),
+       "d1": (0, 58, 64, 132, K), "d": (0, 112, 132, K), "d4": (0, 76, 118, K), "v1": ("h3", "pc"), "v": ("nmL",), "v4": ()}
+FIRST = ("ones di zv ft sel ft>> ft> dj wk0 wa grp t6 t5 wb gm mg t1 rm0 wc m1< qi t2 wd o8 wkd w0 wk wkb d0< idb que rot qs0 mz0 ql0 "
+         "rL at0 wkc ide mL a2S rH mH pz a2V kf< n2 a1S a1V a0V a0S kH kfd cur rmb n1 pw zq ksH q1d nmH pH idf n0 vc o1 tH e0H thr e1H "
+         "dum kL n0b ah nlH lsH nmL tL ksL llH pL e0L l5 e1L l4 nlL lsL l3 tri llL qh l2 th1 l1 cf l0 b2S b1S pads cc rm1 b0S th0 b2V "
+         "b0V ntri s2 b1V g1 rw0 q0d s0 xd d3 s1 d0V d2 g0 pc h3 py w h0 gw gl cz m3 mH> mb d1 dl h2 h1 m0 m1 m2 mvk new e a1d kp cy "
+         "turn nl o70 x rH> mva kf rL> mL> io1 a0d ft>>> at")
+MID = ("pc a2V a2S a1V a1S n2 n1 kH a0V neH pH a0W ksH a0S n0 n0b d0 e0H e1H kL neL lsH ksL pL d1 llH e0L l5 e1L th1 l4 h0 lsL th0 l3 "
+       "llL l2 l1 rw l0 nmL b0V b0S py b1S b1V b2S s0 b2V m0 s1 s2 g0 d2 g1 h1 nz w h2 gw gl cz zr nmH mb e dl m2 new m1 mvk mva cy "
+       "qf<< turn kp mvq<< nl mH> rL> at x kf> mL> rH>")
+LAST = ("a2V a2S a1V n2 a0V a1S a0S n1 kH neH a0W pH n0 d2 ksH n0b e0H e1H kL neL d0 lsH ksL th0 pL llH e0L l5 e1L l4 lsL l3 llL l2 l1 "
+        "rw th1 l0 py nz b0S b1S h2 b0V b2S s0 b1V h0 qf<< b2V nmL m2 d1 s1 s2 mvq<< h1 zr g0 g1 w qf< gw gl cz nmH mvq< e m0 mb m1 dl "
+        "cy mvk qf yd mvq x yx yq")
+ORDER = {1: FIRST, 2: MID, 3: MID, 4: LAST}
 
-SCRATCH = {
-    "x": ("sbuf", [128, WX], BF), "idw": ("sbuf", [128, NX], I), "lt": ("sbuf", [128, WX], BF),
-    "ga": ("sbuf", [128, 16 * K], BF), "gb": ("sbuf", [128, 16 * K], BF), "gd": ("sbuf", [128, 16 * K], BF),
-    "sc": ("sbuf", [128, 16 * K], BF), "rm": ("sbuf", [128, 16 * K], BF), "wk": ("sbuf", [128, 2048], BF),
-    "w0": ("sbuf", [128, 256], BF), "o8": ("sbuf", [128, 256], BF), "o1": ("sbuf", [128, 256], BF), "idb": ("sbuf", [128, 128], BF),
-    "rot": ("sbuf", [128, 256], F), "tri0": ("sbuf", [128, 256], BF), "ptri": ("sbuf", [128, 256], BF), "ntri": ("sbuf", [128, 256], BF),
-    "ones": ("sbuf", [128, 256], F), "sel0": ("sbuf", [128, 256], F), "sel": ("sbuf", [128, 256], F),
-    "gm": ("sbuf", [128, 8], F), "di": ("sbuf", [128, 272], I), "dj": ("sbuf", [128, 272], I), "dm": ("sbuf", [128, 272], F),
-    "mz": ("sbuf", [128, 2 * K], BF), "d0": ("sbuf", [128, K], F), "da": ("sbuf", [128, K], F),
-    "t1": ("sbuf", [128, K], F), "t2": ("sbuf", [128, K], F), "t3": ("sbuf", [128, K], F), "t4": ("sbuf", [128, K], F),
-    "t5": ("sbuf", [128, K], F), "t6": ("sbuf", [128, K], BF),
-    "vc": ("sbuf", [128, K], BF), "thr": ("sbuf", [128, K], BF), "ft": ("sbuf", [128, 128], BF),
-    "io1": ("sbuf", [128, K], F), "mg": ("sbuf", [128, 64], BF),
-    "col": ("sbuf", [128, 8], F), "wa": ("sbuf", [128, 16], F), "wb": ("sbuf", [128, 16], F),
-    "wc": ("sbuf", [128, 16], F), "wd": ("sbuf", [128, 16], F),
-    "pz": ("sbuf", [128, 16], BF), "dum": ("sbuf", [128, 12], F), "pw": ("sbuf", [128, 12], F), "tw": ("sbuf", [128, 12], F),
-    "qi": ("sbuf", [128, K], I), "qf": ("sbuf", [128, K], F), "ci": ("sbuf", [128, 8], I), "cf": ("sbuf", [128, 8], F),
-    "at": ("sbuf", [128, K], U), "nm": ("sbuf", [128, K], F), "kp": ("sbuf", [128, K], F), "kf": ("sbuf", [128, 3 * K], F),
-    "a0": ("sbuf", [128, 3 * K], F), "a1": ("sbuf", [128, 3 * K], F), "q0": ("sbuf", [128, 3 * K], F), "q1": ("sbuf", [128, 3 * K], F),
-    "ne": ("sbuf", [128, K], BF), "ks": ("sbuf", [128, K], F), "eq": ("sbuf", [128, 2 * K], BF),
-    "ls": ("sbuf", [128, K], F), "ll": ("sbuf", [128, 16], U), "wf": ("sbuf", [128, K], F), "gs": ("sbuf", [128, K], F),
-    "gl": ("sbuf", [128, 64], U), "glr": ("sbuf", [128, 64], U), "nl": ("sbuf", [128, 4 * K], U), "nlr": ("sbuf", [128, 4 * K], U),
-    "gw": ("sbuf", [128, 36], BF), "rw": ("sbuf", [128, 40], BF), "cz": ("sbuf", [128, 32], BF), "nz": ("sbuf", [128, 32], BF),
-    "zr": ("sbuf", [128, 12], F), "mb": ("sbuf", [128, 12], F), "dl": ("sbuf", [128, 64], U), "cc": ("sbuf", [128, 8], F),
-    "qs": ("sbuf", [128, K], F), "ql": ("sbuf", [128, 16], U), "px": ("sbuf", [128, 12], F), "s2": ("sbuf", [128, K], BF),
-}
+SCRATCH = {}
+for _names, _cols, _dt in (
+        ("x lt", WX, BF), ("idw", K + NX, I), ("ga gb gd sc rm", 16 * K, BF), ("wk", 2048, BF), ("w0 o8 o1 o70 tri0 ptri ntri", 256, BF),
+        ("idb pz ft", 128, BF), ("rot ones sel0 sel", 256, F), ("idf", 128, F), ("gm col cf cc", 8, F), ("di dj", 272, I), ("dm", 272, F),
+        ("mz eq", 2 * K, BF), ("d0 t1 t2 t3 t4 t5 io1 qf kp ks ls wf gs qs", K, F), ("t6 vc th ne s2", K, BF), ("mg", 160, BF),
+        ("wa wb wc wd", 16, F), ("dum zr px", 24, F), ("qi", K, I), ("ci", 8, I), ("at", K, U), ("nw", K + 32, F),
+        ("kf a0 a1 q0 q1", 3 * K, F), ("ll ql", 16, U), ("gl glr", 128, U), ("nl nlr", 4 * K, U), ("gw", 84, BF), ("rw", 40, BF),
+        ("cz", 48, BF), ("nz", 32, BF), ("dl", 256, U)):
+    for _n in _names.split():
+        SCRATCH[_n] = ("sbuf", [128, _cols], _dt)
 PSUM = ("pa", "pb", "pc", "pd", "pe", "pf", "py", "pr")
-for _b in PSUM:
-    SCRATCH[_b] = ("psum", [128, 512], F)
+for _n in PSUM:
+    SCRATCH[_n] = ("psum", [128, 512], F)
 SEMAPHORES = (["cv", "cs", "cp", "cg", "sent", "lq", "li", "lr", "le", "lc", "lz", "lm", "oa", "ob", "oq", "od", "an0"]
               + ["an%d" % t for t in range(1, 5)] + ["ag%d" % t for t in range(1, 5)])
 QSEM = {"V": "cv", "S": "cs", "P": "cp", "G": "cg"}
@@ -153,9 +132,10 @@ def rank_program(g, core, T, topo):
     V, S, P = g.vector, g.scalar, g.tensor
     n = len(T.cores)
     ne = min(len(topo.engines(a, b)) for a in T.cores for b in T.cores if a != b)
-    ops = []
-    sends = []
-    tag = [None]
+    ops, sends, tag = [], [], [None]
+
+    def cfg(name, t):
+        return CFG[name + {1: "1", 4: "4"}.get(t, "")]
 
     def op(q, fn, r=(), w=(), ext=(), dma=None, remote=False):
         ops.append({"q": q, "fn": fn, "r": list(r), "w": list(w), "ext": list(ext), "dma": dma, "remote": remote, "tag": tag[0]})
@@ -179,7 +159,12 @@ def rank_program(g, core, T, topo):
         op("V", lambda: V.memset(ap, c), (), w)
 
     def act(out, in_, r, w, bias=None, scale=None, ext=(), func=None):
-        if bias is None and scale is None:
+        if tag[0][1] in cfg("v", tag[0][0]):
+            if bias is None:
+                cp(out, in_, r, w, ext)
+            else:
+                ts(out, in_, bias, None, A.add, None, r, w, ext)
+        elif bias is None and scale is None:
             op("S", lambda: S.activation(out, in_, func or AF.Copy), r, w, ext)
         elif bias is None:
             op("S", lambda: S.activation(out, in_, AF.Identity, scale=scale), r, w, ext)
@@ -189,14 +174,14 @@ def rank_program(g, core, T, topo):
     def mm(out, lhsT, rhs, start, stop, r, w):
         op("P", lambda: P.matmul(out, lhsT, rhs, start, stop), r, w)
 
-    def iota(out, pat, base, cm, w):
-        op("G", lambda: g.iota(out, pat, base, cm, allow_small_or_imprecise_dtypes=True), (), w)
+    def iota(out, pat, base, w):
+        op("G", lambda: g.iota(out, pat, base, 0, allow_small_or_imprecise_dtypes=True), (), w)
 
     def pick(out, in_, pat, cmp, fill, base, cm, r, w):
         op("G", lambda: g.affine_select(out, in_, pat, cmp, fill, base, cm), r, w)
 
-    def load(out, in_, r, w, sem, q="Y", ext=()):
-        op(q, lambda: (g.sync if q == "Y" else g.scalar).dma_start(out, in_), r, w, ext, dma=sem)
+    def load(out, in_, r, w, sem, q="Y"):
+        op(q, lambda: (g.sync if q == "Y" else g.scalar).dma_start(out, in_), r, w, dma=sem)
 
     def send(t, dst_ap, src_ap, sem, r):
         dst = T.cores[(rank + SR[t % 3]) % n]
@@ -217,18 +202,12 @@ def rank_program(g, core, T, topo):
         else:
             ts(out, src, scale, None, A.mult, None, r, w, ext)
 
-    xw = T.x
-    DM = T.dm[:, 1:K + 1]
-    IDB = T.idb[:]
-    BIG = float(2 ** 22)
-    CH = {"H": (CFG["lo"], K), "L": (0, CFG["lo"])}
+    xw, DM, IDB, BIG = T.x, T.dm[:, 1:K + 1], T.idb[:], float(2 ** 22)
+    CH = {"H": (64, K), "L": (0, 64)}
     NB, KB, LB = {"H": "pa", "L": "pb"}, {"H": "pc", "L": "pd"}, {"H": "pe", "L": "pf"}
+    SPAN = ((0, 128, "pc"), (128, K, "pd"))
     WK = ["wk%d" % k for k in range(16)]
-    LT = ["lta", "ltb0", "ltb1", "ltb2"]
-    GS = ["gs0", "gs1"]
-
-    def cfg(name, t):
-        return CFG[name + {1: "1", 4: "4"}.get(t, "")]
+    LT = ["lta", "ltb"]
 
     def queue(name):
         return T[name][:, 2 * K:3 * K]
@@ -253,128 +232,131 @@ def rank_program(g, core, T, topo):
         mm(T.pr[:, 0:K], IDB, T.mz[:, 0:K], False, True, ["idb", "m1"], ["pr"])
         mm(T.py[:, 0:K], T.sel[0:8, 0:128], T.qf[0:8, :], True, True, ["sel", "qf"], ["py"])
 
-    def c_wk(t):
-        for k in range(16):
+    def c_wk(j):
+        for k in range(4 * j, 4 * j + 4):
             act(T.wk[:, 129 * k:128 * (k + 1):16], T.gm[:], ["gm", "wd", "wk"], ["wk%d" % k], scale=T.wd[:, k:k + 1])
 
     def c_tri(t):
         pick(T.tri0[:], T.o1[:], [[0, 2], [1, 128]], A.is_ge, 0.0, 0, -1, ["o1"], ["tri0"])
         pick(T.ptri[:], T.tri0[:], [[0, 2], [1, 128]], A.not_equal, 512.0, 0, -1, ["tri0"], ["ptri"])
 
-    def c_ft(t):
-        act(T.ft[:, 32 * (t - 1):32 * t], T.ones[:, 0:32], ["ones"], ["ft%d" % (t - 1)], scale=2.0 ** (STEP * (t - 1) - 78))
-
     def c_pz(t):
         ts(T.col[:, 1:2], T.dj[:, 1:2], float(-W), None, A.add, None, ["dj"], ["col1"])
-        act(T.pz[:, 0:12], T.t1[:, 0:K:16], ["t1", "col1"], ["pz"], bias=T.col[:, 1:2])
+        act(T.pz[:, 12:24], T.t1[:, 0:K:16], ["t1", "col1"], ["pz"], bias=T.col[:, 1:2])
 
     def c_pads(t):
-        iota(T.pz[:, 12:14], [[320, 2]], -320, 0, ["pz0"])
-        iota(T.gw[:], [[0, 36]], 0, 0, ["gw", "gw0"])
+        iota(T.pz[:, 24:88], [[0, 64]], 0, ["pz0"])
+        iota(T.pz[:, 88:112], [[192, 2], [0, 12]], -896, ["pz0"])
+        iota(T.pz[:, 112:116], [[0, 4]], -320, ["pz0"])
+        iota(T.pz[:, 116:128], [[0, 12]], -2 ** 22, ["pz0"])
+        iota(T.gw[:], [[0, 84]], 0, ["gw", "gw0"])
+        iota(T.dum[:, 0:12], [[0, 12]], W, ["zw"])
 
-    def spare(name):
-        return lambda t: iota(T[name][:, 0:2 * K], [[0, 2 * K]], 0, 0, [name + "d"])
-
-    def c_rm1(t):
-        iota(T.rm[:, 0:16 * K:16], [[0, K]], -64, 0, ["rma", "rmb", "rm0"])
+    def c_rw(t):
+        iota(T.rw[:], [[0, 40]], 0, ["rw", "rw0"])
+        iota(T.zr[:, 0:12], [[0, 12]], W, ["zw"])
 
     def c_cf(t):
         cp(T.cf[0:8, 0:1], T.ci[0:8, 0:1], ["ci"], ["cf"])
         mm(T.pr[:, 256:257], T.sel[0:8, 0:128], T.cf[0:8, 0:1], True, True, ["sel", "cf"], ["pr"])
 
-    def c_zq(t):
-        for j, a in enumerate(range(CFG["z"], WX, 8 * K)):
-            b = min(a + 8 * K, WX)
-            load(T.lt[:, a:b], T.rm[:, 0:b - a], ["rma"], ["ltb%d" % j], "lz")
+    def spare(name):
+        return lambda t: iota(T[name][:, 0:2 * K], [[0, 2 * K]], 0, [name + "d"])
 
     steps = {
+        "sel": c_sel, "dj": c_dj, "grp": c_grp, "que": c_que, "tri": c_tri, "pz": c_pz, "pads": c_pads, "rw0": c_rw, "cf": c_cf,
+        "wk": lambda t: c_wk(0), "wkb": lambda t: c_wk(1), "wkc": lambda t: c_wk(2), "wkd": lambda t: c_wk(3),
+        "a0d": spare("a0"), "a1d": spare("a1"), "kfd": spare("kf"), "q0d": spare("q0"), "q1d": spare("q1"),
         "ones": lambda t: ms(T.ones[:], 1.0, ["ones"]),
-        "di": lambda t: op("G", lambda: g.iota(T.di[:], [[-1, 272]], 273, 1), (), ["di"]),
-        "sel": c_sel, "dj": c_dj, "grp": c_grp, "wk": c_wk, "tri": c_tri, "ft": c_ft, "pz": c_pz, "pads": c_pads,
-        "rm1": c_rm1, "cf": c_cf, "zq": c_zq,
-        "t1": lambda t: iota(T.t1[:], [[1, K]], W, 0, ["t1"]),
         "mz0": lambda t: ms(T.mz[:, K:2 * K], 0.0, ["mz0"]),
-        "t2": lambda t: act(T.t2[:], DM, ["dm"], ["t2"], scale=8192.0, bias=-10.0),
-        "que": c_que,
-        "ide": lambda t: load(T.idw[:, NT:NX], T.idx[:, 0:NX - NT], (), ["ide"], "le"),
-        "rmb": lambda t: load(T.rm[:, 8 * K:16 * K], T.rm[:, 0:8 * K], ["rma"], ["rmb"], "lm"),
-        "t5": lambda t: act(T.t5[:], DM, ["dm"], ["t5"], scale=1.0 / BASE - 1.0, bias=1.0),
-        "m1": lambda t: act(T.mz[:, 0:K], DM, ["dm"], ["m1"], scale=-BIG, bias=BIG),
-        "t6": lambda t: act(T.t6[:], DM, ["dm"], ["t6"], scale=-2.0 ** 70, bias=2.0 ** 70),
         "wk0": lambda t: ms(T.wk[:], 0.0, ["wk"]),
+        "zv": lambda t: ms(T.lt[:, 0:ZV], 0.0, ["lta"]),
+        "zq": lambda t: load(T.lt[:, ZV:WX], T.rm[:, 0:WX - ZV], ["rma"], ["ltb"], "lz"),
+        "ide": lambda t: load(T.idw[:, K + NT:K + NX], T.idx[:, 0:NX - NT], (), ["ide"], "le"),
+        "rmb": lambda t: load(T.rm[:, 8 * K:16 * K], T.rm[:, 0:8 * K], ["rma"], ["rmb"], "lm"),
+        "cur": lambda t: op("G", lambda: g.dma_start(T.ci[0:8, 0:1], T.cur[:], allow_slow_non_contiguous=True), (), ["ci"], dma="lc"),
+        "di": lambda t: op("G", lambda: g.iota(T.di[:], [[-1, 272]], 273, 1), (), ["di"]),
+        "t1": lambda t: iota(T.t1[:], [[1, K]], W, ["t1"]),
+        "xd": lambda t: iota(xw[:, W:WX], [[0, K]], 0, ["xd"]),
+        "io1": lambda t: iota(T.io1[:], [[1, K]], UP - K, ["io1"]),
+        "rm0": lambda t: iota(T.rm[:, 0:8 * K], [[0, 8 * K]], 0, ["rma"]),
+        "rm1": lambda t: iota(T.rm[:, 0:16 * K:16], [[0, K]], -64, ["rma", "rmb", "rm0"]),
+        "mg": lambda t: iota(T.mg[:], [[0, 160]], int(MAGIC), ["mg"]),
+        "ft": lambda t: act(T.ft[:, 32 * (t - 1):32 * t], T.ones[:, 0:32], ["ones"], ["ft%d" % (t - 1)], scale=2.0 ** (STEP * (t - 1) - 78)),
+        "t2": lambda t: act(T.t2[:], DM, ["dm"], ["t2"], scale=8192.0, bias=-10.0),
+        "t5": lambda t: act(T.t5[:], DM, ["dm"], ["t5"], scale=1.0 / BASE - 1.0, bias=1.0),
+        "t6": lambda t: act(T.t6[:], DM, ["dm"], ["t6"], scale=-2.0 ** 70, bias=2.0 ** 70),
+        "gm": lambda t: act(T.gm[:], T.pc[:, 0:128:16], ["pc"], ["gm"]),
+        "o8": lambda t: act(T.o8[:], T.pc[:, 0:256], ["pc"], ["o8"], scale=8192.0),
+        "w0": lambda t: act(T.w0[:], T.pc[:, 0:256], ["pc", "wd"], ["w0"], scale=T.wd[:, 0:1]),
+        "o1": lambda t: act(T.o1[:], T.o8[:], ["o8"], ["o1"], scale=1.0 / 8192),
+        "o70": lambda t: act(T.o70[:], T.o8[:], ["o8"], ["o70"], scale=2.0 ** 57),
+        "idf": lambda t: act(T.idf[:], IDB, ["idb"], ["idf"]),
+        "thr": lambda t: act(T.th[:], T.vc[:], ["vc"], ["th"], scale=-18.0 * 2 ** 15),
+        "ntri": lambda t: act(T.ntri[:], T.ptri[:], ["ptri"], ["ntri"], scale=-1.0),
+        "dum": lambda t: act(T.dum[:, 12:24], T.pz[:, 12:24], ["pz"], ["dum"], bias=128.0),
+        "pw": lambda t: act(T.pz[:, 0:12], T.pz[:, 12:24], ["pz"], ["pw"], bias=8192.0, scale=8192.0),
+        "cc": lambda t: act(T.cc[:, 0:1], T.pr[:, 256:257], ["pr"], ["cc0"]),
+        "qh": lambda t: op("S", lambda: S.activation(queue("q0"), T.py[:, 0:K], AF.Silu, bias=float(UP)), ["py"], ["q0"]),
         "wa": lambda t: ts(T.wa[:], T.dm[:, 1:17], 256.0, None, A.mult, None, ["dm"], ["wa"]),
         "wb": lambda t: ts(T.wb[:], T.dm[:, 2:18], 16.0, None, A.mult, None, ["dm"], ["wb"]),
         "wc": lambda t: tt(T.wc[:], T.wa[:], T.dm[:, 3:19], A.add, ["wa", "dm"], ["wc"]),
         "wd": lambda t: tt(T.wd[:], T.wc[:], T.wb[:], A.add, ["wc", "wb"], ["wd"]),
-        "gm": lambda t: act(T.gm[:], T.pc[:, 0:128:16], ["pc"], ["gm"]),
-        "o8": lambda t: act(T.o8[:], T.pc[:, 0:256], ["pc"], ["o8"], scale=8192.0),
-        "w0": lambda t: act(T.w0[:], T.pc[:, 0:256], ["pc", "wd"], ["w0"], scale=T.wd[:, 0:1]) if t == 0 else waits(0),
-        "o1": lambda t: act(T.o1[:], T.o8[:], ["o8"], ["o1"], scale=1.0 / 8192),
-        "qs0": lambda t: scan(T.qs[:], T.d0[:], T.pr[:, 0:K], -5.0, A.max, A.min, ["d0", "pr"], ["qs"]),
-        "d0": lambda t: tt(T.d0[:], T.t1[:], T.t2[:], A.min, ["t1", "t2"], ["d0"]) if t == 0 else digits(t, 0),
-        "ql0": lambda t: cp(T.ql[:, 0:12], wrapped(T.qs), ["qs"], ["ql"]),
-        "qh": lambda t: op("S", lambda: S.activation(queue("q0"), T.py[:, 0:K], AF.Silu, bias=float(UP)), ["py"], ["q0"]),
         "idb": lambda t: tt(IDB, T.pd[:, 0:128], T.dm[:, 1:129], A.mult, ["pd", "dm"], ["idb"]),
         "rot": lambda t: tt(T.rot[:], T.pd[:, 0:256], T.dm[:, 2:258], A.mult, ["pd", "dm"], ["rot"]),
         "vc": lambda t: scan(T.vc[:], T.t5[:], T.mz[:, K:2 * K], BASE ** 12 / 8, A.mult, A.add, ["t5", "mz0"], ["vc"]),
-        "xd": lambda t: iota(xw[:, W:WX], [[0, K]], 0, 0, ["xd"]),
-        "io1": lambda t: iota(T.io1[:], [[1, K]], UP - K, 0, ["io1"]),
-        "a0d": spare("a0"), "a1d": spare("a1"), "kfd": spare("kf"), "q0d": spare("q0"), "q1d": spare("q1"),
-        "rw0": lambda t: iota(T.rw[:], [[0, 40]], 0, 0, ["rw", "rw0"]),
-        "thr": lambda t: act(T.thr[:], T.vc[:], ["vc"], ["thr"], scale=-18.0 * 2 ** 15),
-        "at0": lambda t: cp(T.at[:], T.idw[:, 0:NT].indirect(T.ql[:, 0:12]), ["idw", "ql"], ["at"]),
-        "zv": lambda t: ms(T.lt[:, 0:CFG["z"]], 0.0, ["lta"]),
-        "ntri": lambda t: act(T.ntri[:], T.ptri[:], ["ptri"], ["ntri"], scale=-1.0),
-        "dum": lambda t: act(T.dum[:], T.pz[:, 0:12], ["pz"], ["dum"], bias=128.0),
-        "pw": lambda t: act(T.pw[:], T.pz[:, 0:12], ["pz"], ["pw"], bias=-511.0 * 8192, scale=8192.0),
-        "rm0": lambda t: iota(T.rm[:, 0:8 * K], [[0, 8 * K]], 0, 0, ["rma"]),
-        "cur": lambda t: op("G", lambda: g.dma_start(T.ci[0:8, 0:1], T.cur[:], allow_slow_non_contiguous=True), (), ["ci"], dma="lc"),
-        "cc": lambda t: cp(T.cc[:, 0:1], T.pr[:, 256:257], ["pr"], ["cc0"]),
-        "mg": lambda t: iota(T.mg[:], [[0, 64]], int(MAGIC), 0, ["mg"]),
-        "px": lambda t: act(T.px[:], T.pz[:, 0:12], ["pz"], ["px"], bias=float(-K)),
+        "qi": lambda t: cp(T.qf[0:8, :], T.qi[0:8, :], ["qi"], ["qf"]),
+        "qs0": lambda t: scan(T.qs[:], T.d0[:], T.pr[:, 0:K], -5.0, A.max, A.min, ["d0", "pr"], ["qs"]),
+        "ql0": lambda t: cp(T.ql[:, 0:12], wrapped(T.qs), ["qs"], ["ql"]),
+        "at0": lambda t: cp(T.at[:], T.idw[:, K:K + NT].indirect(T.ql[:, 0:12]), ["idw", "ql"], ["at"]),
+        "ah": lambda t: ts(queue("a0"), T.at[:], float(UP), None, A.add, None, ["at"], ["a0"]),
     }
 
-    def masks(t, h):
+    def part(e, buf, name, win, lst, o, c, v, w, r, scale=None):
+        a = 64 * c
+        lo, hi = {"V": (a, a + v), "W": (a + v, a + v + w), "S": (a + v + w, a + 64)}[e]
+        gather("S" if e == "S" else "V", buf[:, 16 * lo:16 * hi], win[:, 0:W].indirect(lst[:, o + lo:o + hi]), r,
+               ["%s%s%d" % (name, e, c)], scale=scale)
+
+    def index_digits(t, c, e):
+        part(e, T.ga, "ga", xw, T.at, 0, c, cfg("a", t)[c], 0 if c else cfg("aw", t), ["x", "at"])
+
+    def round_up(t, h):
         a, b = CH[h]
-        m = b - a
+        mm(T[NB[h]][:, 0:b - a], IDB, T.mg[:, 0:b - a], True, False, ["idb", "mg"], [NB[h]])
+
+    def names(t, c, ks=range(16)):
+        h, a = "H" if c else "L", 64 * c
+        for k in ks:
+            mm(T[NB[h]][:, a - CH[h][0]:a + 64 - CH[h][0]], T.wk[:, 128 * k:128 * (k + 1)], T.ga[:, 16 * a + k:16 * (a + 64):16],
+               False, k == 15 and c < 2, ["ga%s%d" % (e, c) for e in "VWS"] + WK, [NB[h]])
+
+    def keep_names(t, h):
+        a, b = CH[h]
+        act(T.nw[:, 16 + a:16 + b], T[NB[h]][:, 0:b - a], [NB[h]], ["nm" + h], bias=(0 if t == 4 else UP) - MAGIC)
+
+    def masks(t, h):
+        m = CH[h][1] - CH[h][0]
         mm(T[KB[h]][:, 0:2 * m], IDB, T.mz[:, K - m:K + m], True, False, ["idb", "m1", "mz0"], [KB[h]])
         mm(T[LB[h]][:, 0:m], IDB, T.mz[:, 0:m], True, False, ["idb", "m1"], [LB[h]])
 
-    def part(e, buf, name, win, lst, o, c, v, r, scale=None):
-        a = 64 * c
-        lo, hi = (a, a + v) if e == "V" else (a + v, a + 64)
-        if hi > lo:
-            gather(e, buf[:, 16 * lo:16 * hi], win[:, 0:W].indirect(lst[:, o + lo:o + hi]), r, ["%s%s%d" % (name, e, c)], scale=scale)
-
-    def index_digits(t, c, e):
-        part(e, T.ga, "ga", xw, T.at, 0, c, cfg("a", t)[c], ["x", "at"])
-
-    def names(t, c):
-        h = "H" if 64 * c >= CFG["lo"] else "L"
-        a = 64 * c
-        out = T[NB[h]][:, a - CH[h][0]:a - CH[h][0] + 64]
-        mm(out, IDB, T.mg[:], True, False, ["idb", "mg"], [NB[h]])
-        for k in range(16):
-            mm(out, T.wk[:, 128 * k:128 * (k + 1)], T.ga[:, 16 * a + k:16 * (a + 64):16], False, k == 15,
-               ["gaV%d" % c, "gaS%d" % c] + WK, [NB[h]])
-
-    def keys(t, h):
+    def keys(t, h, holder=False):
         a, b = CH[h]
         m, u = b - a, SG[t % 3]
-        r = ["ga%s%d" % (e, c) for e in "VS" for c in range(a // 64, b // 64)] + ["w0"]
+        r = ["ga%s%d" % (e, c) for e in "VWS" for c in ((1, 2) if a else (0,))] + ["w0"]
         g0 = T.ga[:, 16 * a:16 * b:16]
-        mm(T[KB[h]][:, 0:m], turn(T.w0, 0, u), g0, False, False, r, [KB[h]])
-        mm(T[KB[h]][:, m:2 * m], turn(T.w0, 0, u), g0, False, t == 1, r, [KB[h]])
-        mm(T[LB[h]][:, 0:m], turn(T.w0, 0, u), g0, False, False, r, [LB[h]])
+        if holder:
+            mm(T[LB[h]][:, 0:m], turn(T.w0, 0, u), g0, False, False, r, [LB[h]])
+            if t > 1:
+                mm(T[LB[h]][:, 0:m], turn(T.o8, 0, u), T.ne[:, a:b], False, False, ["o8", "ne" + h], [LB[h]])
+        else:
+            mm(T[KB[h]][:, 0:m], turn(T.w0, 0, u), g0, False, False, r, [KB[h]])
+            mm(T[KB[h]][:, m:2 * m], turn(T.w0, 0, u), g0, False, t == 1, r, [KB[h]])
 
     def changed(t, h):
         a, b = CH[h]
-        m, u = b - a, SG[t % 3]
-        tt(T.ne[:, a:b], T[NB[h]][:, 0:m], T.kp[:, a:b], A.not_equal, [NB[h], "kp"], ["ne" + h])
-        r = ["o8", "ne" + h]
-        mm(T[KB[h]][:, 0:m], turn(T.o8, 0, u), T.ne[:, a:b], False, False, r, [KB[h]])
-        mm(T[KB[h]][:, m:2 * m], turn(T.o8, 0, u), T.ne[:, a:b], False, True, r, [KB[h]])
-        mm(T[LB[h]][:, 0:m], turn(T.o8, 0, u), T.ne[:, a:b], False, False, r, [LB[h]])
+        tt(T.ne[:, a:b], T[NB[h]][:, 0:b - a], T.kp[:, a:b], A.not_equal, [NB[h], "kp"], ["ne" + h])
+        mm(T[KB[h]][:, 0:b - a], turn(T.o8, 0, SG[t % 3]), T.ne[:, a:b], False, True, ["o8", "ne" + h], [KB[h]])
 
     def hold_keys(t, h):
         a, b = CH[h]
@@ -383,8 +365,9 @@ def rank_program(g, core, T, topo):
     def twins(t, j, h):
         a, b = CH[h]
         m, d = b - a, 1 + 16 * j
-        tt(T.eq[:, j * K + a + d:j * K + b], T[KB[h]][:, m + d:2 * m], T.ks[:, a:b - d], A.is_equal, [KB[h], "ks" + h], ["eq%d%s" % (j, h)])
-        mm(T[LB[h]][:, d:m], T.o8[:, 0:128], T.eq[:, j * K + a + d:j * K + b], False, j == 1, ["o8", "eq%d%s" % (j, h)], [LB[h]])
+        eq = T.eq[:, j * K + a + d:j * K + b]
+        tt(eq, T[KB[h]][:, m + d:2 * m], T.ks[:, a:b - d], A.is_equal, [KB[h], "ks" + h], ["eq%d%s" % (j, h)])
+        mm(T[LB[h]][:, d:m], T.o8[:, 0:128], eq, False, j == 1, ["o8", "eq%d%s" % (j, h)], [LB[h]])
 
     def holders(t, h):
         a, b = CH[h]
@@ -396,11 +379,34 @@ def rank_program(g, core, T, topo):
 
     def lock(t, j):
         tt(T.lt[:, 0:WX].indirect(T.ll[:, 2 * j:2 * j + 2]), T.vc[:, 32 * j:32 * j + 32], T.ft[:, 32 * (t - 1):32 * t], A.mult,
-           ["vc", "ft%d" % (t - 1), "llH" if 32 * j >= CFG["lo"] else "llL"], LT)
+           ["vc", "ft%d" % (t - 1), "llH" if j > 1 else "llL"], LT)
 
-    def keep_names(t, h):
-        a, b = CH[h]
-        act(T.nm[:, a:b], T[NB[h]][:, 0:b - a], [NB[h]], ["nm" + h], bias=(0 if t == 4 else UP) - MAGIC)
+    def locks(t, c, e):
+        part(e, T.gb, "gb", T.lt, T.nl, K * (t - 1), c, cfg("b", t)[c], 0, LT + ["nl%d_0" % t, "nl%d_64" % t],
+             scale=2.0 ** (93 - STEP * (t - 1)))
+
+    def thresholds(t, j):
+        lo, hi, b = SPAN[j]
+        mm(T[b][:, 0:hi - lo], IDB, T.th[:, lo:hi], True, False, ["idb", "th"], [b])
+        mm(T[b][:, 0:hi - lo], IDB, T.t6[:, 0:hi - lo], False, False, ["idb", "t6"], [b])
+        if t > 1:
+            mm(T[b][:, 0:hi - lo], turn(T.o70, 0, SG[t % 3]), T.ne[:, lo:hi], False, False, ["o70", "neH", "neL"], [b])
+
+    def lock_sums(t, c):
+        a = 64 * c
+        lo, hi, b = SPAN[c // 2]
+        for k in range(16):
+            mm(T[b][:, a - lo:a + 64 - lo], IDB, T.gb[:, 16 * a + k:16 * (a + 64):16], False, k == 15 and a + 64 == hi,
+               ["gbV%d" % c, "gbS%d" % c, "idb"], [b])
+
+    def goes(t, j):
+        lo, hi, b = SPAN[j]
+        scan(T.gs[:, lo:hi], T.d0[:, lo:hi], T[b][:, 0:hi - lo], -5.0, A.max, A.min, ["d0", b], ["gs%d" % j])
+
+    def go_list(t):
+        c = slice(32 * t - 16, 32 * t - 4)
+        cp(T.gl[:, c], T.wf[:, 0:12], ["wf"], ["gl%d" % t])
+        send(t, T.glr[:, c], T.gl[:, c], "ag%d" % t, ["gl%d" % t])
 
     def turn_list(t, src, a, b, key):
         mm(T.pr[:, a:b], turn(T.rot, 0, SG[t % 3]), src, True, True, ["rot", key], ["pr"])
@@ -410,37 +416,6 @@ def rank_program(g, core, T, topo):
         ts(T.nl[:, o + a:o + b], T.pr[:, a:b], 0.25 - UP, None, A.add, None, ["pr"], ["nl%d_%d" % (t, a)])
         send(t, T.nlr[:, o + a:o + b], T.nl[:, o + a:o + b], sem, ["nl%d_%d" % (t, a)])
 
-    def locks(t, c, e):
-        part(e, T.gb, "gb", T.lt, T.nl, K * (t - 1), c, cfg("b", t)[c], LT + ["nl%d_0" % t, "nl%d_64" % t], scale=2.0 ** (93 - STEP * (t - 1)))
-
-    def span(j):
-        return (0, CFG["w"], "pc") if j == 0 else (CFG["w"], K, "pd")
-
-    def lock_sums(t, c):
-        a = 64 * c
-        lo, hi, b = span(0 if a < CFG["w"] else 1)
-        if a == lo:
-            mm(T[b][:, 0:hi - lo], IDB, T.thr[:, lo:hi], True, False, ["idb", "thr"], [b])
-            mm(T[b][:, 0:hi - lo], IDB, T.t6[:, 0:hi - lo], False, False, ["idb", "t6"], [b])
-        for k in range(16):
-            mm(T[b][:, a - lo:a - lo + 64], IDB, T.gb[:, 16 * a + k:16 * (a + 64):16], False, k == 15 and a + 64 == hi,
-               ["gbV%d" % c, "gbS%d" % c, "idb"], [b])
-
-    def waits(j):
-        lo, hi, b = span(j)
-        if hi > lo:
-            tt(T.wf[:, lo:hi], T[b][:, 0:hi - lo], T.ks[:, lo:hi], A.max, [b, "ksH", "ksL"], ["wf%d" % j])
-
-    def goes(t, j):
-        lo, hi, b = span(j)
-        if hi > lo:
-            scan(T.gs[:, lo:hi], T.d0[:, lo:hi], T.wf[:, lo:hi], -5.0, A.max, A.min, ["d0", "wf%d" % j], ["gs%d" % j])
-
-    def go_list(t):
-        o = 16 * (t - 1)
-        cp(T.gl[:, o:o + 12], wrapped(T.gs), GS, ["gl%d" % t])
-        send(t, T.glr[:, o:o + 12], T.gl[:, o:o + 12], "ag%d" % t, ["gl%d" % t])
-
     def digits(t, j, q="S"):
         a, b = cfg("d", t)[j:j + 2]
         o = K * (t - 1)
@@ -449,40 +424,56 @@ def rank_program(g, core, T, topo):
 
     def own_digit(t, j):
         a, b = cfg("d", t)[j:j + 2]
-        gather(CFG["own"], T.rm[:, 16 * a + 15:16 * b:16], T.gd[:, 16 * a + 15:16 * b:16], ["gd%d" % j, "rm0"], ["rh%d" % j] + RH)
+        act(T.rm[:, 16 * a + 15:16 * b:16], T.gd[:, 16 * a + 15:16 * b:16], ["gd%d" % j, "rm0"], ["rh%d" % j])
 
     def largest(t, j):
         a, b = cfg("d", t)[j:j + 2]
         scan(T.sc[:, 16 * a:16 * b], T.rm[:, 16 * a:16 * b], T.gd[:, 16 * a:16 * b], 0.0, A.add, A.max, ["rh%d" % j, "gd%d" % j], ["sc%d" % j])
 
-    SC = ["sc%d" % j for j in range(4)]
-    RH = []
+    def sums(t):
+        return ["sc%d" % j for j in range(len(cfg("d", t)) - 1)]
 
     def write_records(t):
-        o = 16 * (t - 1)
-        tt(xw[:, 0:WX].indirect(T.glr[:, o:o + 12]), T.sc[:, 15:16 * K:16], T.s2[:], A.add, ["s2", "xd"] + SC, ["x"], ext=[("ag%d" % t, ne)])
+        tt(xw[:, 0:WX].indirect(T.glr[:, 32 * t - 16:32 * t - 4]), T.sc[:, 15:16 * K:16], T.s2[:], A.add, ["s2", "xd"] + sums(t), ["x"],
+           ext=[("ag%d" % t, ne)])
 
     def restart_counts(t):
         u = SG[t % 3]
         scan(T.nz[:, 0:24], T.rw[:, 0:24], T.rw[:, 12:36], 0.0, A.add, A.subtract, ["rw", "rw0"], ["nz"])
         mm(T.pr[:, 0:12], turn(T.o1, u, 0), T.nz[:, 12:24], True, False, ["o1", "nz"], ["pr"])
         mm(T.pr[:, 0:12], turn(T.ptri, u, 0), T.rw[:, 13:25], False, True, ["ptri", "rw"], ["pr"])
-        mm(T.py[:, 0:12], turn(T.o1, u, 0), T.nz[:, 0:12], False, False, ["o1", "nz"], ["py"])
-        mm(T.py[:, 0:12], turn(T.ntri, u, 0), T.rw[:, 13:25], False, False, ["ntri", "rw"], ["py"])
+        mm(T.py[:, 12:24], turn(T.o1, u, 0), T.nz[:, 0:12], False, False, ["o1", "nz"], ["py"])
+        mm(T.py[:, 12:24], turn(T.ntri, u, 0), T.rw[:, 13:25], False, False, ["ntri", "rw"], ["py"])
+
+    def place_terms(t):
+        mm(T.py[:, 0:113], IDB, T.pz[:, 0:113], True, False, ["idb", "pz", "pz0", "pw"], ["py"])
+        if t < 4:
+            mm(T.py[:, 0:12], IDB, T.pz[:, 116:128], False, False, ["idb", "pz0"], ["py"])
+            mm(T.py[:, 88:100], T.idf[:], T.px[:, 12:24], False, False, ["idf", "px2"], ["py"])
 
     def go_counts(t):
         u = SG[t % 3]
-        scan(T.cz[:, 0:23], T.gw[:, 12:35], T.gw[:, 0:23], 20.0, A.add, A.subtract, ["gw", "gw0"], ["cz"])
-        mm(T.py[:, 0:12], turn(T.ntri, u, 0), T.gw[:, 12:24], False, False, ["ntri", "gw"], ["py"])
-        mm(T.pf[:, 0:1], IDB, T.pz[:, 12:13], True, False, ["idb", "pz0"], ["pf"])
-        mm(T.py[:, 0:12], turn(T.o1, u, 0), T.cz[:, 11:23], False, False, ["o1", "cz"], ["py"])
-        mm(T.py[:, 12:13], turn(T.o1, u, 0), T.cz[:, 11:12], False, t == 4, ["o1", "cz"], ["py"])
+        scan(T.cz[:, 0:47], T.gw[:, 36:83], T.gw[:, 0:47], 20.0, A.add, A.subtract, ["gw", "gw0"], ["cz"])
+        mm(T.py[:, 12:24], turn(T.ntri, u, 0), T.gw[:, 36:48], False, False, ["ntri", "gw"], ["py"])
+        mm(T.pf[:, 0:1], IDB, T.pz[:, 112:113], True, False, ["idb", "pz0"], ["pf"])
+        mm(T.py[:, 12:24], turn(T.o1, u, 0), T.cz[:, 35:47], False, False, ["o1", "cz"], ["py"])
         if t < 4:
-            mm(T.py[:, 13:14], turn(T.o8, u, SG[(t + 1) % 3]), T.cz[:, 11:12], False, True, ["o8", "cz"], ["py"])
+            mm(T.py[:, 0:12], turn(T.o8, u, SG[(t + 1) % 3]), T.cz[:, 11:23], False, False, ["o8", "cz"], ["py"])
+            for j in range(2):
+                mm(T.py[:, 88:112], turn(T.o1, u, 0), T.cz[:, 11:35], False, False, ["o1", "cz"], ["py"])
+        mm(T.py[:, 112:113], turn(T.o1, u, 0), T.cz[:, 11:12], False, True, ["o1", "cz"], ["py"])
         mm(T.pf[:, 0:1], turn(T.o1, u, 0), T.cz[:, 11:12], False, True, ["o1", "cz"], ["pf"])
 
+    def places(t):
+        a = 12 if t == 4 else 0
+        tt(T.py[:, 64 + a:88], T.py[:, a:24], (T.dum if t == 1 else T.zr)[:, a:24], A.max, ["py", "dum", "zr", "zw"], ["py"])
+
+    def place_list(t):
+        m = 12 if t == 4 else 24
+        ts(T.dl[:, 48 * t:48 * t + m], T.py[:, 76:76 + m], T.py[:, 112:113], 64.0, A.subtract, A.add, ["py"], ["dl%d" % t])
+
     def move(t, q, to, src, key):
-        out, r = T[to][:, 0:3 * K].indirect(T.dl[:, 16 * (t - 1):16 * (t - 1) + 12]), key + ["dl%d" % t, to + "d", to]
+        out, r = T[to][:, 0:3 * K].indirect(T.dl[:, 48 * t:48 * t + 12]), key + ["dl%d" % t, to + "d", to]
         if q == "S":
             act(out, src, r, [to], func=AF.Silu)
         else:
@@ -490,7 +481,12 @@ def rank_program(g, core, T, topo):
 
     def along(name, t):
         a, b = "%s%d" % (name, t % 2), "%s%d" % (name, (t + 1) % 2)
-        move(t, cfg("m" + name, t), a, queue(b), [b])
+        if t > 0:
+            move(t, "S", a, queue(b), [b])
+
+    def new_numbers(t):
+        if t > 0:
+            act(queue("q%d" % (t % 2)), T.io1[:], ["io1", "cc%d" % t], ["q%d" % (t % 2)], bias=T.cc[:, t:t + 1])
 
     def numbers(t):
         ts(T.t2[:], queue("q0"), MAGIC - UP, -MAGIC, A.add, A.add, ["q0"], ["t2"])
@@ -500,61 +496,55 @@ def rank_program(g, core, T, topo):
 
     def store(t):
         load(T.yx[0:64, :], xw[0:64, 0:W], ["x"], (), "oa")
-        load(T.yx[64:128, :], xw[64:128, 0:W], ["x"], (), "ob", q="S")
+        load(T.yx[64:128, :], xw[64:128, 0:W], ["x"], (), "ob")
 
     for h in "HL":
-        for name, f in (("m", masks), ("k", keys), ("ne", changed), ("ks", hold_keys), ("ls", holders), ("ll", lock_list), ("nm", keep_names)):
-            steps[name + h] = lambda t, f=f, h=h: f(t, h) if CH[h][1] else None
+        for name, f in (("m", masks), ("r", round_up), ("k", keys), ("p", lambda t, h: keys(t, h, True)), ("ne", changed),
+                        ("ks", hold_keys), ("ls", holders), ("ll", lock_list), ("nm", keep_names)):
+            steps[name + h] = lambda t, f=f, h=h: f(t, h)
         for j in range(2):
-            steps["e%d%s" % (j, h)] = lambda t, j=j, h=h: twins(t, j, h) if CH[h][1] else None
-        a, b = (64, K) if h == "H" else (0, 64)
-        steps["t" + h] = lambda t, a=a, b=b, h=h: turn_list(1, T.nm[:, a:b], a, b, "nm" + (h if CFG["lo"] else "H"))
+            steps["e%d%s" % (j, h)] = lambda t, j=j, h=h: twins(t, j, h)
+        a, b = CH[h]
+        steps["t" + h] = lambda t, a=a, b=b, h=h: turn_list(1, T.nw[:, 16 + a:16 + b], a, b, "nm" + h)
         steps["nl" + h] = lambda t, a=a, b=b: send_list(1, a, b, "an1" if a else "an0")
     for j in range(6):
-        for name, f in (("n", names), ("s", lock_sums), ("l", lock), ("g", goes), ("h", own_digit), ("m", largest), ("d", digits)):
-            steps.setdefault("%s%d" % (name, j), lambda t, f=f, j=j: f(t, j))
-        for e in "VS":
+        for name, f in (("n", names), ("s", lock_sums), ("l", lock), ("g", goes), ("h", own_digit), ("m", largest), ("d", digits),
+                        ("th", thresholds)):
+            steps["%s%d" % (name, j)] = lambda t, f=f, j=j: f(t, j)
+        for e in "VWS":
             steps["a%d%s" % (j, e)] = lambda t, j=j, e=e: index_digits(t, j, e)
             steps["b%d%s" % (j, e)] = lambda t, j=j, e=e: locks(t, j, e)
-        steps["d%dV" % j] = lambda t, j=j: digits(t, j, "V")
-    mask_tile = steps["m1"]
     steps.update({
-        "m1": lambda t: mask_tile(t) if t == 0 else largest(t, 1),
-        "w1": lambda t: waits(1),
-        "ah": lambda t: ts(queue("a0"), T.at[:], float(UP), None, A.add, None, ["at"], ["a0"]),
-        "rw": lambda t: tt(T.rw[:, 13:25], wrapped(T.ks), T.tw[:], A.is_ge, ["ksH", "ksL", "tw", "rw0"], ["rw"]),
-        "py": lambda t: mm(T.py[:, 0:14], IDB, T.pz[:, 0:14], True, False, ["idb", "pz", "pz0"], ["py"]),
-        "nz": restart_counts,
-        "zr": lambda t: tt(T.zr[:], T.pr[:, 0:12], T.dum[:], A.max, ["pr", "dum"], ["zr"]),
+        "m1": lambda t: largest(t, 1) if t else act(T.mz[:, 0:K], DM, ["dm"], ["m1"], scale=-BIG, bias=BIG),
+        "d0": lambda t: digits(t, 0) if t else tt(T.d0[:], T.t1[:], T.t2[:], A.min, ["t1", "t2"], ["d0"]),
+        "d0V": lambda t: digits(t, 0, "V"),
+        "n0": lambda t: names(t, 0, range(8)), "n0b": lambda t: names(t, 0, range(8, 16)),
+        "w": lambda t: tt(T.wf[:, 0:12], wrapped(T.gs), wrapped(T.ks), A.max, ["ksH", "ksL", "gs1", "gs0"], ["wf"]),
         "gl": go_list,
-        "gw": lambda t: ts(T.gw[:, 12:24], wrapped(T.gs), float(W), None, A.is_lt, None, GS + ["gw0"], ["gw"]),
-        "cz": go_counts,
+        "gw": lambda t: ts(T.gw[:, 36:48], wrapped(T.gs), float(W), None, A.is_lt, None, ["gs0", "gs1", "gw0"], ["gw"]),
+        "rw": lambda t: tt(T.rw[:, 13:25], wrapped(T.ks), T.py[:, 64:76], A.is_ge, ["ksH", "ksL", "py", "rw0"], ["rw"]),
+        "zr": lambda t: tt(T.zr[:, 12:24], T.pr[:, 0:12], T.dum[:, 12:24], A.max, ["pr", "dum"], ["zr"]),
+        "py": place_terms, "nz": restart_counts, "cz": go_counts, "mb": places, "dl": place_list,
         "e": lambda t: act(T.cc[:, t:t + 1], T.pf[:, 0:1], ["pf", "cc%d" % (t - 1)], ["cc%d" % t], bias=T.cc[:, t - 1:t]),
-        "mb": lambda t: tt(T.mb[:], T.py[:, 0:12], (T.dum if t == 1 else T.zr)[:], A.max, ["py", "dum", "zr"], ["mb"]),
-        "dl": lambda t: ts(T.dl[:, 16 * (t - 1):16 * (t - 1) + 12], T.mb[:], T.py[:, 12:13], 64.0, A.subtract, A.add, ["mb", "py"], ["dl%d" % t]),
-        "tw": lambda t: ts(T.tw[:], T.pw[:], T.py[:, 13:14], float(W), A.add, A.max, ["pw", "py"], ["tw"]),
-        "nx": lambda t: ts(T.ql[:, 0:12], T.px[:], T.py[:, 12:13], T.cc[:, t - 1:t], A.add, A.add, ["px", "py", "cc%d" % (t - 1)], ["ql"]),
-        "new": lambda t: ts(queue("a%d" % (t % 2)), T.idw[:, 0:NX].indirect(T.ql[:, 0:12]), float(UP), None, A.add, None,
-                            ["idw", "ide", "ql"], ["a%d" % (t % 2)]),
-        "mva": lambda t: along("a", t),
+        "pc": lambda t: act(T.px[:, 12:24], T.pz[:, 12:24], ["pz", "cc%d" % (t - 1)], ["px2"], bias=T.cc[:, t - 1:t]),
+        "new": lambda t: ts(queue("a%d" % (t % 2)), T.idw[:, K:K + NX].indirect(T.dl[:, 48 * t + 12:48 * t + 24]), float(UP), None,
+                            A.add, None, ["idw", "ide", "dl%d" % t], ["a%d" % (t % 2)]),
+        "mva": lambda t: along("a", t), "mvq": lambda t: along("q", t), "qf": new_numbers,
         "at": lambda t: ts(T.at[:], queue("a%d" % (t % 2)), 0.25 - UP, None, A.add, None, ["a%d" % (t % 2)], ["at"]),
-        "kf": lambda t: iota(queue("kf"), [[0, K]], -1 if t == 4 else UP - 1, 0, ["kf"]),
-        "mvk": lambda t: move(t, cfg("mk", t), "kf", T.nm[:], ["nmH", "nmL"]),
+        "kf": lambda t: iota(queue("kf"), [[0, K]], -1 if t == 4 else UP - 1, ["kf"]),
+        "mvk": lambda t: move(t, "V" if t == 4 else "S", "kf", T.nw[:, 16:16 + K], ["nmH", "nmL"]),
         "kp": lambda t: act(T.kp[:], queue("kf"), ["kf"], ["kp"], bias=MAGIC - UP),
         "turn": lambda t: turn_list(t + 1, queue("kf"), 0, K, "kf"),
-        "qf": lambda t: act(queue("q%d" % (t % 2)), T.io1[:], ["io1", "cc%d" % t], ["q%d" % (t % 2)], bias=T.cc[:, t:t + 1])
-        if t else cp(T.qf[0:8, :], T.qi[0:8, :], ["qi"], ["qf"]),
-        "mvq": lambda t: along("q", t),
-        "cy": lambda t: ts(T.s2[:], T.sc[:, 15:16 * K:16], 16.0, -16.0, A.is_ge, A.mult, SC, ["s2"]),
         "nl": lambda t: send_list(t + 1, 0, K, "an%d" % (t + 1)),
+        "cy": lambda t: ts(T.s2[:], T.sc[:, 15:16 * K:16], 16.0, -16.0, A.is_ge, A.mult, sums(t), ["s2"]),
         "x": write_records, "yx": store, "yq": numbers,
         "yd": lambda t: load(T.yd[:], queue("kf"), ["kf"], (), "od"),
     })
 
     load(T.qi[0:8, :], T.que[:], (), ["qi"], "lq", q="S")
-    load(T.idw[:, 0:NT], T.idx[:], (), ["idw"], "li")
+    load(T.idw[:, K:K + NT], T.idx[:], (), ["idw"], "li")
     load(xw[:, 0:W], T.rec[:], (), ["x"], "lr")
-    for t in range(5):
+    for t in range(1, 5):
         for name in ORDER[t].split():
             tag[0] = (t, name)
             steps[name.rstrip("<>")](t - name.count("<") + name.count(">"))

from concourse.mybir import AluOpType, ActivationFunctionType

K = 192
W = 4096
WX = W + K
NT = 2048
NX = NT + 4 * K
SR, SG = (1, 5, 3), (0, 3, 1)
BF, F, I, U = "bfloat16", "float32", "int32", "uint16"
BASE, STEP = 20.0, 52
UP = 32
MAGIC = 1.5 * 2 ** 23
ZV = 2752
CFG = {"a1": (28, 36, 34), "a": (28, 32, 32), "a4": (34, 34, 32), "aw1": 0, "aw": 8, "aw4": 8,
       "b1": (42, 32, 42), "b": (32, 30, 32), "b4": (30, 34, 36),
       "d1": (0, 58, 64, 132, K), "d": (0, 112, 132, K), "d4": (0, 76, 118, K), "v1": ("h3", "pc"), "v": ("nmL",), "v4": ()}
FIRST = ("ones di zv ft sel ft>> ft> dj wk0 wa grp t6 t5 wb gm mg t1 rm0 wc m1< qi t2 wd o8 wkd w0 wk wkb d0< idb que rot qs0 mz0 ql0 "
         "rL at0 wkc ide mL a2S rH mH pz a2V kf< n2 a1S a1V a0V a0S kH kfd cur rmb n1 pw zq ksH q1d nmH pH idf n0 vc o1 tH e0H thr e1H "
         "dum kL n0b ah nlH lsH nmL tL ksL llH pL e0L l5 e1L l4 nlL lsL l3 tri llL qh l2 th1 l1 cf l0 b2S b1S pads cc rm1 b0S th0 b2V "
         "b0V ntri s2 b1V g1 rw0 q0d s0 xd d3 s1 d0V d2 g0 pc h3 py w h0 gw gl cz m3 mH> mb d1 dl h2 h1 m0 m1 m2 mvk new e a1d kp cy "
         "turn nl o70 x rH> mva kf rL> mL> io1 a0d ft>>> at")
MID = ("pc a2V a2S a1V a1S n2 n1 kH a0V neH pH a0W ksH a0S n0 n0b d0 e0H e1H kL neL lsH ksL pL d1 llH e0L l5 e1L th1 l4 h0 lsL th0 l3 "
       "llL l2 l1 rw l0 nmL b0V b0S py b1S b1V b2S s0 b2V m0 s1 s2 g0 d2 g1 h1 nz w h2 gw gl cz zr nmH mb e dl m2 new m1 mvk mva cy "
       "qf<< turn kp mvq<< nl mH> rL> at x kf> mL> rH>")
LAST = ("a2V a2S a1V n2 a0V a1S a0S n1 kH neH a0W pH n0 d2 ksH n0b e0H e1H kL neL d0 lsH ksL th0 pL llH e0L l5 e1L l4 lsL l3 llL l2 l1 "
        "rw th1 l0 py nz b0S b1S h2 b0V b2S s0 b1V h0 qf<< b2V nmL m2 d1 s1 s2 mvq<< h1 zr g0 g1 w qf< gw gl cz nmH mvq< e m0 mb m1 dl "
        "cy mvk qf yd mvq x yx yq")
ORDER = {1: FIRST, 2: MID, 3: MID, 4: LAST}

SCRATCH = {}
for _names, _cols, _dt in (
        ("x lt", WX, BF), ("idw", K + NX, I), ("ga gb gd sc rm", 16 * K, BF), ("wk", 2048, BF), ("w0 o8 o1 o70 tri0 ptri ntri", 256, BF),
        ("idb pz ft", 128, BF), ("rot ones sel0 sel", 256, F), ("idf", 128, F), ("gm col cf cc", 8, F), ("di dj", 272, I), ("dm", 272, F),
        ("mz eq", 2 * K, BF), ("d0 t1 t2 t3 t4 t5 io1 qf kp ks ls wf gs qs", K, F), ("t6 vc th ne s2", K, BF), ("mg", 160, BF),
        ("wa wb wc wd", 16, F), ("dum zr px", 24, F), ("qi", K, I), ("ci", 8, I), ("at", K, U), ("nw", K + 32, F),
        ("kf a0 a1 q0 q1", 3 * K, F), ("ll ql", 16, U), ("gl glr", 128, U), ("nl nlr", 4 * K, U), ("gw", 84, BF), ("rw", 40, BF),
        ("cz", 48, BF), ("nz", 32, BF), ("dl", 256, U)):
    for _n in _names.split():
        SCRATCH[_n] = ("sbuf", [128, _cols], _dt)
PSUM = ("pa", "pb", "pc", "pd", "pe", "pf", "py", "pr")
for _n in PSUM:
    SCRATCH[_n] = ("psum", [128, 512], F)
SEMAPHORES = (["cv", "cs", "cp", "cg", "sent", "lq", "li", "lr", "le", "lc", "lz", "lm", "oa", "ob", "oq", "od", "an0"]
              + ["an%d" % t for t in range(1, 5)] + ["ag%d" % t for t in range(1, 5)])
QSEM = {"V": "cv", "S": "cs", "P": "cp", "G": "cg"}


def emit(g, T, ops):
    eng = {"V": g.vector, "S": g.scalar, "P": g.tensor, "G": g, "Y": g.sync}
    writer, readers = {}, {}
    known = {q: {} for q in eng}
    clock, waits, needed = [], [], set()
    for n, o in enumerate(ops):
        q = o["q"]
        deps = set()
        for k in o["r"]:
            if k in writer:
                deps.add(writer[k])
            if k in PSUM:
                deps.update(m for m in readers.get(k, []) if ops[m]["q"] != q)
        for k in o["w"]:
            if k in writer:
                deps.add(writer[k])
            deps.update(readers.get(k, []))
        kn = known[q]
        mine = []
        for m in sorted(deps, reverse=True):
            d = ops[m]
            if d["remote"]:
                continue
            if d["dma"] is None and d["q"] == q and o["dma"] is None and q == "P":
                continue
            key = d["q"] if d["dma"] is None else "dma:" + d["dma"]
            if kn.get(key, -1) >= m:
                continue
            mine.append(m)
            needed.add(m)
            for a, b in clock[m].items():
                if kn.get(a, -1) < b:
                    kn[a] = b
            kn[key] = max(kn.get(key, -1), m)
        ext = []
        for s, v in o["ext"]:
            if kn.get("ext:" + s, -1) < v:
                ext.append((s, v))
                kn["ext:" + s] = v
        waits.append((mine, ext))
        clock.append(dict(kn))
        for k in o["r"]:
            readers.setdefault(k, []).append(n)
        for k in o["w"]:
            writer[k] = n
            readers[k] = []
    count, total = {}, {}
    for n, o in enumerate(ops):
        if o["dma"] is not None:
            total[o["dma"]] = total.get(o["dma"], 0) + 16
        elif n in needed:
            total[o["q"]] = total.get(o["q"], 0) + 1
            count[n] = total[o["q"]]
    seen = set()
    for n, o in enumerate(ops):
        e = eng[o["q"]]
        mine, ext = waits[n]
        for s, v in ext:
            e.wait_ge(T.sem[s], v)
        done = set()
        for m in mine:
            d = ops[m]
            if d["dma"] is not None:
                if d["dma"] not in done:
                    e.wait_ge(T.sem[d["dma"]], total[d["dma"]])
                    done.add(d["dma"])
                    seen.add(d["dma"])
            else:
                e.wait_ge(T.sem[QSEM[d["q"]]], count[m])
        ins = o["fn"]()
        if o["dma"] is not None:
            ins.then_inc(T.sem[o["dma"]], 16)
        elif n in needed:
            ins.then_inc(T.sem[QSEM[o["q"]]], 1)
    for s in total:
        if s not in QSEM and s not in seen:
            g.wait_ge(T.sem[s], total[s])


def rank_program(g, core, T, topo):
    rank = T.rank_of(core)
    if rank is None:
        return
    A, AF = AluOpType, ActivationFunctionType
    V, S, P = g.vector, g.scalar, g.tensor
    n = len(T.cores)
    ne = min(len(topo.engines(a, b)) for a in T.cores for b in T.cores if a != b)
    ops, sends, tag = [], [], [None]

    def cfg(name, t):
        return CFG[name + {1: "1", 4: "4"}.get(t, "")]

    def op(q, fn, r=(), w=(), ext=(), dma=None, remote=False):
        ops.append({"q": q, "fn": fn, "r": list(r), "w": list(w), "ext": list(ext), "dma": dma, "remote": remote, "tag": tag[0]})

    def ts(out, in0, s1, s2, o0, o1, r, w, ext=()):
        if o1 is None:
            op("V", lambda: V.tensor_scalar(out, in0, s1, None, o0), r, w, ext)
        else:
            op("V", lambda: V.tensor_scalar(out, in0, s1, s2, o0, o1), r, w, ext)

    def tt(out, in0, in1, o, r, w, ext=()):
        op("V", lambda: V.tensor_tensor(out, in0, in1, o), r, w, ext)

    def cp(out, in_, r, w, ext=()):
        op("V", lambda: V.tensor_copy(out, in_), r, w, ext)

    def scan(out, d0, d1, init, o0, o1, r, w):
        op("V", lambda: V.tensor_tensor_scan(out, d0, d1, init, o0, o1), r, w)

    def ms(ap, c, w):
        op("V", lambda: V.memset(ap, c), (), w)

    def act(out, in_, r, w, bias=None, scale=None, ext=(), func=None):
        if tag[0][1] in cfg("v", tag[0][0]):
            if bias is None:
                cp(out, in_, r, w, ext)
            else:
                ts(out, in_, bias, None, A.add, None, r, w, ext)
        elif bias is None and scale is None:
            op("S", lambda: S.activation(out, in_, func or AF.Copy), r, w, ext)
        elif bias is None:
            op("S", lambda: S.activation(out, in_, AF.Identity, scale=scale), r, w, ext)
        else:
            op("S", lambda: S.activation(out, in_, AF.Identity, bias=bias, scale=1.0 if scale is None else scale), r, w, ext)

    def mm(out, lhsT, rhs, start, stop, r, w):
        op("P", lambda: P.matmul(out, lhsT, rhs, start, stop), r, w)

    def iota(out, pat, base, w):
        op("G", lambda: g.iota(out, pat, base, 0, allow_small_or_imprecise_dtypes=True), (), w)

    def pick(out, in_, pat, cmp, fill, base, cm, r, w):
        op("G", lambda: g.affine_select(out, in_, pat, cmp, fill, base, cm), r, w)

    def load(out, in_, r, w, sem, q="Y"):
        op(q, lambda: (g.sync if q == "Y" else g.scalar).dma_start(out, in_), r, w, dma=sem)

    def send(t, dst_ap, src_ap, sem, r):
        dst = T.cores[(rank + SR[t % 3]) % n]
        rid, pid, _ = topo.addr(dst)
        mask = sum(1 << e for e in topo.engines(core, dst)[:ne])
        sends.append(sem)
        op("G", lambda: g.remote_dma(dst_ap, src_ap, T.sem[sem], T.sem.sent, pid, rid, mask), r, (), remote=True)

    def turn(buf, frm, to):
        a = (16 * (frm - to)) % 128
        return buf[:, a:a + 128]

    def gather(q, out, src, r, w, ext=(), scale=None):
        if q == "S":
            act(out, src, r, w, ext=ext, scale=scale)
        elif scale is None:
            cp(out, src, r, w, ext)
        else:
            ts(out, src, scale, None, A.mult, None, r, w, ext)

    xw, DM, IDB, BIG = T.x, T.dm[:, 1:K + 1], T.idb[:], float(2 ** 22)
    CH = {"H": (64, K), "L": (0, 64)}
    NB, KB, LB = {"H": "pa", "L": "pb"}, {"H": "pc", "L": "pd"}, {"H": "pe", "L": "pf"}
    SPAN = ((0, 128, "pc"), (128, K, "pd"))
    WK = ["wk%d" % k for k in range(16)]
    LT = ["lta", "ltb"]

    def queue(name):
        return T[name][:, 2 * K:3 * K]

    def wrapped(buf):
        return buf[:, 15:K:16]

    def c_sel(t):
        pick(T.sel0[0:8, :], T.ones[0:8, :], [[0, 2], [1, 128]], A.is_ge, 0.0, 0, -16, ["ones"], ["sel0"])
        pick(T.sel[0:8, :], T.sel0[0:8, :], [[0, 2], [-1, 128]], A.is_ge, 0.0, 15, 16, ["sel0"], ["sel"])

    def c_dj(t):
        ts(T.dj[:], T.di[:], 15, None, A.bitwise_and, None, ["di"], ["dj"])
        ts(T.dm[:], T.dj[:], 0.0, None, A.is_equal, None, ["dj"], ["dm"])

    def c_grp(t):
        mm(T.pc[:, 0:256], T.sel[0:8, 0:128], T.sel[0:8, :], True, True, ["sel"], ["pc"])
        mm(T.pd[:, 0:256], T.sel[0:8, 0:128], T.sel[0:8, :], True, True, ["sel"], ["pd"])

    def c_que(t):
        mm(T.pr[:, 0:K], T.sel[0:8, 0:128], T.qf[0:8, :], True, False, ["sel", "qf"], ["pr"])
        mm(T.pr[:, 0:K], IDB, T.mz[:, 0:K], False, True, ["idb", "m1"], ["pr"])
        mm(T.py[:, 0:K], T.sel[0:8, 0:128], T.qf[0:8, :], True, True, ["sel", "qf"], ["py"])

    def c_wk(j):
        for k in range(4 * j, 4 * j + 4):
            act(T.wk[:, 129 * k:128 * (k + 1):16], T.gm[:], ["gm", "wd", "wk"], ["wk%d" % k], scale=T.wd[:, k:k + 1])

    def c_tri(t):
        pick(T.tri0[:], T.o1[:], [[0, 2], [1, 128]], A.is_ge, 0.0, 0, -1, ["o1"], ["tri0"])
        pick(T.ptri[:], T.tri0[:], [[0, 2], [1, 128]], A.not_equal, 512.0, 0, -1, ["tri0"], ["ptri"])

    def c_pz(t):
        ts(T.col[:, 1:2], T.dj[:, 1:2], float(-W), None, A.add, None, ["dj"], ["col1"])
        act(T.pz[:, 12:24], T.t1[:, 0:K:16], ["t1", "col1"], ["pz"], bias=T.col[:, 1:2])

    def c_pads(t):
        iota(T.pz[:, 24:88], [[0, 64]], 0, ["pz0"])
        iota(T.pz[:, 88:112], [[192, 2], [0, 12]], -896, ["pz0"])
        iota(T.pz[:, 112:116], [[0, 4]], -320, ["pz0"])
        iota(T.pz[:, 116:128], [[0, 12]], -2 ** 22, ["pz0"])
        iota(T.gw[:], [[0, 84]], 0, ["gw", "gw0"])
        iota(T.dum[:, 0:12], [[0, 12]], W, ["zw"])

    def c_rw(t):
        iota(T.rw[:], [[0, 40]], 0, ["rw", "rw0"])
        iota(T.zr[:, 0:12], [[0, 12]], W, ["zw"])

    def c_cf(t):
        cp(T.cf[0:8, 0:1], T.ci[0:8, 0:1], ["ci"], ["cf"])
        mm(T.pr[:, 256:257], T.sel[0:8, 0:128], T.cf[0:8, 0:1], True, True, ["sel", "cf"], ["pr"])

    def spare(name):
        return lambda t: iota(T[name][:, 0:2 * K], [[0, 2 * K]], 0, [name + "d"])

    steps = {
        "sel": c_sel, "dj": c_dj, "grp": c_grp, "que": c_que, "tri": c_tri, "pz": c_pz, "pads": c_pads, "rw0": c_rw, "cf": c_cf,
        "wk": lambda t: c_wk(0), "wkb": lambda t: c_wk(1), "wkc": lambda t: c_wk(2), "wkd": lambda t: c_wk(3),
        "a0d": spare("a0"), "a1d": spare("a1"), "kfd": spare("kf"), "q0d": spare("q0"), "q1d": spare("q1"),
        "ones": lambda t: ms(T.ones[:], 1.0, ["ones"]),
        "mz0": lambda t: ms(T.mz[:, K:2 * K], 0.0, ["mz0"]),
        "wk0": lambda t: ms(T.wk[:], 0.0, ["wk"]),
        "zv": lambda t: ms(T.lt[:, 0:ZV], 0.0, ["lta"]),
        "zq": lambda t: load(T.lt[:, ZV:WX], T.rm[:, 0:WX - ZV], ["rma"], ["ltb"], "lz"),
        "ide": lambda t: load(T.idw[:, K + NT:K + NX], T.idx[:, 0:NX - NT], (), ["ide"], "le"),
        "rmb": lambda t: load(T.rm[:, 8 * K:16 * K], T.rm[:, 0:8 * K], ["rma"], ["rmb"], "lm"),
        "cur": lambda t: op("G", lambda: g.dma_start(T.ci[0:8, 0:1], T.cur[:], allow_slow_non_contiguous=True), (), ["ci"], dma="lc"),
        "di": lambda t: op("G", lambda: g.iota(T.di[:], [[-1, 272]], 273, 1), (), ["di"]),
        "t1": lambda t: iota(T.t1[:], [[1, K]], W, ["t1"]),
        "xd": lambda t: iota(xw[:, W:WX], [[0, K]], 0, ["xd"]),
        "io1": lambda t: iota(T.io1[:], [[1, K]], UP - K, ["io1"]),
        "rm0": lambda t: iota(T.rm[:, 0:8 * K], [[0, 8 * K]], 0, ["rma"]),
        "rm1": lambda t: iota(T.rm[:, 0:16 * K:16], [[0, K]], -64, ["rma", "rmb", "rm0"]),
        "mg": lambda t: iota(T.mg[:], [[0, 160]], int(MAGIC), ["mg"]),
        "ft": lambda t: act(T.ft[:, 32 * (t - 1):32 * t], T.ones[:, 0:32], ["ones"], ["ft%d" % (t - 1)], scale=2.0 ** (STEP * (t - 1) - 78)),
        "t2": lambda t: act(T.t2[:], DM, ["dm"], ["t2"], scale=8192.0, bias=-10.0),
        "t5": lambda t: act(T.t5[:], DM, ["dm"], ["t5"], scale=1.0 / BASE - 1.0, bias=1.0),
        "t6": lambda t: act(T.t6[:], DM, ["dm"], ["t6"], scale=-2.0 ** 70, bias=2.0 ** 70),
        "gm": lambda t: act(T.gm[:], T.pc[:, 0:128:16], ["pc"], ["gm"]),
        "o8": lambda t: act(T.o8[:], T.pc[:, 0:256], ["pc"], ["o8"], scale=8192.0),
        "w0": lambda t: act(T.w0[:], T.pc[:, 0:256], ["pc", "wd"], ["w0"], scale=T.wd[:, 0:1]),
        "o1": lambda t: act(T.o1[:], T.o8[:], ["o8"], ["o1"], scale=1.0 / 8192),
        "o70": lambda t: act(T.o70[:], T.o8[:], ["o8"], ["o70"], scale=2.0 ** 57),
        "idf": lambda t: act(T.idf[:], IDB, ["idb"], ["idf"]),
        "thr": lambda t: act(T.th[:], T.vc[:], ["vc"], ["th"], scale=-18.0 * 2 ** 15),
        "ntri": lambda t: act(T.ntri[:], T.ptri[:], ["ptri"], ["ntri"], scale=-1.0),
        "dum": lambda t: act(T.dum[:, 12:24], T.pz[:, 12:24], ["pz"], ["dum"], bias=128.0),
        "pw": lambda t: act(T.pz[:, 0:12], T.pz[:, 12:24], ["pz"], ["pw"], bias=8192.0, scale=8192.0),
        "cc": lambda t: act(T.cc[:, 0:1], T.pr[:, 256:257], ["pr"], ["cc0"]),
        "qh": lambda t: op("S", lambda: S.activation(queue("q0"), T.py[:, 0:K], AF.Silu, bias=float(UP)), ["py"], ["q0"]),
        "wa": lambda t: ts(T.wa[:], T.dm[:, 1:17], 256.0, None, A.mult, None, ["dm"], ["wa"]),
        "wb": lambda t: ts(T.wb[:], T.dm[:, 2:18], 16.0, None, A.mult, None, ["dm"], ["wb"]),
        "wc": lambda t: tt(T.wc[:], T.wa[:], T.dm[:, 3:19], A.add, ["wa", "dm"], ["wc"]),
        "wd": lambda t: tt(T.wd[:], T.wc[:], T.wb[:], A.add, ["wc", "wb"], ["wd"]),
        "idb": lambda t: tt(IDB, T.pd[:, 0:128], T.dm[:, 1:129], A.mult, ["pd", "dm"], ["idb"]),
        "rot": lambda t: tt(T.rot[:], T.pd[:, 0:256], T.dm[:, 2:258], A.mult, ["pd", "dm"], ["rot"]),
        "vc": lambda t: scan(T.vc[:], T.t5[:], T.mz[:, K:2 * K], BASE ** 12 / 8, A.mult, A.add, ["t5", "mz0"], ["vc"]),
        "qi": lambda t: cp(T.qf[0:8, :], T.qi[0:8, :], ["qi"], ["qf"]),
        "qs0": lambda t: scan(T.qs[:], T.d0[:], T.pr[:, 0:K], -5.0, A.max, A.min, ["d0", "pr"], ["qs"]),
        "ql0": lambda t: cp(T.ql[:, 0:12], wrapped(T.qs), ["qs"], ["ql"]),
        "at0": lambda t: cp(T.at[:], T.idw[:, K:K + NT].indirect(T.ql[:, 0:12]), ["idw", "ql"], ["at"]),
        "ah": lambda t: ts(queue("a0"), T.at[:], float(UP), None, A.add, None, ["at"], ["a0"]),
    }

    def part(e, buf, name, win, lst, o, c, v, w, r, scale=None):
        a = 64 * c
        lo, hi = {"V": (a, a + v), "W": (a + v, a + v + w), "S": (a + v + w, a + 64)}[e]
        gather("S" if e == "S" else "V", buf[:, 16 * lo:16 * hi], win[:, 0:W].indirect(lst[:, o + lo:o + hi]), r,
               ["%s%s%d" % (name, e, c)], scale=scale)

    def index_digits(t, c, e):
        part(e, T.ga, "ga", xw, T.at, 0, c, cfg("a", t)[c], 0 if c else cfg("aw", t), ["x", "at"])

    def round_up(t, h):
        a, b = CH[h]
        mm(T[NB[h]][:, 0:b - a], IDB, T.mg[:, 0:b - a], True, False, ["idb", "mg"], [NB[h]])

    def names(t, c, ks=range(16)):
        h, a = "H" if c else "L", 64 * c
        for k in ks:
            mm(T[NB[h]][:, a - CH[h][0]:a + 64 - CH[h][0]], T.wk[:, 128 * k:128 * (k + 1)], T.ga[:, 16 * a + k:16 * (a + 64):16],
               False, k == 15 and c < 2, ["ga%s%d" % (e, c) for e in "VWS"] + WK, [NB[h]])

    def keep_names(t, h):
        a, b = CH[h]
        act(T.nw[:, 16 + a:16 + b], T[NB[h]][:, 0:b - a], [NB[h]], ["nm" + h], bias=(0 if t == 4 else UP) - MAGIC)

    def masks(t, h):
        m = CH[h][1] - CH[h][0]
        mm(T[KB[h]][:, 0:2 * m], IDB, T.mz[:, K - m:K + m], True, False, ["idb", "m1", "mz0"], [KB[h]])
        mm(T[LB[h]][:, 0:m], IDB, T.mz[:, 0:m], True, False, ["idb", "m1"], [LB[h]])

    def keys(t, h, holder=False):
        a, b = CH[h]
        m, u = b - a, SG[t % 3]
        r = ["ga%s%d" % (e, c) for e in "VWS" for c in ((1, 2) if a else (0,))] + ["w0"]
        g0 = T.ga[:, 16 * a:16 * b:16]
        if holder:
            mm(T[LB[h]][:, 0:m], turn(T.w0, 0, u), g0, False, False, r, [LB[h]])
            if t > 1:
                mm(T[LB[h]][:, 0:m], turn(T.o8, 0, u), T.ne[:, a:b], False, False, ["o8", "ne" + h], [LB[h]])
        else:
            mm(T[KB[h]][:, 0:m], turn(T.w0, 0, u), g0, False, False, r, [KB[h]])
            mm(T[KB[h]][:, m:2 * m], turn(T.w0, 0, u), g0, False, t == 1, r, [KB[h]])

    def changed(t, h):
        a, b = CH[h]
        tt(T.ne[:, a:b], T[NB[h]][:, 0:b - a], T.kp[:, a:b], A.not_equal, [NB[h], "kp"], ["ne" + h])
        mm(T[KB[h]][:, 0:b - a], turn(T.o8, 0, SG[t % 3]), T.ne[:, a:b], False, True, ["o8", "ne" + h], [KB[h]])

    def hold_keys(t, h):
        a, b = CH[h]
        scan(T.ks[:, a:b], T.d0[:, a:b], T[KB[h]][:, 0:b - a], -5.0, A.max, A.min, ["d0", KB[h]], ["ks" + h])

    def twins(t, j, h):
        a, b = CH[h]
        m, d = b - a, 1 + 16 * j
        eq = T.eq[:, j * K + a + d:j * K + b]
        tt(eq, T[KB[h]][:, m + d:2 * m], T.ks[:, a:b - d], A.is_equal, [KB[h], "ks" + h], ["eq%d%s" % (j, h)])
        mm(T[LB[h]][:, d:m], T.o8[:, 0:128], eq, False, j == 1, ["o8", "eq%d%s" % (j, h)], [LB[h]])

    def holders(t, h):
        a, b = CH[h]
        scan(T.ls[:, a:b], T.d0[:, a:b], T[LB[h]][:, 0:b - a], -5.0, A.max, A.min, ["d0", LB[h]], ["ls" + h])

    def lock_list(t, h):
        a, b = CH[h]
        cp(T.ll[:, a // 16:b // 16], T.ls[:, a + 15:b:16], ["ls" + h], ["ll" + h])

    def lock(t, j):
        tt(T.lt[:, 0:WX].indirect(T.ll[:, 2 * j:2 * j + 2]), T.vc[:, 32 * j:32 * j + 32], T.ft[:, 32 * (t - 1):32 * t], A.mult,
           ["vc", "ft%d" % (t - 1), "llH" if j > 1 else "llL"], LT)

    def locks(t, c, e):
        part(e, T.gb, "gb", T.lt, T.nl, K * (t - 1), c, cfg("b", t)[c], 0, LT + ["nl%d_0" % t, "nl%d_64" % t],
             scale=2.0 ** (93 - STEP * (t - 1)))

    def thresholds(t, j):
        lo, hi, b = SPAN[j]
        mm(T[b][:, 0:hi - lo], IDB, T.th[:, lo:hi], True, False, ["idb", "th"], [b])
        mm(T[b][:, 0:hi - lo], IDB, T.t6[:, 0:hi - lo], False, False, ["idb", "t6"], [b])
        if t > 1:
            mm(T[b][:, 0:hi - lo], turn(T.o70, 0, SG[t % 3]), T.ne[:, lo:hi], False, False, ["o70", "neH", "neL"], [b])

    def lock_sums(t, c):
        a = 64 * c
        lo, hi, b = SPAN[c // 2]
        for k in range(16):
            mm(T[b][:, a - lo:a + 64 - lo], IDB, T.gb[:, 16 * a + k:16 * (a + 64):16], False, k == 15 and a + 64 == hi,
               ["gbV%d" % c, "gbS%d" % c, "idb"], [b])

    def goes(t, j):
        lo, hi, b = SPAN[j]
        scan(T.gs[:, lo:hi], T.d0[:, lo:hi], T[b][:, 0:hi - lo], -5.0, A.max, A.min, ["d0", b], ["gs%d" % j])

    def go_list(t):
        c = slice(32 * t - 16, 32 * t - 4)
        cp(T.gl[:, c], T.wf[:, 0:12], ["wf"], ["gl%d" % t])
        send(t, T.glr[:, c], T.gl[:, c], "ag%d" % t, ["gl%d" % t])

    def turn_list(t, src, a, b, key):
        mm(T.pr[:, a:b], turn(T.rot, 0, SG[t % 3]), src, True, True, ["rot", key], ["pr"])

    def send_list(t, a, b, sem):
        o = K * (t - 1)
        ts(T.nl[:, o + a:o + b], T.pr[:, a:b], 0.25 - UP, None, A.add, None, ["pr"], ["nl%d_%d" % (t, a)])
        send(t, T.nlr[:, o + a:o + b], T.nl[:, o + a:o + b], sem, ["nl%d_%d" % (t, a)])

    def digits(t, j, q="S"):
        a, b = cfg("d", t)[j:j + 2]
        o = K * (t - 1)
        sem = "an0" if t == 1 and a < 64 else "an%d" % t
        gather(q, T.gd[:, 16 * a:16 * b], xw[:, 0:W].indirect(T.nlr[:, o + a:o + b]), ["x"], ["gd%d" % j], ext=[(sem, ne)])

    def own_digit(t, j):
        a, b = cfg("d", t)[j:j + 2]
        act(T.rm[:, 16 * a + 15:16 * b:16], T.gd[:, 16 * a + 15:16 * b:16], ["gd%d" % j, "rm0"], ["rh%d" % j])

    def largest(t, j):
        a, b = cfg("d", t)[j:j + 2]
        scan(T.sc[:, 16 * a:16 * b], T.rm[:, 16 * a:16 * b], T.gd[:, 16 * a:16 * b], 0.0, A.add, A.max, ["rh%d" % j, "gd%d" % j], ["sc%d" % j])

    def sums(t):
        return ["sc%d" % j for j in range(len(cfg("d", t)) - 1)]

    def write_records(t):
        tt(xw[:, 0:WX].indirect(T.glr[:, 32 * t - 16:32 * t - 4]), T.sc[:, 15:16 * K:16], T.s2[:], A.add, ["s2", "xd"] + sums(t), ["x"],
           ext=[("ag%d" % t, ne)])

    def restart_counts(t):
        u = SG[t % 3]
        scan(T.nz[:, 0:24], T.rw[:, 0:24], T.rw[:, 12:36], 0.0, A.add, A.subtract, ["rw", "rw0"], ["nz"])
        mm(T.pr[:, 0:12], turn(T.o1, u, 0), T.nz[:, 12:24], True, False, ["o1", "nz"], ["pr"])
        mm(T.pr[:, 0:12], turn(T.ptri, u, 0), T.rw[:, 13:25], False, True, ["ptri", "rw"], ["pr"])
        mm(T.py[:, 12:24], turn(T.o1, u, 0), T.nz[:, 0:12], False, False, ["o1", "nz"], ["py"])
        mm(T.py[:, 12:24], turn(T.ntri, u, 0), T.rw[:, 13:25], False, False, ["ntri", "rw"], ["py"])

    def place_terms(t):
        mm(T.py[:, 0:113], IDB, T.pz[:, 0:113], True, False, ["idb", "pz", "pz0", "pw"], ["py"])
        if t < 4:
            mm(T.py[:, 0:12], IDB, T.pz[:, 116:128], False, False, ["idb", "pz0"], ["py"])
            mm(T.py[:, 88:100], T.idf[:], T.px[:, 12:24], False, False, ["idf", "px2"], ["py"])

    def go_counts(t):
        u = SG[t % 3]
        scan(T.cz[:, 0:47], T.gw[:, 36:83], T.gw[:, 0:47], 20.0, A.add, A.subtract, ["gw", "gw0"], ["cz"])
        mm(T.py[:, 12:24], turn(T.ntri, u, 0), T.gw[:, 36:48], False, False, ["ntri", "gw"], ["py"])
        mm(T.pf[:, 0:1], IDB, T.pz[:, 112:113], True, False, ["idb", "pz0"], ["pf"])
        mm(T.py[:, 12:24], turn(T.o1, u, 0), T.cz[:, 35:47], False, False, ["o1", "cz"], ["py"])
        if t < 4:
            mm(T.py[:, 0:12], turn(T.o8, u, SG[(t + 1) % 3]), T.cz[:, 11:23], False, False, ["o8", "cz"], ["py"])
            for j in range(2):
                mm(T.py[:, 88:112], turn(T.o1, u, 0), T.cz[:, 11:35], False, False, ["o1", "cz"], ["py"])
        mm(T.py[:, 112:113], turn(T.o1, u, 0), T.cz[:, 11:12], False, True, ["o1", "cz"], ["py"])
        mm(T.pf[:, 0:1], turn(T.o1, u, 0), T.cz[:, 11:12], False, True, ["o1", "cz"], ["pf"])

    def places(t):
        a = 12 if t == 4 else 0
        tt(T.py[:, 64 + a:88], T.py[:, a:24], (T.dum if t == 1 else T.zr)[:, a:24], A.max, ["py", "dum", "zr", "zw"], ["py"])

    def place_list(t):
        m = 12 if t == 4 else 24
        ts(T.dl[:, 48 * t:48 * t + m], T.py[:, 76:76 + m], T.py[:, 112:113], 64.0, A.subtract, A.add, ["py"], ["dl%d" % t])

    def move(t, q, to, src, key):
        out, r = T[to][:, 0:3 * K].indirect(T.dl[:, 48 * t:48 * t + 12]), key + ["dl%d" % t, to + "d", to]
        if q == "S":
            act(out, src, r, [to], func=AF.Silu)
        else:
            cp(out, src, r, [to])

    def along(name, t):
        a, b = "%s%d" % (name, t % 2), "%s%d" % (name, (t + 1) % 2)
        if t > 0:
            move(t, "S", a, queue(b), [b])

    def new_numbers(t):
        if t > 0:
            act(queue("q%d" % (t % 2)), T.io1[:], ["io1", "cc%d" % t], ["q%d" % (t % 2)], bias=T.cc[:, t:t + 1])

    def numbers(t):
        ts(T.t2[:], queue("q0"), MAGIC - UP, -MAGIC, A.add, A.add, ["q0"], ["t2"])
        ts(T.t3[:], T.t2[:], float(NT), float(-NT), A.is_ge, A.mult, ["t2"], ["t3"])
        tt(T.t4[:], T.t2[:], T.t3[:], A.add, ["t2", "t3"], ["t4"])
        load(T.yq[:], T.t4[0:128:16, :], ["t4"], (), "oq")

    def store(t):
        load(T.yx[0:64, :], xw[0:64, 0:W], ["x"], (), "oa")
        load(T.yx[64:128, :], xw[64:128, 0:W], ["x"], (), "ob")

    for h in "HL":
        for name, f in (("m", masks), ("r", round_up), ("k", keys), ("p", lambda t, h: keys(t, h, True)), ("ne", changed),
                        ("ks", hold_keys), ("ls", holders), ("ll", lock_list), ("nm", keep_names)):
            steps[name + h] = lambda t, f=f, h=h: f(t, h)
        for j in range(2):
            steps["e%d%s" % (j, h)] = lambda t, j=j, h=h: twins(t, j, h)
        a, b = CH[h]
        steps["t" + h] = lambda t, a=a, b=b, h=h: turn_list(1, T.nw[:, 16 + a:16 + b], a, b, "nm" + h)
        steps["nl" + h] = lambda t, a=a, b=b: send_list(1, a, b, "an1" if a else "an0")
    for j in range(6):
        for name, f in (("n", names), ("s", lock_sums), ("l", lock), ("g", goes), ("h", own_digit), ("m", largest), ("d", digits),
                        ("th", thresholds)):
            steps["%s%d" % (name, j)] = lambda t, f=f, j=j: f(t, j)
        for e in "VWS":
            steps["a%d%s" % (j, e)] = lambda t, j=j, e=e: index_digits(t, j, e)
            steps["b%d%s" % (j, e)] = lambda t, j=j, e=e: locks(t, j, e)
    steps.update({
        "m1": lambda t: largest(t, 1) if t else act(T.mz[:, 0:K], DM, ["dm"], ["m1"], scale=-BIG, bias=BIG),
        "d0": lambda t: digits(t, 0) if t else tt(T.d0[:], T.t1[:], T.t2[:], A.min, ["t1", "t2"], ["d0"]),
        "d0V": lambda t: digits(t, 0, "V"),
        "n0": lambda t: names(t, 0, range(8)), "n0b": lambda t: names(t, 0, range(8, 16)),
        "w": lambda t: tt(T.wf[:, 0:12], wrapped(T.gs), wrapped(T.ks), A.max, ["ksH", "ksL", "gs1", "gs0"], ["wf"]),
        "gl": go_list,
        "gw": lambda t: ts(T.gw[:, 36:48], wrapped(T.gs), float(W), None, A.is_lt, None, ["gs0", "gs1", "gw0"], ["gw"]),
        "rw": lambda t: tt(T.rw[:, 13:25], wrapped(T.ks), T.py[:, 64:76], A.is_ge, ["ksH", "ksL", "py", "rw0"], ["rw"]),
        "zr": lambda t: tt(T.zr[:, 12:24], T.pr[:, 0:12], T.dum[:, 12:24], A.max, ["pr", "dum"], ["zr"]),
        "py": place_terms, "nz": restart_counts, "cz": go_counts, "mb": places, "dl": place_list,
        "e": lambda t: act(T.cc[:, t:t + 1], T.pf[:, 0:1], ["pf", "cc%d" % (t - 1)], ["cc%d" % t], bias=T.cc[:, t - 1:t]),
        "pc": lambda t: act(T.px[:, 12:24], T.pz[:, 12:24], ["pz", "cc%d" % (t - 1)], ["px2"], bias=T.cc[:, t - 1:t]),
        "new": lambda t: ts(queue("a%d" % (t % 2)), T.idw[:, K:K + NX].indirect(T.dl[:, 48 * t + 12:48 * t + 24]), float(UP), None,
                            A.add, None, ["idw", "ide", "dl%d" % t], ["a%d" % (t % 2)]),
        "mva": lambda t: along("a", t), "mvq": lambda t: along("q", t), "qf": new_numbers,
        "at": lambda t: ts(T.at[:], queue("a%d" % (t % 2)), 0.25 - UP, None, A.add, None, ["a%d" % (t % 2)], ["at"]),
        "kf": lambda t: iota(queue("kf"), [[0, K]], -1 if t == 4 else UP - 1, ["kf"]),
        "mvk": lambda t: move(t, "V" if t == 4 else "S", "kf", T.nw[:, 16:16 + K], ["nmH", "nmL"]),
        "kp": lambda t: act(T.kp[:], queue("kf"), ["kf"], ["kp"], bias=MAGIC - UP),
        "turn": lambda t: turn_list(t + 1, queue("kf"), 0, K, "kf"),
        "nl": lambda t: send_list(t + 1, 0, K, "an%d" % (t + 1)),
        "cy": lambda t: ts(T.s2[:], T.sc[:, 15:16 * K:16], 16.0, -16.0, A.is_ge, A.mult, sums(t), ["s2"]),
        "x": write_records, "yx": store, "yq": numbers,
        "yd": lambda t: load(T.yd[:], queue("kf"), ["kf"], (), "od"),
    })

    load(T.qi[0:8, :], T.que[:], (), ["qi"], "lq", q="S")
    load(T.idw[:, K:K + NT], T.idx[:], (), ["idw"], "li")
    load(xw[:, 0:W], T.rec[:], (), ["x"], "lr")
    for t in range(1, 5):
        for name in ORDER[t].split():
            tag[0] = (t, name)
            steps[name.rstrip("<>")](t - name.count("<") + name.count(">"))
    emit(g, T, ops)
    g.wait_ge(T.sem.sent, len(sends) * ne)
